import numpy as np
import ml_dtypes


def mxq(x, axis, fmt="e4m3"):
    dtype, down = {"e4m3": (ml_dtypes.float8_e4m3fn, 7), "e5m2": (ml_dtypes.float8_e5m2, 14)}[fmt]
    v = np.moveaxis(np.asarray(x, np.float32).astype(ml_dtypes.bfloat16).astype(np.float64), axis, -1)
    blocks = v.reshape(v.shape[:-1] + (-1, 32))
    amax = np.abs(blocks).max(-1, keepdims=True)
    byte = np.maximum(np.where(amax > 0, np.frexp(amax)[1] - 1 + 127, 0) - down, 1)
    scale = np.exp2(byte - 127.0)
    codes = (blocks / scale).astype(np.float32).astype(dtype).astype(np.float64)
    return np.moveaxis((codes * scale).reshape(v.shape), -1, axis)


WIDE = False


def mx_kscale(k):
    if not WIDE:
        return np.ones(k)
    levels = np.array([24, -24, 12, -12, 0])
    if k % 512:
        return np.exp2(np.random.permutation(np.resize(levels, k // 32))).repeat(32)
    a = np.empty((k // 512, 16))
    for p in range(k // 512):
        a[p, :8] = np.random.permutation(np.resize(levels, 8))
        for g in range(8):
            far = levels[np.abs(levels - a[p, g]) >= 10]
            a[p, g + 8] = far[np.random.randint(len(far))]
    return np.exp2(a.ravel()).repeat(32)


def f64(x):
    return np.asarray(x).astype(np.float64)


def striped(idx):
    return np.tile(idx.reshape(-1, 16).T, (8, 1)).astype(np.uint16)


def unstriped(offs):
    return offs[:16].T.reshape(-1).astype(np.int64)


E2M1 = np.array([0.0, 0.5, 1.0, 1.5, 2.0, 3.0, 4.0, 6.0, -0.0, -0.5, -1.0, -1.5, -2.0, -3.0, -4.0, -6.0])


def pack_weight(w, fmt):
    k, n = w.shape
    w = f64(np.asarray(w, np.float32).astype(ml_dtypes.bfloat16)).reshape(k // 32, 32, n)
    amax = np.abs(w).max(1)
    if fmt == "e4m3":
        byte = np.frexp(amax)[1] - 1 + 127 - 7
    else:
        mant, ex = np.frexp(amax / 6.0)
        byte = np.where(mant > 0.5, ex, ex - 1) + 127
    byte = np.clip(np.where(amax > 0, byte, 1), 1, 254)
    scaled = (w * np.exp2(127.0 - byte)[:, None, :]).reshape(k, n).astype(np.float32)
    by_word = np.ascontiguousarray(scaled.reshape(k // 512, 128, 4, n).transpose(0, 1, 3, 2))
    if fmt == "e4m3":
        words = by_word.astype(ml_dtypes.float8_e4m3fn).view(np.uint8)
    else:
        c = by_word.astype(ml_dtypes.float4_e2m1fn).view(np.uint8) & 0xF
        words = (c[..., 0::2] | (c[..., 1::2] << 4)).reshape(k // 512, 128, 2 * n)
    return np.ascontiguousarray(words), np.ascontiguousarray(byte.astype(np.uint8).reshape(k // 512, 16, n))


def unpack_weight(words, scales, fmt):
    g, _, n = scales.shape
    words = np.ascontiguousarray(words).reshape(g, 128, n, -1)
    if fmt == "e4m3":
        vals = words.view(ml_dtypes.float8_e4m3fn).astype(np.float64)
    else:
        nib = np.empty((g, 128, n, 4), np.uint8)
        nib[..., 0::2] = words & 0xF
        nib[..., 1::2] = words >> 4
        vals = E2M1[nib]
    vals = vals * np.repeat(np.exp2(scales.astype(np.float64) - 127.0), 8, axis=1)[..., None]
    return vals.transpose(0, 1, 3, 2).reshape(g * 512, n)


def pack_table4(v):
    words, scales = pack_weight(v, "e2m1")
    g, t = words.shape[0] // 2, v.shape[1]
    return np.ascontiguousarray(words.reshape(g, 2, 128, t, 2).transpose(0, 2, 3, 1, 4).reshape(g, 128, t, 4)), scales


def unpack_table4(words, scales):
    g, _, t, _ = words.shape
    return unpack_weight(words.reshape(g, 128, t, 2, 2).transpose(0, 3, 1, 2, 4).reshape(2 * g, 128, 2 * t), scales, "e2m1")


K, R, N, T, J = 1024, 1024, 512, 2048, 1024


def setup_inputs():
    n = np.random.standard_normal
    s = mx_kscale(K)[:, None]
    u = mx_kscale(R)[:, None]
    wd = n((R, N)) / np.sqrt(R) / u
    wd4 = pack_weight(wd, "e2m1")
    wdrest = wd - unpack_weight(*wd4, "e2m1")
    p_tab = pack_table4(n((K, T)) * s)
    p_wd8 = pack_weight(wdrest, "e4m3")
    return {
        "tab_words": p_tab[0],
        "tab_scales": p_tab[1],
        "ws": (n((K, R)) / np.sqrt(2 * K) / s).astype(np.float32),
        "wt": (n((K, R)) / np.sqrt(2 * K) / s).astype(np.float32),
        "sm": (np.random.uniform(0.5, 2.0, R) * u[:, 0]).astype(np.float32),
        "wd4_words": wd4[0],
        "wd4_scales": wd4[1],
        "wd8_words": p_wd8[0],
        "wd8_scales": p_wd8[1],
        "b": (0.3 * n(N)).astype(np.float32),
        "wgo": np.tile(np.random.uniform(0.5, 2.0, J), (128, 1)).astype(np.float32),
        "offs": striped(np.random.permutation(T)[:J]),
        "offs2": striped(np.random.permutation(T)[:J]),
    }


def reference(tab_words, tab_scales, ws, wt, sm, wd4_words, wd4_scales, wd8_words, wd8_scales, b, wgo, offs, offs2):
    idx = unstriped(offs)
    idx2 = unstriped(offs2)
    tab_ = unpack_table4(tab_words, tab_scales)[:, idx]
    tabb_ = unpack_table4(tab_words, tab_scales)[:, idx2]
    ws_ = mxq(f64(ws), 0, "e4m3")
    wt_ = mxq(f64(wt), 0, "e4m3")
    a = ws_.T @ tab_ + wt_.T @ tabb_
    h = f64(sm)[:, None] * np.tanh(a)
    h_ = mxq(h, 0, "e4m3")
    wd4_ = unpack_weight(wd4_words, wd4_scales, "e2m1")
    wd8_ = unpack_weight(wd8_words, wd8_scales, "e4m3")
    y = wd4_.T @ h_ + wd8_.T @ h_
    out = np.zeros((N, T))
    out[:, idx2] = f64(wgo)[0] * (y + f64(b)[:, None])
    return out

@@ -1,0 +1,263 @@
+from contextlib import ExitStack
+
+import concourse.mybir as mybir
+
+K, R, N, T, J = 1024, 1024, 512, 2048, 1024
+FLOPS = 2 * (2 * K * R * J + 2 * R * N * J)
+
+F32 = mybir.dt.float32
+BF16 = mybir.dt.bfloat16
+I32 = mybir.dt.int32
+U32 = mybir.dt.uint32
+U16 = mybir.dt.uint16
+U8 = mybir.dt.uint8
+FP8X4 = mybir.dt.float8_e4m3fn_x4
+FP4X4 = mybir.dt.float4_e2m1fn_x4
+ACT = mybir.ActivationFunctionType
+MULT = mybir.AluOpType.mult
+
+P = 128
+PASS = 512
+HALF = 512
+SUB = 128
+
+
+def tile_list_msg_tanh_res_bias_kernel(
+    tc, tab_words, tab_scales, ws, wt, sm, wd4_words, wd4_scales, wd8_words, wd8_scales, b, wgo, offs, offs2, out
+):
+    nc = tc.nc
+    with ExitStack() as ctx:
+        keep = ctx.enter_context(tc.tile_pool(name="keep", bufs=1))
+        ring = ctx.enter_context(tc.tile_pool(name="ring", bufs=3))
+        stream = ctx.enter_context(tc.tile_pool(name="stream", bufs=8))
+        psum = ctx.enter_context(tc.psum_pool(name="psum", bufs=1))
+
+        lists = [keep.tile([P, J // 16], U16, name="list%d" % s) for s in range(2)]
+        tab_sc = keep.tile([P, T], U8, name="tab_sc", align_bytes=64)
+        tab_w = keep.tile([P, T], I32, name="tab_w", align_bytes=64)
+        sm_sb = keep.tile([P, 2, 4], F32, name="sm_sb")
+        nc.gpsimd.memset(tab_sc[:].bitcast(I32), 0)
+        nc.sync.dma_start(lists[0][:], offs)
+        nc.sync.dma_start(lists[1][:], offs2)
+        nc.sync.dma_start(out=sm_sb[:], in_=sm.rearrange("(g p t) -> p g t", g=2, t=4))
+        for q in range(4):
+            nc.sync.dma_start(
+                out=tab_sc[32 * q : 32 * q + 8, :].bitcast(I32), in_=tab_scales[:, 4 * q : 4 * q + 4, :].bitcast(I32)
+            )
+        weights = (ws, wt)
+        steps = [(s, a) for a in range(2) for s in range(2)]
+        raw = {}
+
+        def load_w(g, s, a):
+            raw[g, s, a] = stream.tile([P, 4, PASS], F32, name="raw", align_bytes=64)
+            rows = weights[s][PASS * a : PASS * (a + 1), PASS * g : PASS * (g + 1)].rearrange("(p j) c -> p j c", j=4)
+            for j in (0, 2):
+                nc.sync.dma_start(out=raw[g, s, a][:, j : j + 2, :], in_=rows[:, j : j + 2, :])
+
+        def load_table_words():
+            nc.sync.dma_start(out=tab_w[:], in_=tab_words[0].rearrange("p t b -> p (t b)").bitcast(I32))
+
+        warm = keep.tile([P, 1], F32, name="warm")
+        nc.vector.memset(warm[:], 0.0)
+        warm2 = keep.tile([P, 1], F32, name="warm2")
+        nc.scalar.activation(out=warm2[:], in_=warm[:], func=ACT.Tanh)
+
+        picked_sc = keep.tile([P, 2, J], U8, name="picked_sc", align_bytes=64)
+        moved_sc = keep.tile([P, 2, J], U8, name="moved_sc", align_bytes=64)
+        picked_w = keep.tile([P, 2, J], I32, name="picked_w", align_bytes=64)
+        parted = keep.tile([P, 2, 2, 2, 2 * HALF], U8, name="parted", align_bytes=64)
+
+        def entries(s, j0, j1):
+            return lists[s][:, j0 // 16 : j1 // 16]
+
+        def gather_scales(j0, j1):
+            for s in range(2):
+                nc.vector.tensor_copy(picked_sc[:, s, j0:j1], tab_sc[:].indirect(entries(s, j0, j1)))
+                nc.gpsimd.dma_start(
+                    out=moved_sc[0 : P - 4, s, j0:j1].bitcast(I32), in_=picked_sc[4:P, s, j0:j1].bitcast(I32)
+                )
+
+        def gather_words(half):
+            j0, j1 = HALF * half, HALF * (half + 1)
+            for s in range(2):
+                nc.vector.tensor_copy(
+                    picked_w[:, s, j0:j1].bitcast(U32), tab_w[:].bitcast(U32).indirect(entries(s, j0, j1))
+                )
+            for s in range(2):
+                nc.vector.tensor_copy(
+                    out=parted[:, half, s, :, :].bitcast(U16),
+                    in_=picked_w[:, s, j0:j1].bitcast(U16).rearrange("p (j d) -> p d j", d=2),
+                )
+
+        w_codes = {}
+        w_sc = {}
+
+        def prepare_w(g, s, a, on_vector):
+            rounded = ring.tile([P, 4 * PASS], BF16, name="rounded", align_bytes=64)
+            dst = rounded[:].rearrange("p (t m j) -> p m j t", t=4, j=4)
+            src = raw[g, s, a][:].rearrange("p j (m t) -> p m j t", t=4)
+            cut = P - on_vector
+            if cut > 0:
+                nc.scalar.copy(out=dst[:, 0:cut], in_=src[:, 0:cut])
+            if on_vector > 0:
+                nc.vector.tensor_copy(out=dst[:, cut:P], in_=src[:, cut:P])
+            w_codes[g, s, a] = keep.tile([P, PASS], U32, name="wc%d%d%d" % (g, s, a), align_bytes=64)
+            w_sc[g, s, a] = keep.tile([P, PASS], U8, name="wsc%d%d%d" % (g, s, a), align_bytes=64)
+            nc.vector.quantize_mx(out=w_codes[g, s, a][:].bitcast(FP8X4), scales=w_sc[g, s, a][:], in_=rounded[:])
+
+        def first_product(g, half, bank0):
+            banks = [psum.tile([P, HALF], F32, name="bank%d" % (bank0 + t)) for t in range(4)]
+            for s, a in steps:
+                plane = (picked_sc, moved_sc)[a]
+                for t in range(4):
+                    m = slice(P * t, P * (t + 1))
+                    nc.tensor.matmul_mx(
+                        out=banks[t][:],
+                        lhsT=w_codes[g, s, a][:, m].bitcast(FP8X4),
+                        lhsT_scale=w_sc[g, s, a][:, m],
+                        rhs=parted[:, half, s, a, :].bitcast(FP4X4),
+                        rhs_scale=plane[:, s, HALF * half : HALF * (half + 1)],
+                        start=((s, a) == steps[0]),
+                        stop=((s, a) == steps[-1]),
+                    )
+            return banks
+
+        h_codes = [keep.tile([P, J], U32, name="hc%d" % g, align_bytes=64) for g in range(2)]
+        h_sc = [keep.tile([P, J], U8, name="hsc%d" % g, align_bytes=64) for g in range(2)]
+        b_sb = keep.tile([P, 4], F32, name="b_sb")
+        wd_sc = keep.tile([P, 2, 2, N], U8, name="wd_sc", align_bytes=64)
+
+        def activate(banks, j0, j1):
+            w = j1 - j0
+            c0 = j0 % HALF
+            act = ring.tile([P, 4, w], F32, name="act", bufs=4)
+            for t in range(4):
+                nc.scalar.activation(out=act[:, t, :], in_=banks[t][:, c0 : c0 + w], func=ACT.Tanh)
+            return act
+
+        def smooth(g, act, j0, j1, on_vector, c0=0):
+            w = j1 - j0
+            h = ring.tile([P, w, 4], BF16, name="h", align_bytes=64)
+            if not on_vector:
+                scaled = ring.tile([P, 4, w], BF16, name="scaled")
+                for t in range(4):
+                    nc.scalar.activation(
+                        out=scaled[:, t, :], in_=act[:, t, c0 : c0 + w], func=ACT.Copy, scale=sm_sb[:, g, t : t + 1]
+                    )
+            for c in range(0, w, SUB):
+                dst = h[:, c : c + SUB, :].rearrange("p (c i) t -> p c t i", i=4)
+                if on_vector:
+                    nc.vector.tensor_tensor(
+                        out=dst,
+                        in0=act[:, :, c0 + c : c0 + c + SUB].rearrange("p t (c i) -> p c t i", i=4),
+                        in1=sm_sb[:, g, :].unsqueeze(1).unsqueeze(3).to_broadcast([P, SUB // 4, 4, 4]),
+                        op=MULT,
+                    )
+                else:
+                    nc.scalar.copy(out=dst, in_=scaled[:, :, c : c + SUB].rearrange("p t (c i) -> p c t i", i=4))
+            nc.vector.quantize_mx(
+                out=h_codes[g][:, j0:j1].bitcast(FP8X4), scales=h_sc[g][:, j0:j1], in_=h[:].rearrange("p w t -> p (w t)")
+            )
+
+        def hidden(g, banks, j0, j1, on_vector):
+            smooth(g, activate(banks, j0, j1), j0, j1, on_vector)
+
+        placed = [keep.tile([P, T], F32, name="placed%d" % i) for i in range(4)]
+        second = {}
+
+        def load_second():
+            tiers = stream.tile([P, 2, 3 * N // 2], I32, name="raw", align_bytes=64)
+            second["wd4"] = tiers[:, :, 0 : N // 2]
+            second["wd8"] = tiers[:, :, N // 2 : 3 * N // 2]
+            nc.sync.dma_start(out=second["wd4"], in_=wd4_words.rearrange("a p n -> p a n").bitcast(I32))
+            nc.sync.dma_start(out=second["wd8"], in_=wd8_words.rearrange("a p n i -> p a (n i)").bitcast(I32))
+            second["wgo"] = stream.tile([P, J], F32, name="raw", align_bytes=64)
+            nc.sync.dma_start(out=second["wgo"][:], in_=wgo)
+
+        def message(j0, j1, i, bank):
+            w = j1 - j0
+            step = HALF if w == HALF else P
+            y = psum.tile([P, w], F32, name="bank%d" % bank)
+            n = slice(P * i, P * (i + 1))
+            for c in range(0, w, step):
+                for g in range(2):
+                    for tier in range(2):
+                        if tier == 0:
+                            lhs = second["wd4"][:, g, P // 2 * i : P // 2 * (i + 1)].bitcast(FP4X4)
+                        else:
+                            lhs = second["wd8"][:, g, n].bitcast(FP8X4)
+                        nc.tensor.matmul_mx(
+                            out=y[:, c : c + step],
+                            lhsT=lhs,
+                            lhsT_scale=wd_sc[:, tier, g, n],
+                            rhs=h_codes[g][:, j0 + c : j0 + c + step].bitcast(FP8X4),
+                            rhs_scale=h_sc[g][:, j0 + c : j0 + c + step],
+                            start=(g == 0 and tier == 0),
+                            stop=(g == 1 and tier == 1),
+                        )
+            biased = ring.tile([P, w], F32, name="biased", bufs=12)
+            nc.scalar.activation(out=biased[:], in_=y[:], func=ACT.Identity, bias=b_sb[:, i : i + 1])
+            return biased
+
+        def place(j0, j1, i, biased):
+            nc.vector.tensor_tensor(
+                out=placed[i][:].indirect(entries(1, j0, j1)), in0=biased[:], in1=second["wgo"][:, j0:j1], op=MULT
+            )
+
+        def load_small():
+            nc.vector.memset(wd_sc[:].bitcast(I32), 0)
+            for tier, scales in enumerate((wd4_scales, wd8_scales)):
+                for q in range(4):
+                    nc.gpsimd.dma_start(
+                        out=wd_sc[32 * q : 32 * q + 4, tier, :, :].bitcast(I32),
+                        in_=scales[:, 4 * q : 4 * q + 4, :].rearrange("a r n -> r a n").bitcast(I32),
+                    )
+            with nc.allow_non_contiguous_dma(reason="one bias value for each partition"):
+                nc.gpsimd.dma_start(out=b_sb[:], in_=b.rearrange("(i p) -> p i", p=P))
+
+        def store(i):
+            nc.sync.dma_start(out=out[P * i : P * (i + 1), :], in_=placed[i][:])
+
+        nc.vector.memset(moved_sc[:].bitcast(I32), 0)
+        load_w(0, *steps[0])
+        load_table_words()
+        gather_scales(0, J)
+        gather_words(0)
+        share = [0,0,0,32,64,64,64,64]
+        for c in range(4):
+            if c >= 1:
+                load_w(0, *steps[c])
+            prepare_w(0, *steps[c], share[c])
+        gather_words(1)
+        for i in range(4):
+            (nc.vector if i < 1 else nc.gpsimd).memset(placed[i][:], 0.0)
+        load_small()
+        early = activate(first_product(0, 0, 0), 0, 512)
+        late = first_product(0, 1, 4)
+        for c in range(4):
+            load_w(1, *steps[c])
+            prepare_w(1, *steps[c], share[4 + c])
+        load_second()
+        smooth(0, early, 0, 256, 1)
+        banks = first_product(1, 0, 0)
+        first = activate(banks, 0, 256)
+        late = activate(late, 512, 1024)
+        smooth(1, first, 0, 256, 1)
+        y0 = [message(0, 256, i, 4 + i) for i in range(4)]
+        smooth(0, early, 256, 512, 1, 256)
+        hidden(1, banks, 256, 512, 0)
+        banks = first_product(1, 1, 0)
+        y1 = [message(256, 512, i, 4 + i) for i in range(4)]
+        place(0, 256, 0, y0[0])
+        smooth(0, late, 512, 768, 1, 0)
+        smooth(0, late, 768, 1024, 1, 256)
+        last = activate(banks, 512, 1024)
+        smooth(1, last, 512, 768, 0, 0)
+        smooth(1, last, 768, 1024, 0, 256)
+        for i in range(1, 4):
+            place(0, 256, i, y0[i])
+        for i in range(4):
+            place(256, 512, i, y1[i])
+        for i in range(4):
+            place(512, 1024, i, message(512, 1024, i, 4 + i))
+            store(i)

@@ -29,7 +29,7 @@ def tile_list_msg_tanh_res_bias_kernel(
     with ExitStack() as ctx:
         keep = ctx.enter_context(tc.tile_pool(name="keep", bufs=1))
         ring = ctx.enter_context(tc.tile_pool(name="ring", bufs=3))
-        stream = ctx.enter_context(tc.tile_pool(name="stream", bufs=8))
+        stream = ctx.enter_context(tc.tile_pool(name="stream", bufs=6))
         psum = ctx.enter_context(tc.psum_pool(name="psum", bufs=1))
 
         lists = [keep.tile([P, J // 16], U16, name="list%d" % s) for s in range(2)]
@@ -73,8 +73,8 @@ def tile_list_msg_tanh_res_bias_kernel(
         def gather_scales(j0, j1):
             for s in range(2):
                 nc.vector.tensor_copy(picked_sc[:, s, j0:j1], tab_sc[:].indirect(entries(s, j0, j1)))
-                nc.gpsimd.dma_start(
-                    out=moved_sc[0 : P - 4, s, j0:j1].bitcast(I32), in_=picked_sc[4:P, s, j0:j1].bitcast(I32)
+                nc.sync.dma_start(
+                    out=moved_sc[0:112, s, j0:j1].bitcast(I32), in_=picked_sc[4:116, s, j0:j1].bitcast(I32)
                 )
 
         def gather_words(half):
@@ -166,12 +166,12 @@ def tile_list_msg_tanh_res_bias_kernel(
         second = {}
 
         def load_second():
-            tiers = stream.tile([P, 2, 3 * N // 2], I32, name="raw", align_bytes=64)
+            tiers = keep.tile([P, 2, 3 * N // 2], I32, name="tiers", align_bytes=64)
             second["wd4"] = tiers[:, :, 0 : N // 2]
             second["wd8"] = tiers[:, :, N // 2 : 3 * N // 2]
             nc.sync.dma_start(out=second["wd4"], in_=wd4_words.rearrange("a p n -> p a n").bitcast(I32))
             nc.sync.dma_start(out=second["wd8"], in_=wd8_words.rearrange("a p n i -> p a (n i)").bitcast(I32))
-            second["wgo"] = stream.tile([P, J], F32, name="raw", align_bytes=64)
+            second["wgo"] = keep.tile([P, J], F32, name="wgo_sb")
             nc.sync.dma_start(out=second["wgo"][:], in_=wgo)
 
         def message(j0, j1, i, bank):
@@ -204,21 +204,22 @@ def tile_list_msg_tanh_res_bias_kernel(
                 out=placed[i][:].indirect(entries(1, j0, j1)), in0=biased[:], in1=second["wgo"][:, j0:j1], op=MULT
             )
 
-        def load_small():
-            nc.vector.memset(wd_sc[:].bitcast(I32), 0)
+        def load_second_scales(q):
             for tier, scales in enumerate((wd4_scales, wd8_scales)):
-                for q in range(4):
-                    nc.gpsimd.dma_start(
-                        out=wd_sc[32 * q : 32 * q + 4, tier, :, :].bitcast(I32),
-                        in_=scales[:, 4 * q : 4 * q + 4, :].rearrange("a r n -> r a n").bitcast(I32),
-                    )
+                nc.sync.dma_start(
+                    out=wd_sc[32 * q : 32 * q + 4, tier, :, :].bitcast(I32),
+                    in_=scales[:, 4 * q : 4 * q + 4, :].rearrange("a r n -> r a n").bitcast(I32),
+                )
+
+        def load_bias():
             with nc.allow_non_contiguous_dma(reason="one bias value for each partition"):
-                nc.gpsimd.dma_start(out=b_sb[:], in_=b.rearrange("(i p) -> p i", p=P))
+                nc.sync.dma_start(out=b_sb[:], in_=b.rearrange("(i p) -> p i", p=P))
 
         def store(i):
             nc.sync.dma_start(out=out[P * i : P * (i + 1), :], in_=placed[i][:])
 
         nc.vector.memset(moved_sc[:].bitcast(I32), 0)
+        nc.vector.memset(wd_sc[:].bitcast(I32), 0)
         load_w(0, *steps[0])
         load_table_words()
         gather_scales(0, J)
@@ -230,14 +231,15 @@ def tile_list_msg_tanh_res_bias_kernel(
             prepare_w(0, *steps[c], share[c])
         gather_words(1)
         for i in range(4):
-            (nc.vector if i < 1 else nc.gpsimd).memset(placed[i][:], 0.0)
-        load_small()
+            (nc.vector if i < 4 else nc.gpsimd).memset(placed[i][:], 0.0)
         early = activate(first_product(0, 0, 0), 0, 512)
         late = first_product(0, 1, 4)
         for c in range(4):
             load_w(1, *steps[c])
+            load_second_scales(c)
             prepare_w(1, *steps[c], share[4 + c])
         load_second()
+        load_bias()
         smooth(0, early, 0, 256, 1)
         banks = first_product(1, 0, 0)
         first = activate(banks, 0, 256)

@@ -29,7 +29,6 @@ def tile_list_msg_tanh_res_bias_kernel(
     with ExitStack() as ctx:
         keep = ctx.enter_context(tc.tile_pool(name="keep", bufs=1))
         ring = ctx.enter_context(tc.tile_pool(name="ring", bufs=3))
-        stream = ctx.enter_context(tc.tile_pool(name="stream", bufs=6))
         psum = ctx.enter_context(tc.psum_pool(name="psum", bufs=1))
 
         lists = [keep.tile([P, J // 16], U16, name="list%d" % s) for s in range(2)]
@@ -39,20 +38,25 @@ def tile_list_msg_tanh_res_bias_kernel(
         nc.gpsimd.memset(tab_sc[:].bitcast(I32), 0)
         nc.sync.dma_start(lists[0][:], offs)
         nc.sync.dma_start(lists[1][:], offs2)
-        nc.sync.dma_start(out=sm_sb[:], in_=sm.rearrange("(g p t) -> p g t", g=2, t=4))
-        for q in range(4):
-            nc.sync.dma_start(
-                out=tab_sc[32 * q : 32 * q + 8, :].bitcast(I32), in_=tab_scales[:, 4 * q : 4 * q + 4, :].bitcast(I32)
-            )
+
+        def load_sm():
+            nc.sync.dma_start(out=sm_sb[:], in_=sm.rearrange("(g p t) -> p g t", g=2, t=4))
+
+        def load_table_scales():
+            for q in range(4):
+                nc.sync.dma_start(
+                    out=tab_sc[32 * q : 32 * q + 8, :].bitcast(I32), in_=tab_scales[:, 4 * q : 4 * q + 4, :].bitcast(I32)
+                )
+
         weights = (ws, wt)
         steps = [(s, a) for a in range(2) for s in range(2)]
         raw = {}
 
-        def load_w(g, s, a):
-            raw[g, s, a] = stream.tile([P, 4, PASS], F32, name="raw", align_bytes=64)
+        def load_w(g, s, a, tag, pieces=1):
+            raw[g, s, a] = keep.tile([P, 4, PASS], F32, name=tag, align_bytes=64)
             rows = weights[s][PASS * a : PASS * (a + 1), PASS * g : PASS * (g + 1)].rearrange("(p j) c -> p j c", j=4)
-            for j in (0, 2):
-                nc.sync.dma_start(out=raw[g, s, a][:, j : j + 2, :], in_=rows[:, j : j + 2, :])
+            for c in range(0, PASS, PASS // pieces):
+                nc.sync.dma_start(out=raw[g, s, a][:, :, c : c + PASS // pieces], in_=rows[:, :, c : c + PASS // pieces])
 
         def load_table_words():
             nc.sync.dma_start(out=tab_w[:], in_=tab_words[0].rearrange("p t b -> p (t b)").bitcast(I32))
@@ -64,82 +68,100 @@ def tile_list_msg_tanh_res_bias_kernel(
 
         picked_sc = keep.tile([P, 2, J], U8, name="picked_sc", align_bytes=64)
         moved_sc = keep.tile([P, 2, J], U8, name="moved_sc", align_bytes=64)
-        picked_w = keep.tile([P, 2, J], I32, name="picked_w", align_bytes=64)
-        parted = keep.tile([P, 2, 2, 2, 2 * HALF], U8, name="parted", align_bytes=64)
+        parted = {}
 
         def entries(s, j0, j1):
             return lists[s][:, j0 // 16 : j1 // 16]
 
-        def gather_scales(j0, j1):
+        def gather_scales():
             for s in range(2):
-                nc.vector.tensor_copy(picked_sc[:, s, j0:j1], tab_sc[:].indirect(entries(s, j0, j1)))
-                nc.sync.dma_start(
-                    out=moved_sc[0:112, s, j0:j1].bitcast(I32), in_=picked_sc[4:116, s, j0:j1].bitcast(I32)
-                )
+                nc.vector.tensor_copy(picked_sc[:, s, :], tab_sc[:].indirect(lists[s][:]))
 
-        def gather_words(half):
+        def move_scales():
+            nc.gpsimd.dma_start(out=moved_sc[0:112].bitcast(I32), in_=picked_sc[4:116].bitcast(I32))
+
+        def gather_words(half, tag, tag2):
             j0, j1 = HALF * half, HALF * (half + 1)
+            picked_w = keep.tile([P, 2, HALF], I32, name=tag, align_bytes=64)
+            for s in range(2):
+                nc.vector.tensor_copy(picked_w[:, s, :].bitcast(U32), tab_w[:].bitcast(U32).indirect(entries(s, j0, j1)))
+            parted[half] = keep.tile([P, 2, 2, 2 * HALF], U8, name=tag2, align_bytes=64)
             for s in range(2):
                 nc.vector.tensor_copy(
-                    picked_w[:, s, j0:j1].bitcast(U32), tab_w[:].bitcast(U32).indirect(entries(s, j0, j1))
-                )
-            for s in range(2):
-                nc.vector.tensor_copy(
-                    out=parted[:, half, s, :, :].bitcast(U16),
-                    in_=picked_w[:, s, j0:j1].bitcast(U16).rearrange("p (j d) -> p d j", d=2),
+                    out=parted[half][:, s, :, :].bitcast(U16),
+                    in_=picked_w[:, s, :].bitcast(U16).rearrange("p (j d) -> p d j", d=2),
                 )
 
         w_codes = {}
         w_sc = {}
 
-        def prepare_w(g, s, a, on_vector):
-            rounded = ring.tile([P, 4 * PASS], BF16, name="rounded", align_bytes=64)
+        def prepare_w(g, s, a, cuts, tag, pieces=1):
+            rounded = keep.tile([P, 4 * PASS], BF16, name=tag, align_bytes=64)
             dst = rounded[:].rearrange("p (t m j) -> p m j t", t=4, j=4)
             src = raw[g, s, a][:].rearrange("p j (m t) -> p m j t", t=4)
-            cut = P - on_vector
-            if cut > 0:
-                nc.scalar.copy(out=dst[:, 0:cut], in_=src[:, 0:cut])
-            if on_vector > 0:
-                nc.vector.tensor_copy(out=dst[:, cut:P], in_=src[:, cut:P])
+            for m0, m1, on_vector in cuts:
+                if on_vector:
+                    nc.vector.tensor_copy(out=dst[:, m0:m1], in_=src[:, m0:m1])
+                else:
+                    nc.scalar.copy(out=dst[:, m0:m1], in_=src[:, m0:m1])
             w_codes[g, s, a] = keep.tile([P, PASS], U32, name="wc%d%d%d" % (g, s, a), align_bytes=64)
             w_sc[g, s, a] = keep.tile([P, PASS], U8, name="wsc%d%d%d" % (g, s, a), align_bytes=64)
-            nc.vector.quantize_mx(out=w_codes[g, s, a][:].bitcast(FP8X4), scales=w_sc[g, s, a][:], in_=rounded[:])
+            for c in range(0, PASS, PASS // pieces):
+                words = slice(c, c + PASS // pieces)
+                nc.vector.quantize_mx(
+                    out=w_codes[g, s, a][:, words].bitcast(FP8X4),
+                    scales=w_sc[g, s, a][:, words],
+                    in_=rounded[:, 4 * c : 4 * (c + PASS // pieces)],
+                )
+
+        def first_pass(g, half, bank, t, s, a):
+            m = slice(P * t, P * (t + 1))
+            nc.tensor.matmul_mx(
+                out=bank[:],
+                lhsT=w_codes[g, s, a][:, m].bitcast(FP8X4),
+                lhsT_scale=w_sc[g, s, a][:, m],
+                rhs=parted[half][:, s, a, :].bitcast(FP4X4),
+                rhs_scale=(picked_sc, moved_sc)[a][:, s, HALF * half : HALF * (half + 1)],
+                start=((s, a) == steps[0]),
+                stop=((s, a) == steps[-1]),
+            )
 
         def first_product(g, half, bank0):
             banks = [psum.tile([P, HALF], F32, name="bank%d" % (bank0 + t)) for t in range(4)]
             for s, a in steps:
-                plane = (picked_sc, moved_sc)[a]
                 for t in range(4):
-                    m = slice(P * t, P * (t + 1))
-                    nc.tensor.matmul_mx(
-                        out=banks[t][:],
-                        lhsT=w_codes[g, s, a][:, m].bitcast(FP8X4),
-                        lhsT_scale=w_sc[g, s, a][:, m],
-                        rhs=parted[:, half, s, a, :].bitcast(FP4X4),
-                        rhs_scale=plane[:, s, HALF * half : HALF * (half + 1)],
-                        start=((s, a) == steps[0]),
-                        stop=((s, a) == steps[-1]),
-                    )
+                    first_pass(g, half, banks[t], t, s, a)
             return banks
+
+        def first_product_activated(g, half, bank_of, tag):
+            act = keep.tile([P, 4, HALF], F32, name=tag, align_bytes=64)
+            for t in range(4):
+                bank = psum.tile([P, HALF], F32, name="bank%d" % bank_of[t])
+                for s, a in steps:
+                    first_pass(g, half, bank, t, s, a)
+                nc.scalar.activation(out=act[:, t, :], in_=bank[:], func=ACT.Tanh)
+            return act
 
         h_codes = [keep.tile([P, J], U32, name="hc%d" % g, align_bytes=64) for g in range(2)]
         h_sc = [keep.tile([P, J], U8, name="hsc%d" % g, align_bytes=64) for g in range(2)]
         b_sb = keep.tile([P, 4], F32, name="b_sb")
-        wd_sc = keep.tile([P, 2, 2, N], U8, name="wd_sc", align_bytes=64)
 
-        def activate(banks, j0, j1):
+        def activate(banks, j0, j1, tag, pieces=1):
             w = j1 - j0
             c0 = j0 % HALF
-            act = ring.tile([P, 4, w], F32, name="act", bufs=4)
-            for t in range(4):
-                nc.scalar.activation(out=act[:, t, :], in_=banks[t][:, c0 : c0 + w], func=ACT.Tanh)
+            act = keep.tile([P, 4, w], F32, name=tag, align_bytes=64)
+            for c in range(0, w, w // pieces):
+                for t in range(4):
+                    nc.scalar.activation(
+                        out=act[:, t, c : c + w // pieces], in_=banks[t][:, c0 + c : c0 + c + w // pieces], func=ACT.Tanh
+                    )
             return act
 
-        def smooth(g, act, j0, j1, on_vector, c0=0):
+        def smooth(g, act, j0, j1, on_vector, c0, tag):
             w = j1 - j0
-            h = ring.tile([P, w, 4], BF16, name="h", align_bytes=64)
+            h = keep.tile([P, w, 4], BF16, name=tag, align_bytes=64)
             if not on_vector:
-                scaled = ring.tile([P, 4, w], BF16, name="scaled")
+                scaled = ring.tile([P, 4, w], BF16, name="scaled", bufs=2)
                 for t in range(4):
                     nc.scalar.activation(
                         out=scaled[:, t, :], in_=act[:, t, c0 : c0 + w], func=ACT.Copy, scale=sm_sb[:, g, t : t + 1]
@@ -159,10 +181,12 @@ def tile_list_msg_tanh_res_bias_kernel(
                 out=h_codes[g][:, j0:j1].bitcast(FP8X4), scales=h_sc[g][:, j0:j1], in_=h[:].rearrange("p w t -> p (w t)")
             )
 
-        def hidden(g, banks, j0, j1, on_vector):
-            smooth(g, activate(banks, j0, j1), j0, j1, on_vector)
+        placed = {}
 
-        placed = [keep.tile([P, T], F32, name="placed%d" % i) for i in range(4)]
+        def clear(i, tag):
+            placed[i] = keep.tile([P, T], F32, name=tag, align_bytes=64)
+            nc.vector.memset(placed[i][:], 0.0)
+
         second = {}
 
         def load_second():
@@ -174,7 +198,7 @@ def tile_list_msg_tanh_res_bias_kernel(
             second["wgo"] = keep.tile([P, J], F32, name="wgo_sb")
             nc.sync.dma_start(out=second["wgo"][:], in_=wgo)
 
-        def message(j0, j1, i, bank):
+        def message(j0, j1, i, bank, tag=None):
             w = j1 - j0
             step = HALF if w == HALF else P
             y = psum.tile([P, w], F32, name="bank%d" % bank)
@@ -189,13 +213,13 @@ def tile_list_msg_tanh_res_bias_kernel(
                         nc.tensor.matmul_mx(
                             out=y[:, c : c + step],
                             lhsT=lhs,
-                            lhsT_scale=wd_sc[:, tier, g, n],
+                            lhsT_scale=second["scales"][:, tier, g, n],
                             rhs=h_codes[g][:, j0 + c : j0 + c + step].bitcast(FP8X4),
                             rhs_scale=h_sc[g][:, j0 + c : j0 + c + step],
                             start=(g == 0 and tier == 0),
                             stop=(g == 1 and tier == 1),
                         )
-            biased = ring.tile([P, w], F32, name="biased", bufs=12)
+            biased = keep.tile([P, w], F32, name=tag or "biased%d_%d" % (j0, i), align_bytes=64)
             nc.scalar.activation(out=biased[:], in_=y[:], func=ACT.Identity, bias=b_sb[:, i : i + 1])
             return biased
 
@@ -204,12 +228,15 @@ def tile_list_msg_tanh_res_bias_kernel(
                 out=placed[i][:].indirect(entries(1, j0, j1)), in0=biased[:], in1=second["wgo"][:, j0:j1], op=MULT
             )
 
-        def load_second_scales(q):
-            for tier, scales in enumerate((wd4_scales, wd8_scales)):
-                nc.sync.dma_start(
-                    out=wd_sc[32 * q : 32 * q + 4, tier, :, :].bitcast(I32),
-                    in_=scales[:, 4 * q : 4 * q + 4, :].rearrange("a r n -> r a n").bitcast(I32),
-                )
+        def load_second_scales(tag):
+            second["scales"] = keep.tile([P, 2, 2, N], U8, name=tag, align_bytes=64)
+            nc.vector.memset(second["scales"][:].bitcast(I32), 0)
+            for q in range(4):
+                for tier, scales in enumerate((wd4_scales, wd8_scales)):
+                    nc.scalar.dma_start(
+                        out=second["scales"][32 * q : 32 * q + 4, tier, :, :].bitcast(I32),
+                        in_=scales[:, 4 * q : 4 * q + 4, :].rearrange("a r n -> r a n").bitcast(I32),
+                    )
 
         def load_bias():
             with nc.allow_non_contiguous_dma(reason="one bias value for each partition"):
@@ -219,47 +246,54 @@ def tile_list_msg_tanh_res_bias_kernel(
             nc.sync.dma_start(out=out[P * i : P * (i + 1), :], in_=placed[i][:])
 
         nc.vector.memset(moved_sc[:].bitcast(I32), 0)
-        nc.vector.memset(wd_sc[:].bitcast(I32), 0)
-        load_w(0, *steps[0])
+        wtag = ["w0","w1","w2","w3","w4","w0","w1","w2"]
+        load_w(0, *steps[0], wtag[0])
+        load_table_scales()
+        load_w(0, *steps[1], wtag[1])
         load_table_words()
-        gather_scales(0, J)
-        gather_words(0)
-        share = [0,0,0,32,64,64,64,64]
+        load_sm()
+        clear(0, "placed0")
+        clear(1, "placed1")
+        clear(2, "placed2")
+        clear(3, "placed3")
+        load_second_scales("wsc")
+        gather_scales()
+        gather_words(0, "picked", "parted")
+        share = [[[0,128,0]],[[0,128,0]],[[0,128,0]],[[0,128,0]],[[0,96,0],[96,128,1]],[[0,64,0],[64,128,1]],[[0,128,1]],[[0,64,0],[64,96,0],[96,128,1]]]
+        rtag = ["r0","r1","r2","r3","r0","r1","r6","r7"]
         for c in range(4):
-            if c >= 1:
-                load_w(0, *steps[c])
-            prepare_w(0, *steps[c], share[c])
-        gather_words(1)
-        for i in range(4):
-            (nc.vector if i < 4 else nc.gpsimd).memset(placed[i][:], 0.0)
-        early = activate(first_product(0, 0, 0), 0, 512)
-        late = first_product(0, 1, 4)
+            if c >= 2:
+                load_w(0, *steps[c], wtag[c])
+            prepare_w(0, *steps[c], share[c], rtag[c])
+        move_scales()
+        gather_words(1, "r2", "r3")
+        early = activate(first_product(0, 0, 0), 0, 512, "early")
         for c in range(4):
-            load_w(1, *steps[c])
-            load_second_scales(c)
-            prepare_w(1, *steps[c], share[4 + c])
+            load_w(1, *steps[c], wtag[4 + c], 2 if c == 3 else 1)
+            prepare_w(1, *steps[c], share[4 + c], rtag[4 + c], 1 if c == 3 else 1)
         load_second()
         load_bias()
-        smooth(0, early, 0, 256, 1)
-        banks = first_product(1, 0, 0)
-        first = activate(banks, 0, 256)
-        late = activate(late, 512, 1024)
-        smooth(1, first, 0, 256, 1)
-        y0 = [message(0, 256, i, 4 + i) for i in range(4)]
-        smooth(0, early, 256, 512, 1, 256)
-        hidden(1, banks, 256, 512, 0)
-        banks = first_product(1, 1, 0)
-        y1 = [message(256, 512, i, 4 + i) for i in range(4)]
+        smooth(0, early, 0, 256, 1, 0, "r6")
+        banks = first_product(1, 0, 4)
+        smooth(1, activate(banks, 0, 256, "first", 1), 0, 256, 1, 0, "h1")
+        y0 = [message(0, 256, i, 2 + i % 2) for i in range(2)]
         place(0, 256, 0, y0[0])
-        smooth(0, late, 512, 768, 1, 0)
-        smooth(0, late, 768, 1024, 1, 256)
-        last = activate(banks, 512, 1024)
-        smooth(1, last, 512, 768, 0, 0)
-        smooth(1, last, 768, 1024, 0, 256)
+        smooth(0, early, 256, 512, 1, 256, "r7")
+        smooth(1, activate(banks, 256, 512, "second"), 256, 512, 1, 0, "h3")
+        y0 += [message(0, 256, i, 2 + i % 2, ["","","",""][i]) for i in range(2, 4)]
+        late = first_product_activated(0, 1, (0, 1, 0, 1), "w2")
+        last = first_product_activated(1, 1, (4, 5, 6, 7), "early")
+        y1 = [message(256, 512, i, 2 + i % 2) for i in range(1)]
+        smooth(0, late, 512, 768, 0, 0, "h3")
+        smooth(1, last, 512, 768, 0, 0, "h6")
+
+        smooth(0, late, 768, 1024, 1, 256, "h5")
+        smooth(1, last, 768, 1024, 0, 256, "h7")
+        y1 += [message(256, 512, i, 2 + i % 2, ["h6","","",""][i]) for i in range(1, 4)]
         for i in range(1, 4):
             place(0, 256, i, y0[i])
         for i in range(4):
             place(256, 512, i, y1[i])
         for i in range(4):
-            place(512, 1024, i, message(512, 1024, i, 4 + i))
+            place(512, 1024, i, message(512, 1024, i, i % 4))
             store(i)

@@ -19,7 +19,9 @@ MULT = mybir.AluOpType.mult
 P = 128
 PASS = 512
 HALF = 512
-SUB = 128
+CHUNK = 256
+NARROW = 128
+SCALE_ROWS_AT = 96
 
 
 def tile_list_msg_tanh_res_bias_kernel(
@@ -35,265 +37,288 @@ def tile_list_msg_tanh_res_bias_kernel(
         tab_sc = keep.tile([P, T], U8, name="tab_sc", align_bytes=64)
         tab_w = keep.tile([P, T], I32, name="tab_w", align_bytes=64)
         sm_sb = keep.tile([P, 2, 4], F32, name="sm_sb")
-        nc.gpsimd.memset(tab_sc[:].bitcast(I32), 0)
-        nc.sync.dma_start(lists[0][:], offs)
-        nc.sync.dma_start(lists[1][:], offs2)
-
-        def load_sm():
-            nc.sync.dma_start(out=sm_sb[:], in_=sm.rearrange("(g p t) -> p g t", g=2, t=4))
-
-        def load_table_scales():
-            for q in range(4):
-                nc.sync.dma_start(
-                    out=tab_sc[32 * q : 32 * q + 8, :].bitcast(I32), in_=tab_scales[:, 4 * q : 4 * q + 4, :].bitcast(I32)
-                )
+        b_sb = keep.tile([P, 4], F32, name="b_sb")
+        picked_sc = keep.tile([P, 2, J], U8, name="picked_sc", align_bytes=64)
+        planes = [keep.tile([P, 2, J], U8, name="plane%d" % a, align_bytes=64) for a in range(2)]
+        wd_sc = [keep.tile([P, 2, N], U8, name="wd_sc%d" % tier, align_bytes=64) for tier in range(2)]
+        wd4 = keep.tile([P, 2, N // 2], I32, name="wd4", align_bytes=64)
+        wd8 = keep.tile([P, 2, N], I32, name="wd8", align_bytes=64)
+        wgo_sb = keep.tile([P, J], F32, name="wgo_sb")
+        placed = [keep.tile([P, T], F32, name="placed%d" % i, align_bytes=64) for i in range(4)]
+        biased = [keep.tile([P, J], F32, name="biased%d" % i, align_bytes=64) for i in range(4)]
+        h_codes = [keep.tile([P, J], U32, name="hc%d" % g, align_bytes=64) for g in range(2)]
+        h_sc = [keep.tile([P, J], U8, name="hsc%d" % g, align_bytes=64) for g in range(2)]
 
         weights = (ws, wt)
         steps = [(s, a) for a in range(2) for s in range(2)]
-        raw = {}
-
-        def load_w(g, s, a, tag, pieces=1):
-            raw[g, s, a] = keep.tile([P, 4, PASS], F32, name=tag, align_bytes=64)
-            rows = weights[s][PASS * a : PASS * (a + 1), PASS * g : PASS * (g + 1)].rearrange("(p j) c -> p j c", j=4)
-            for c in range(0, PASS, PASS // pieces):
-                nc.sync.dma_start(out=raw[g, s, a][:, :, c : c + PASS // pieces], in_=rows[:, :, c : c + PASS // pieces])
-
-        def load_table_words():
-            nc.sync.dma_start(out=tab_w[:], in_=tab_words[0].rearrange("p t b -> p (t b)").bitcast(I32))
-
-        warm = keep.tile([P, 1], F32, name="warm")
-        nc.vector.memset(warm[:], 0.0)
-        warm2 = keep.tile([P, 1], F32, name="warm2")
-        nc.scalar.activation(out=warm2[:], in_=warm[:], func=ACT.Tanh)
-
-        picked_sc = keep.tile([P, 2, J], U8, name="picked_sc", align_bytes=64)
-        moved_sc = keep.tile([P, 2, J], U8, name="moved_sc", align_bytes=64)
-        parted = {}
+        raw, rounded, w_codes, w_sc, parted, act = {}, {}, {}, {}, {}, {}
 
         def entries(s, j0, j1):
             return lists[s][:, j0 // 16 : j1 // 16]
+
+        def load_w(n, c0=0, c1=PASS):
+            g, (s, a) = n // 4, steps[n % 4]
+            raw[n, c0] = keep.tile([P, 4, c1 - c0], F32, name="raw%d_%d" % (n, c0), align_bytes=64)
+            rows = weights[s][PASS * a : PASS * (a + 1), PASS * g + c0 : PASS * g + c1]
+            nc.sync.dma_start(out=raw[n, c0][:], in_=rows.rearrange("(p j) c -> p j c", j=4))
+
+        def round_w(n, m0, m1, engine, c0=0):
+            if n not in rounded:
+                if n == 7:
+                    rounded[n] = keep.tile([P, 4 * PASS], BF16, name="last", align_bytes=64)
+                else:
+                    rounded[n] = ring.tile([P, 4 * PASS], BF16, name="rounded", align_bytes=64)
+            dst = rounded[n][:].rearrange("p (t m j) -> p m j t", t=4, j=4)[:, m0:m1]
+            src = raw[n, c0][:].rearrange("p j (m t) -> p m j t", t=4)[:, m0 - c0 // 4 : m1 - c0 // 4]
+            if engine == "vector":
+                nc.vector.tensor_copy(out=dst, in_=src)
+            else:
+                nc.scalar.copy(out=dst, in_=src)
+
+        def quantize_w(n, pieces=1, tag=None):
+            w_codes[n] = keep.tile([P, PASS], U32, name=tag or "wc%d" % n, align_bytes=64)
+            w_sc[n] = keep.tile([P, PASS], U8, name="wsc%d" % n, align_bytes=64)
+            step = PASS // pieces
+            for c in range(0, PASS, step):
+                nc.vector.quantize_mx(
+                    out=w_codes[n][:, c : c + step].bitcast(FP8X4),
+                    scales=w_sc[n][:, c : c + step],
+                    in_=rounded[n][:, 4 * c : 4 * (c + step)],
+                )
 
         def gather_scales():
             for s in range(2):
                 nc.vector.tensor_copy(picked_sc[:, s, :], tab_sc[:].indirect(lists[s][:]))
 
-        def move_scales():
-            nc.gpsimd.dma_start(out=moved_sc[0:112].bitcast(I32), in_=picked_sc[4:116].bitcast(I32))
+        def move_scales(a):
+            for q in range(4):
+                row = SCALE_ROWS_AT + 16 * a + 4 * q
+                nc.sync.dma_start(
+                    out=planes[a][32 * q : 32 * q + 4].bitcast(I32), in_=picked_sc[row : row + 4].bitcast(I32)
+                )
 
-        def gather_words(half, tag, tag2):
+        def gather_words(half):
             j0, j1 = HALF * half, HALF * (half + 1)
-            picked_w = keep.tile([P, 2, HALF], I32, name=tag, align_bytes=64)
+            picked_w = keep.tile([P, 2, HALF], I32, name="picked%d" % half, align_bytes=64)
             for s in range(2):
                 nc.vector.tensor_copy(picked_w[:, s, :].bitcast(U32), tab_w[:].bitcast(U32).indirect(entries(s, j0, j1)))
-            parted[half] = keep.tile([P, 2, 2, 2 * HALF], U8, name=tag2, align_bytes=64)
+            parted[half] = keep.tile([P, 2, 2, 2 * HALF], U8, name="parted%d" % half, align_bytes=64)
             for s in range(2):
                 nc.vector.tensor_copy(
                     out=parted[half][:, s, :, :].bitcast(U16),
                     in_=picked_w[:, s, :].bitcast(U16).rearrange("p (j d) -> p d j", d=2),
                 )
 
-        w_codes = {}
-        w_sc = {}
-
-        def prepare_w(g, s, a, cuts, tag, pieces=1):
-            rounded = keep.tile([P, 4 * PASS], BF16, name=tag, align_bytes=64)
-            dst = rounded[:].rearrange("p (t m j) -> p m j t", t=4, j=4)
-            src = raw[g, s, a][:].rearrange("p j (m t) -> p m j t", t=4)
-            for m0, m1, on_vector in cuts:
-                if on_vector:
-                    nc.vector.tensor_copy(out=dst[:, m0:m1], in_=src[:, m0:m1])
-                else:
-                    nc.scalar.copy(out=dst[:, m0:m1], in_=src[:, m0:m1])
-            w_codes[g, s, a] = keep.tile([P, PASS], U32, name="wc%d%d%d" % (g, s, a), align_bytes=64)
-            w_sc[g, s, a] = keep.tile([P, PASS], U8, name="wsc%d%d%d" % (g, s, a), align_bytes=64)
-            for c in range(0, PASS, PASS // pieces):
-                words = slice(c, c + PASS // pieces)
-                nc.vector.quantize_mx(
-                    out=w_codes[g, s, a][:, words].bitcast(FP8X4),
-                    scales=w_sc[g, s, a][:, words],
-                    in_=rounded[:, 4 * c : 4 * (c + PASS // pieces)],
+        def load_wd_scales(tier):
+            scales = (wd4_scales, wd8_scales)[tier]
+            for q in range(4):
+                nc.sync.dma_start(
+                    out=wd_sc[tier][32 * q : 32 * q + 4].bitcast(I32),
+                    in_=scales[:, 4 * q : 4 * q + 4, :].rearrange("a r n -> r a n").bitcast(I32),
                 )
 
-        def first_pass(g, half, bank, t, s, a):
+        def bank(number, width=HALF):
+            return psum.tile([P, width], F32, name="bank%d" % number)
+
+        def first_pass(g, half, sums, t, k):
+            s, a = steps[k]
             m = slice(P * t, P * (t + 1))
             nc.tensor.matmul_mx(
-                out=bank[:],
-                lhsT=w_codes[g, s, a][:, m].bitcast(FP8X4),
-                lhsT_scale=w_sc[g, s, a][:, m],
+                out=sums[:],
+                lhsT=w_codes[4 * g + k][:, m].bitcast(FP8X4),
+                lhsT_scale=w_sc[4 * g + k][:, m],
                 rhs=parted[half][:, s, a, :].bitcast(FP4X4),
-                rhs_scale=(picked_sc, moved_sc)[a][:, s, HALF * half : HALF * (half + 1)],
-                start=((s, a) == steps[0]),
-                stop=((s, a) == steps[-1]),
+                rhs_scale=planes[a][:, s, HALF * half : HALF * (half + 1)],
+                start=(k == 0),
+                stop=(k == 3),
             )
 
-        def first_product(g, half, bank0):
-            banks = [psum.tile([P, HALF], F32, name="bank%d" % (bank0 + t)) for t in range(4)]
-            for s, a in steps:
-                for t in range(4):
-                    first_pass(g, half, banks[t], t, s, a)
-            return banks
+        def first_sum(g, half, t, number):
+            sums = bank(number)
+            for k in range(4):
+                first_pass(g, half, sums, t, k)
+            return sums
 
-        def first_product_activated(g, half, bank_of, tag):
-            act = keep.tile([P, 4, HALF], F32, name=tag, align_bytes=64)
-            for t in range(4):
-                bank = psum.tile([P, HALF], F32, name="bank%d" % bank_of[t])
-                for s, a in steps:
-                    first_pass(g, half, bank, t, s, a)
-                nc.scalar.activation(out=act[:, t, :], in_=bank[:], func=ACT.Tanh)
-            return act
+        def activate(g, sums, t, j0, j1):
+            half = j0 // HALF
+            if (g, half) not in act:
+                act[g, half] = keep.tile([P, 4, HALF], F32, name="raw%d_0" % (4 - len(act)), align_bytes=64)
+            cols = slice(j0 % HALF, j0 % HALF + j1 - j0)
+            nc.scalar.activation(out=act[g, half][:, t, cols], in_=sums[:, cols], func=ACT.Tanh)
 
-        h_codes = [keep.tile([P, J], U32, name="hc%d" % g, align_bytes=64) for g in range(2)]
-        h_sc = [keep.tile([P, J], U8, name="hsc%d" % g, align_bytes=64) for g in range(2)]
-        b_sb = keep.tile([P, 4], F32, name="b_sb")
-
-        def activate(banks, j0, j1, tag, pieces=1):
-            w = j1 - j0
-            c0 = j0 % HALF
-            act = keep.tile([P, 4, w], F32, name=tag, align_bytes=64)
-            for c in range(0, w, w // pieces):
-                for t in range(4):
-                    nc.scalar.activation(
-                        out=act[:, t, c : c + w // pieces], in_=banks[t][:, c0 + c : c0 + c + w // pieces], func=ACT.Tanh
-                    )
-            return act
-
-        def smooth(g, act, j0, j1, on_vector, c0, tag):
-            w = j1 - j0
-            h = keep.tile([P, w, 4], BF16, name=tag, align_bytes=64)
-            if not on_vector:
-                scaled = ring.tile([P, 4, w], BF16, name="scaled", bufs=2)
-                for t in range(4):
-                    nc.scalar.activation(
-                        out=scaled[:, t, :], in_=act[:, t, c0 : c0 + w], func=ACT.Copy, scale=sm_sb[:, g, t : t + 1]
-                    )
-            for c in range(0, w, SUB):
-                dst = h[:, c : c + SUB, :].rearrange("p (c i) t -> p c t i", i=4)
-                if on_vector:
-                    nc.vector.tensor_tensor(
-                        out=dst,
-                        in0=act[:, :, c0 + c : c0 + c + SUB].rearrange("p t (c i) -> p c t i", i=4),
-                        in1=sm_sb[:, g, :].unsqueeze(1).unsqueeze(3).to_broadcast([P, SUB // 4, 4, 4]),
-                        op=MULT,
-                    )
-                else:
-                    nc.scalar.copy(out=dst, in_=scaled[:, :, c : c + SUB].rearrange("p t (c i) -> p c t i", i=4))
+        def quantize_h(g, j0, j1, h):
             nc.vector.quantize_mx(
                 out=h_codes[g][:, j0:j1].bitcast(FP8X4), scales=h_sc[g][:, j0:j1], in_=h[:].rearrange("p w t -> p (w t)")
             )
 
-        placed = {}
+        def by_fours(view):
+            return view.rearrange("p t (c i) -> p c t i", i=4)
 
-        def clear(i, tag):
-            placed[i] = keep.tile([P, T], F32, name=tag, align_bytes=64)
-            nc.vector.memset(placed[i][:], 0.0)
-
-        second = {}
-
-        def load_second():
-            tiers = keep.tile([P, 2, 3 * N // 2], I32, name="tiers", align_bytes=64)
-            second["wd4"] = tiers[:, :, 0 : N // 2]
-            second["wd8"] = tiers[:, :, N // 2 : 3 * N // 2]
-            nc.sync.dma_start(out=second["wd4"], in_=wd4_words.rearrange("a p n -> p a n").bitcast(I32))
-            nc.sync.dma_start(out=second["wd8"], in_=wd8_words.rearrange("a p n i -> p a (n i)").bitcast(I32))
-            second["wgo"] = keep.tile([P, J], F32, name="wgo_sb")
-            nc.sync.dma_start(out=second["wgo"][:], in_=wgo)
-
-        def message(j0, j1, i, bank, tag=None):
+        def smooth_on_vector(g, j0, j1, tag=None):
             w = j1 - j0
-            step = HALF if w == HALF else P
-            y = psum.tile([P, w], F32, name="bank%d" % bank)
-            n = slice(P * i, P * (i + 1))
-            for c in range(0, w, step):
-                for g in range(2):
-                    for tier in range(2):
-                        if tier == 0:
-                            lhs = second["wd4"][:, g, P // 2 * i : P // 2 * (i + 1)].bitcast(FP4X4)
-                        else:
-                            lhs = second["wd8"][:, g, n].bitcast(FP8X4)
-                        nc.tensor.matmul_mx(
-                            out=y[:, c : c + step],
-                            lhsT=lhs,
-                            lhsT_scale=second["scales"][:, tier, g, n],
-                            rhs=h_codes[g][:, j0 + c : j0 + c + step].bitcast(FP8X4),
-                            rhs_scale=h_sc[g][:, j0 + c : j0 + c + step],
-                            start=(g == 0 and tier == 0),
-                            stop=(g == 1 and tier == 1),
-                        )
-            biased = keep.tile([P, w], F32, name=tag or "biased%d_%d" % (j0, i), align_bytes=64)
-            nc.scalar.activation(out=biased[:], in_=y[:], func=ACT.Identity, bias=b_sb[:, i : i + 1])
-            return biased
-
-        def place(j0, j1, i, biased):
+            h = keep.tile([P, w, 4], BF16, name=tag or "h%d_%d" % (g, j0), align_bytes=64)
             nc.vector.tensor_tensor(
-                out=placed[i][:].indirect(entries(1, j0, j1)), in0=biased[:], in1=second["wgo"][:, j0:j1], op=MULT
+                out=h[:].rearrange("p (c i) t -> p c t i", i=4),
+                in0=by_fours(act[g, j0 // HALF][:, :, j0 % HALF : j0 % HALF + w]),
+                in1=sm_sb[:, g, :].unsqueeze(1).unsqueeze(3).to_broadcast([P, w // 4, 4, 4]),
+                op=MULT,
             )
+            return h
 
-        def load_second_scales(tag):
-            second["scales"] = keep.tile([P, 2, 2, N], U8, name=tag, align_bytes=64)
-            nc.vector.memset(second["scales"][:].bitcast(I32), 0)
-            for q in range(4):
-                for tier, scales in enumerate((wd4_scales, wd8_scales)):
-                    nc.scalar.dma_start(
-                        out=second["scales"][32 * q : 32 * q + 4, tier, :, :].bitcast(I32),
-                        in_=scales[:, 4 * q : 4 * q + 4, :].rearrange("a r n -> r a n").bitcast(I32),
-                    )
+        def scale_on_scalar(g, j0):
+            scaled = ring.tile([P, 4, CHUNK], BF16, name="scaled", bufs=2)
+            for t in range(4):
+                nc.scalar.activation(
+                    out=scaled[:, t, :],
+                    in_=act[g, j0 // HALF][:, t, j0 % HALF : j0 % HALF + CHUNK],
+                    func=ACT.Copy,
+                    scale=sm_sb[:, g, t : t + 1],
+                )
+            return scaled
 
-        def load_bias():
-            with nc.allow_non_contiguous_dma(reason="one bias value for each partition"):
-                nc.sync.dma_start(out=b_sb[:], in_=b.rearrange("(i p) -> p i", p=P))
+        def weave_on_scalar(g, j0, scaled):
+            h = keep.tile([P, CHUNK, 4], BF16, name="h%d_%d" % (g, j0), align_bytes=64)
+            nc.scalar.copy(out=h[:].rearrange("p (c i) t -> p c t i", i=4), in_=by_fours(scaled[:]))
+            quantize_h(g, j0, j0 + CHUNK, h)
 
-        def store(i):
-            nc.sync.dma_start(out=out[P * i : P * (i + 1), :], in_=placed[i][:])
+        sent = []
 
-        nc.vector.memset(moved_sc[:].bitcast(I32), 0)
-        wtag = ["w0","w1","w2","w3","w4","w0","w1","w2"]
-        load_w(0, *steps[0], wtag[0])
-        load_table_scales()
-        load_w(0, *steps[1], wtag[1])
-        load_table_words()
-        load_sm()
-        clear(0, "placed0")
-        clear(1, "placed1")
-        clear(2, "placed2")
-        clear(3, "placed3")
-        load_second_scales("wsc")
+        def message(i, j0, j1, groups):
+            w = j1 - j0
+            y = bank(len(sent) if len(sent) < 4 else len(sent) % 2, w)
+            sent.append((i, j0))
+            n = slice(P * i, P * (i + 1))
+            passes = []
+            for g in groups:
+                narrow = [(c, c + NARROW) for c in range(0, w, NARROW)] if w < HALF else [(0, w)]
+                if j0 == 0 and g == groups[-1]:
+                    passes += [(g, tier, cols) for cols in narrow for tier in (1, 0)]
+                else:
+                    passes += [(g, 1, (0, w))] + [(g, 0, cols) for cols in narrow]
+            for number, (g, tier, (c0, c1)) in enumerate(passes):
+                if tier == 0:
+                    lhs = wd4[:, g, P // 2 * i : P // 2 * (i + 1)].bitcast(FP4X4)
+                else:
+                    lhs = wd8[:, g, n].bitcast(FP8X4)
+                nc.tensor.matmul_mx(
+                    out=y[:, c0:c1],
+                    lhsT=lhs,
+                    lhsT_scale=wd_sc[tier][:, g, n],
+                    rhs=h_codes[g][:, j0 + c0 : j0 + c1].bitcast(FP8X4),
+                    rhs_scale=h_sc[g][:, j0 + c0 : j0 + c1],
+                    start=(number == 0),
+                    stop=(number == len(passes) - 1),
+                )
+            nc.scalar.activation(out=biased[i][:, j0:j1], in_=y[:], func=ACT.Identity, bias=b_sb[:, i : i + 1])
+            nc.vector.tensor_tensor(
+                out=placed[i][:].indirect(entries(1, j0, j1)), in0=biased[i][:, j0:j1], in1=wgo_sb[:, j0:j1], op=MULT
+            )
+            if j1 == J:
+                nc.sync.dma_start(out=out[n, :], in_=placed[i][:])
+
+        nc.gpsimd.memset(tab_sc[0:SCALE_ROWS_AT].bitcast(I32), 0)
+        nc.sync.dma_start(lists[0][:], offs)
+        nc.sync.dma_start(lists[1][:], offs2)
+        nc.sync.dma_start(
+            out=tab_sc[SCALE_ROWS_AT:P].bitcast(I32), in_=tab_scales.rearrange("a q t -> (a q) t").bitcast(I32)
+        )
+        load_w(0)
+        nc.sync.dma_start(out=tab_w[:], in_=tab_words[0].rearrange("p t b -> p (t b)").bitcast(I32))
+        warm = keep.tile([P, 1], F32, name="warm")
+        nc.vector.memset(warm[:], 0.0)
+        warmed = keep.tile([P, 1], F32, name="warmed")
+        nc.scalar.activation(out=warmed[:], in_=warm[:], func=ACT.Tanh)
+        for plane in planes + wd_sc:
+            nc.vector.memset(plane[:].bitcast(I32), 0)
+        for i in range(4):
+            for c in range(0, T, T // 2):
+                nc.gpsimd.memset(placed[i][:, c : c + T // 2], 0.0)
+
         gather_scales()
-        gather_words(0, "picked", "parted")
-        share = [[[0,128,0]],[[0,128,0]],[[0,128,0]],[[0,128,0]],[[0,96,0],[96,128,1]],[[0,64,0],[64,128,1]],[[0,128,1]],[[0,64,0],[64,96,0],[96,128,1]]]
-        rtag = ["r0","r1","r2","r3","r0","r1","r6","r7"]
-        for c in range(4):
-            if c >= 2:
-                load_w(0, *steps[c], wtag[c])
-            prepare_w(0, *steps[c], share[c], rtag[c])
-        move_scales()
-        gather_words(1, "r2", "r3")
-        early = activate(first_product(0, 0, 0), 0, 512, "early")
-        for c in range(4):
-            load_w(1, *steps[c], wtag[4 + c], 2 if c == 3 else 1)
-            prepare_w(1, *steps[c], share[4 + c], rtag[4 + c], 1 if c == 3 else 1)
-        load_second()
-        load_bias()
-        smooth(0, early, 0, 256, 1, 0, "r6")
-        banks = first_product(1, 0, 4)
-        smooth(1, activate(banks, 0, 256, "first", 1), 0, 256, 1, 0, "h1")
-        y0 = [message(0, 256, i, 2 + i % 2) for i in range(2)]
-        place(0, 256, 0, y0[0])
-        smooth(0, early, 256, 512, 1, 256, "r7")
-        smooth(1, activate(banks, 256, 512, "second"), 256, 512, 1, 0, "h3")
-        y0 += [message(0, 256, i, 2 + i % 2, ["","","",""][i]) for i in range(2, 4)]
-        late = first_product_activated(0, 1, (0, 1, 0, 1), "w2")
-        last = first_product_activated(1, 1, (4, 5, 6, 7), "early")
-        y1 = [message(256, 512, i, 2 + i % 2) for i in range(1)]
-        smooth(0, late, 512, 768, 0, 0, "h3")
-        smooth(1, last, 512, 768, 0, 0, "h6")
+        round_w(0, 0, P, "scalar")
+        quantize_w(0)
+        gather_words(0)
+        load_w(1)
+        load_w(2)
+        move_scales(0)
+        load_w(3)
+        move_scales(1)
+        load_w(4)
+        nc.sync.dma_start(out=sm_sb[:], in_=sm.rearrange("(g p t) -> p g t", g=2, t=4))
+        load_wd_scales(0)
+        load_w(5)
+        load_wd_scales(1)
+        load_w(6)
+        load_w(7, 0, PASS // 2)
+        load_w(7, PASS // 2, PASS)
+        nc.sync.dma_start(out=wd8[:], in_=wd8_words.rearrange("a p n i -> p a (n i)").bitcast(I32))
+        nc.sync.dma_start(out=wd4[:], in_=wd4_words.rearrange("a p n -> p a n").bitcast(I32))
+        with nc.allow_non_contiguous_dma(reason="one bias value for each partition"):
+            nc.sync.dma_start(out=b_sb[:], in_=b.rearrange("(i p) -> p i", p=P))
+        nc.sync.dma_start(out=wgo_sb[:], in_=wgo)
 
-        smooth(0, late, 768, 1024, 1, 256, "h5")
-        smooth(1, last, 768, 1024, 0, 256, "h7")
-        y1 += [message(256, 512, i, 2 + i % 2, ["h6","","",""][i]) for i in range(1, 4)]
-        for i in range(1, 4):
-            place(0, 256, i, y0[i])
-        for i in range(4):
-            place(256, 512, i, y1[i])
-        for i in range(4):
-            place(512, 1024, i, message(512, 1024, i, i % 4))
-            store(i)
+        for n in range(1, 4):
+            round_w(n, 0, P, "scalar")
+            quantize_w(n)
+        gather_words(1)
+        sums = [bank(t) for t in range(4)]
+        for k in range(4):
+            for t in range(4):
+                first_pass(0, 0, sums[t], t, k)
+        round_w(4, 0, P, "scalar")
+        for t in range(4):
+            activate(0, sums[t], t, 0, HALF)
+        round_w(5, 0, P, "vector")
+        quantize_w(4, tag="raw5_0")
+        quantize_w(5)
+        round_w(6, 0, P, "vector")
+        quantize_w(6)
+        round_w(7, 0, P // 2, "scalar")
+        round_w(7, P // 2, P, "vector", PASS // 2)
+        quantize_w(7, 4)
+        sums = [bank(4 + t) for t in range(4)]
+        for k in range(4):
+            for t in range(4):
+                first_pass(1, 0, sums[t], t, k)
+        quantize_h(0, 0, CHUNK, smooth_on_vector(0, 0, CHUNK, "last"))
+        for j0 in range(0, CHUNK, NARROW):
+            for t in range(4):
+                activate(1, sums[t], t, j0, j0 + NARROW)
+            quantize_h(1, j0, j0 + NARROW, smooth_on_vector(1, j0, j0 + NARROW, "h1_%d" % j0))
+        h = smooth_on_vector(0, CHUNK, HALF, "h1_%d" % NARROW)
+        for t in range(4):
+            activate(1, sums[t], t, CHUNK, HALF)
+
+        c0, c1, c2, c3 = 0, CHUNK, 2 * CHUNK, 3 * CHUNK
+        message(0, c0, c1, (0, 1))
+        quantize_h(0, c1, c2, h)
+        scaled = scale_on_scalar(1, c1)
+        message(1, c0, c1, (0, 1))
+        weave_on_scalar(1, c1, scaled)
+        message(2, c0, c1, (0, 1))
+        for t in range(2):
+            activate(1, first_sum(1, 1, t, 4 + t), t, HALF, J)
+        message(3, c0, c1, (0, 1))
+        for t in range(2, 4):
+            activate(1, first_sum(1, 1, t, 4 + t), t, HALF, J)
+        message(0, c1, c2, (0, 1))
+        scaled = scale_on_scalar(1, c2)
+        message(1, c1, c2, (0, 1))
+        weave_on_scalar(1, c2, scaled)
+        message(2, c1, c2, (0, 1))
+        sums = [first_sum(0, 1, t, (2, 3, 4, 5)[t]) for t in range(4)]
+        for t in range(4):
+            activate(0, sums[t], t, c2, c3)
+        quantize_h(0, c2, c3, smooth_on_vector(0, c2, c3))
+        message(3, c1, c2, (0, 1))
+        for t in range(4):
+            activate(0, sums[t], t, c3, J)
+        weave_on_scalar(1, c3, scale_on_scalar(1, c3))
+        message(0, c2, c3, (1, 0))
+        scaled = scale_on_scalar(0, c3)
+        message(1, c2, c3, (1, 0))
+        weave_on_scalar(0, c3, scaled)
+        message(2, c2, c3, (1, 0))
+        for i in range(3):
+            message(i, c3, J, (1, 0))
+        message(3, c2, J, (1, 0))

@@ -44,7 +44,7 @@ def tile_list_msg_tanh_res_bias_kernel(
         wd4 = keep.tile([P, 2, N // 2], I32, name="wd4", align_bytes=64)
         wd8 = keep.tile([P, 2, N], I32, name="wd8", align_bytes=64)
         wgo_sb = keep.tile([P, J], F32, name="wgo_sb")
-        placed = [keep.tile([P, T], F32, name="placed%d" % i, align_bytes=64) for i in range(4)]
+        placed = {}
         biased = [keep.tile([P, J], F32, name="biased%d" % i, align_bytes=64) for i in range(4)]
         h_codes = [keep.tile([P, J], U32, name="hc%d" % g, align_bytes=64) for g in range(2)]
         h_sc = [keep.tile([P, J], U8, name="hsc%d" % g, align_bytes=64) for g in range(2)]
@@ -67,7 +67,7 @@ def tile_list_msg_tanh_res_bias_kernel(
                 if n == 7:
                     rounded[n] = keep.tile([P, 4 * PASS], BF16, name="last", align_bytes=64)
                 else:
-                    rounded[n] = ring.tile([P, 4 * PASS], BF16, name="rounded", align_bytes=64)
+                    rounded[n] = ring.tile([P, 4 * PASS], BF16, name="rounded", align_bytes=64, bufs=4)
             dst = rounded[n][:].rearrange("p (t m j) -> p m j t", t=4, j=4)[:, m0:m1]
             src = raw[n, c0][:].rearrange("p j (m t) -> p m j t", t=4)[:, m0 - c0 // 4 : m1 - c0 // 4]
             if engine == "vector":
@@ -86,6 +86,10 @@ def tile_list_msg_tanh_res_bias_kernel(
                     in_=rounded[n][:, 4 * c : 4 * (c + step)],
                 )
 
+        def clear(i, tag):
+            placed[i] = keep.tile([P, T], F32, name=tag, align_bytes=64)
+            nc.vector.memset(placed[i][:], 0.0)
+
         def gather_scales():
             for s in range(2):
                 nc.vector.tensor_copy(picked_sc[:, s, :], tab_sc[:].indirect(lists[s][:]))
@@ -97,9 +101,9 @@ def tile_list_msg_tanh_res_bias_kernel(
                     out=planes[a][32 * q : 32 * q + 4].bitcast(I32), in_=picked_sc[row : row + 4].bitcast(I32)
                 )
 
-        def gather_words(half):
+        def gather_words(half, tag):
             j0, j1 = HALF * half, HALF * (half + 1)
-            picked_w = keep.tile([P, 2, HALF], I32, name="picked%d" % half, align_bytes=64)
+            picked_w = keep.tile([P, 2, HALF], I32, name=tag, align_bytes=64)
             for s in range(2):
                 nc.vector.tensor_copy(picked_w[:, s, :].bitcast(U32), tab_w[:].bitcast(U32).indirect(entries(s, j0, j1)))
             parted[half] = keep.tile([P, 2, 2, 2 * HALF], U8, name="parted%d" % half, align_bytes=64)
@@ -142,7 +146,7 @@ def tile_list_msg_tanh_res_bias_kernel(
         def activate(g, sums, t, j0, j1):
             half = j0 // HALF
             if (g, half) not in act:
-                act[g, half] = keep.tile([P, 4, HALF], F32, name="raw%d_0" % (4 - len(act)), align_bytes=64)
+                act[g, half] = keep.tile([P, 4, HALF], F32, name=("raw7_0", "raw4_0", "raw5_0", "act")[len(act)], align_bytes=64)
             cols = slice(j0 % HALF, j0 % HALF + j1 - j0)
             nc.scalar.activation(out=act[g, half][:, t, cols], in_=sums[:, cols], func=ACT.Tanh)
 
@@ -216,7 +220,7 @@ def tile_list_msg_tanh_res_bias_kernel(
             if j1 == J:
                 nc.sync.dma_start(out=out[n, :], in_=placed[i][:])
 
-        nc.gpsimd.memset(tab_sc[0:SCALE_ROWS_AT].bitcast(I32), 0)
+        nc.vector.memset(tab_sc[0:SCALE_ROWS_AT].bitcast(I32), 0)
         nc.sync.dma_start(lists[0][:], offs)
         nc.sync.dma_start(lists[1][:], offs2)
         nc.sync.dma_start(
@@ -230,14 +234,13 @@ def tile_list_msg_tanh_res_bias_kernel(
         nc.scalar.activation(out=warmed[:], in_=warm[:], func=ACT.Tanh)
         for plane in planes + wd_sc:
             nc.vector.memset(plane[:].bitcast(I32), 0)
-        for i in range(4):
-            for c in range(0, T, T // 2):
-                nc.gpsimd.memset(placed[i][:, c : c + T // 2], 0.0)
 
         gather_scales()
+        clear(0, "page0")
         round_w(0, 0, P, "scalar")
         quantize_w(0)
-        gather_words(0)
+        gather_words(0, "picked0")
+        clear(1, "raw0_0")
         load_w(1)
         load_w(2)
         move_scales(0)
@@ -260,20 +263,23 @@ def tile_list_msg_tanh_res_bias_kernel(
         for n in range(1, 4):
             round_w(n, 0, P, "scalar")
             quantize_w(n)
-        gather_words(1)
+        clear(2, "raw1_0")
+        gather_words(1, "raw2_0")
+        clear(3, "raw3_0")
         sums = [bank(t) for t in range(4)]
         for k in range(4):
             for t in range(4):
                 first_pass(0, 0, sums[t], t, k)
         round_w(4, 0, P, "scalar")
-        for t in range(4):
-            activate(0, sums[t], t, 0, HALF)
-        round_w(5, 0, P, "vector")
-        quantize_w(4, tag="raw5_0")
-        quantize_w(5)
+        quantize_w(4)
+        round_w(5, 0, P, "scalar")
         round_w(6, 0, P, "vector")
+        quantize_w(5, tag="raw6_0")
         quantize_w(6)
         round_w(7, 0, P // 2, "scalar")
+        for j0 in range(0, HALF, CHUNK):
+            for t in range(4):
+                activate(0, sums[t], t, j0, j0 + CHUNK)
         round_w(7, P // 2, P, "vector", PASS // 2)
         quantize_w(7, 4)
         sums = [bank(4 + t) for t in range(4)]

@@ -22,6 +22,7 @@ HALF = 512
 CHUNK = 256
 NARROW = 128
 SCALE_ROWS_AT = 96
+PAGE = 4 * T
 
 
 def tile_list_msg_tanh_res_bias_kernel(
@@ -31,6 +32,7 @@ def tile_list_msg_tanh_res_bias_kernel(
     with ExitStack() as ctx:
         keep = ctx.enter_context(tc.tile_pool(name="keep", bufs=1))
         ring = ctx.enter_context(tc.tile_pool(name="ring", bufs=3))
+        late = ctx.enter_context(tc.tile_pool(name="late", bufs=1))
         psum = ctx.enter_context(tc.psum_pool(name="psum", bufs=1))
 
         lists = [keep.tile([P, J // 16], U16, name="list%d" % s) for s in range(2)]
@@ -90,6 +92,11 @@ def tile_list_msg_tanh_res_bias_kernel(
             placed[i] = keep.tile([P, T], F32, name=tag, align_bytes=64)
             nc.vector.memset(placed[i][:], 0.0)
 
+        def clear_late(i, offset):
+            placed[i] = late.tile([P, T], F32, name="page%d" % i, align_bytes=64, offset=offset)
+            for c in range(0, T, HALF):
+                nc.gpsimd.memset(placed[i][:, c : c + HALF], 0.0)
+
         def gather_scales():
             for s in range(2):
                 nc.vector.tensor_copy(picked_sc[:, s, :], tab_sc[:].indirect(lists[s][:]))
@@ -146,7 +153,7 @@ def tile_list_msg_tanh_res_bias_kernel(
         def activate(g, sums, t, j0, j1):
             half = j0 // HALF
             if (g, half) not in act:
-                act[g, half] = keep.tile([P, 4, HALF], F32, name=("raw7_0", "raw4_0", "raw5_0", "act")[len(act)], align_bytes=64)
+                act[g, half] = keep.tile([P, 4, HALF], F32, name=("raw4_0", "raw3_0", "raw1_0", "raw0_0")[len(act)], align_bytes=64)
             cols = slice(j0 % HALF, j0 % HALF + j1 - j0)
             nc.scalar.activation(out=act[g, half][:, t, cols], in_=sums[:, cols], func=ACT.Tanh)
 
@@ -158,9 +165,12 @@ def tile_list_msg_tanh_res_bias_kernel(
         def by_fours(view):
             return view.rearrange("p t (c i) -> p c t i", i=4)
 
-        def smooth_on_vector(g, j0, j1, tag=None):
+        def smooth_on_vector(g, j0, j1, tag=None, offset=None):
             w = j1 - j0
-            h = keep.tile([P, w, 4], BF16, name=tag or "h%d_%d" % (g, j0), align_bytes=64)
+            if offset is None:
+                h = keep.tile([P, w, 4], BF16, name=tag or "h%d_%d" % (g, j0), align_bytes=64)
+            else:
+                h = late.tile([P, w, 4], BF16, name="h%d_%d" % (g, j0), align_bytes=64, offset=offset)
             nc.vector.tensor_tensor(
                 out=h[:].rearrange("p (c i) t -> p c t i", i=4),
                 in0=by_fours(act[g, j0 // HALF][:, :, j0 % HALF : j0 % HALF + w]),
@@ -240,22 +250,21 @@ def tile_list_msg_tanh_res_bias_kernel(
         round_w(0, 0, P, "scalar")
         quantize_w(0)
         gather_words(0, "picked0")
-        clear(1, "raw0_0")
+        nc.sync.dma_start(out=sm_sb[:], in_=sm.rearrange("(g p t) -> p g t", g=2, t=4))
         load_w(1)
         load_w(2)
         move_scales(0)
         load_w(3)
-        move_scales(1)
         load_w(4)
-        nc.sync.dma_start(out=sm_sb[:], in_=sm.rearrange("(g p t) -> p g t", g=2, t=4))
-        load_wd_scales(0)
+        move_scales(1)
         load_w(5)
-        load_wd_scales(1)
         load_w(6)
+        load_wd_scales(1)
         load_w(7, 0, PASS // 2)
         load_w(7, PASS // 2, PASS)
         nc.sync.dma_start(out=wd8[:], in_=wd8_words.rearrange("a p n i -> p a (n i)").bitcast(I32))
         nc.sync.dma_start(out=wd4[:], in_=wd4_words.rearrange("a p n -> p a n").bitcast(I32))
+        load_wd_scales(0)
         with nc.allow_non_contiguous_dma(reason="one bias value for each partition"):
             nc.sync.dma_start(out=b_sb[:], in_=b.rearrange("(i p) -> p i", p=P))
         nc.sync.dma_start(out=wgo_sb[:], in_=wgo)
@@ -263,24 +272,22 @@ def tile_list_msg_tanh_res_bias_kernel(
         for n in range(1, 4):
             round_w(n, 0, P, "scalar")
             quantize_w(n)
-        clear(2, "raw1_0")
         gather_words(1, "raw2_0")
-        clear(3, "raw3_0")
         sums = [bank(t) for t in range(4)]
         for k in range(4):
             for t in range(4):
                 first_pass(0, 0, sums[t], t, k)
         round_w(4, 0, P, "scalar")
-        quantize_w(4)
-        round_w(5, 0, P, "scalar")
+        for t in range(4):
+            activate(0, sums[t], t, 0, HALF)
+        round_w(5, 0, P, "vector")
+        quantize_w(4, tag="raw5_0")
+        quantize_w(5)
         round_w(6, 0, P, "vector")
-        quantize_w(5, tag="raw6_0")
         quantize_w(6)
         round_w(7, 0, P // 2, "scalar")
-        for j0 in range(0, HALF, CHUNK):
-            for t in range(4):
-                activate(0, sums[t], t, j0, j0 + CHUNK)
-        round_w(7, P // 2, P, "vector", PASS // 2)
+        round_w(7, P // 2, 104, "vector", PASS // 2)
+        round_w(7, 104, P, "scalar", PASS // 2)
         quantize_w(7, 4)
         sums = [bank(4 + t) for t in range(4)]
         for k in range(4):
@@ -290,14 +297,17 @@ def tile_list_msg_tanh_res_bias_kernel(
         for j0 in range(0, CHUNK, NARROW):
             for t in range(4):
                 activate(1, sums[t], t, j0, j0 + NARROW)
-            quantize_h(1, j0, j0 + NARROW, smooth_on_vector(1, j0, j0 + NARROW, "h1_%d" % j0))
-        h = smooth_on_vector(0, CHUNK, HALF, "h1_%d" % NARROW)
+            quantize_h(1, j0, j0 + NARROW, smooth_on_vector(1, j0, j0 + NARROW, offset=(2 * PAGE, PAGE - 512)[j0 // NARROW]))
+        h = smooth_on_vector(0, CHUNK, HALF, offset=PAGE - 2048)
+        clear_late(1, 2 * PAGE)
+        clear_late(2, PAGE)
         for t in range(4):
             activate(1, sums[t], t, CHUNK, HALF)
 
         c0, c1, c2, c3 = 0, CHUNK, 2 * CHUNK, 3 * CHUNK
         message(0, c0, c1, (0, 1))
         quantize_h(0, c1, c2, h)
+        clear_late(3, 0)
         scaled = scale_on_scalar(1, c1)
         message(1, c0, c1, (0, 1))
         weave_on_scalar(1, c1, scaled)

@@ -22,7 +22,6 @@ HALF = 512
 CHUNK = 256
 NARROW = 128
 SCALE_ROWS_AT = 96
-PAGE = 4 * T
 
 
 def tile_list_msg_tanh_res_bias_kernel(
@@ -32,7 +31,6 @@ def tile_list_msg_tanh_res_bias_kernel(
     with ExitStack() as ctx:
         keep = ctx.enter_context(tc.tile_pool(name="keep", bufs=1))
         ring = ctx.enter_context(tc.tile_pool(name="ring", bufs=3))
-        late = ctx.enter_context(tc.tile_pool(name="late", bufs=1))
         psum = ctx.enter_context(tc.psum_pool(name="psum", bufs=1))
 
         lists = [keep.tile([P, J // 16], U16, name="list%d" % s) for s in range(2)]
@@ -90,12 +88,7 @@ def tile_list_msg_tanh_res_bias_kernel(
 
         def clear(i, tag):
             placed[i] = keep.tile([P, T], F32, name=tag, align_bytes=64)
-            nc.vector.memset(placed[i][:], 0.0)
-
-        def clear_late(i, offset):
-            placed[i] = late.tile([P, T], F32, name="page%d" % i, align_bytes=64, offset=offset)
-            for c in range(0, T, HALF):
-                nc.gpsimd.memset(placed[i][:, c : c + HALF], 0.0)
+            nc.vector.memset(placed[i][:].bitcast(I32), 0)
 
         def gather_scales():
             for s in range(2):
@@ -150,12 +143,51 @@ def tile_list_msg_tanh_res_bias_kernel(
                 first_pass(g, half, sums, t, k)
             return sums
 
-        def activate(g, sums, t, j0, j1):
-            half = j0 // HALF
+        def narrow_passes(g, j0, sums, k):
+            s, a = steps[k]
+            c0 = j0 % HALF
+            for t in range(4):
+                m = slice(P * t, P * (t + 1))
+                nc.tensor.matmul_mx(
+                    out=sums[:, NARROW * t : NARROW * (t + 1)],
+                    lhsT=w_codes[4 * g + k][:, m].bitcast(FP8X4),
+                    lhsT_scale=w_sc[4 * g + k][:, m],
+                    rhs=parted[j0 // HALF][:, s, a, 2 * c0 : 2 * (c0 + NARROW)].bitcast(FP4X4),
+                    rhs_scale=planes[a][:, s, j0 : j0 + NARROW],
+                    start=(k == 0 and t == 0),
+                    stop=(k == 3 and t == 3),
+                )
+
+        def narrow_sums(g, j0, numbers):
+            sums = [bank(number) for number in numbers]
+            for k in range(4):
+                for x in range(len(numbers)):
+                    narrow_passes(g, j0 + NARROW * x, sums[x], k)
+            return sums
+
+        def act_tile(g, half):
             if (g, half) not in act:
-                act[g, half] = keep.tile([P, 4, HALF], F32, name=("raw4_0", "raw3_0", "raw1_0", "raw0_0")[len(act)], align_bytes=64)
-            cols = slice(j0 % HALF, j0 % HALF + j1 - j0)
-            nc.scalar.activation(out=act[g, half][:, t, cols], in_=sums[:, cols], func=ACT.Tanh)
+                act[g, half] = keep.tile([P, 4 * HALF], F32, name=("raw7_0", "raw0_0", "raw1_0", "raw3_0")[len(act)], align_bytes=64)
+            return act[g, half]
+
+        def woven(g, j0, j1):
+            return act_tile(g, j0 // HALF)[:, 4 * (j0 % HALF) : 4 * (j0 % HALF + j1 - j0)].rearrange("p (j t) -> p j t", t=4)
+
+        def planar(g, j0):
+            return act_tile(g, j0 // HALF)[:, 4 * (j0 % HALF) : 4 * (j0 % HALF + CHUNK)].rearrange("p (t j) -> p t j", t=4)
+
+        def activate_woven(g, sums, j0):
+            nc.scalar.activation(out=woven(g, j0, j0 + NARROW), in_=sums[:].rearrange("p (t j) -> p j t", t=4), func=ACT.Tanh)
+
+        def activate_planar(g, sums, j0):
+            c0 = j0 % CHUNK
+            nc.scalar.activation(
+                out=planar(g, j0 - c0)[:, :, c0 : c0 + NARROW], in_=sums[:].rearrange("p (t j) -> p t j", t=4), func=ACT.Tanh
+            )
+
+        def activate(g, sums, t, j0, j1):
+            out_view = act_tile(g, j0 // HALF)[:].rearrange("p (c t j) -> p c t j", c=2, t=4)[:, :, t, :]
+            nc.scalar.activation(out=out_view, in_=sums[:].rearrange("p (c j) -> p c j", c=2), func=ACT.Tanh)
 
         def quantize_h(g, j0, j1, h):
             nc.vector.quantize_mx(
@@ -165,16 +197,13 @@ def tile_list_msg_tanh_res_bias_kernel(
         def by_fours(view):
             return view.rearrange("p t (c i) -> p c t i", i=4)
 
-        def smooth_on_vector(g, j0, j1, tag=None, offset=None):
+        def smooth_on_vector(g, j0, j1, tag=None):
             w = j1 - j0
-            if offset is None:
-                h = keep.tile([P, w, 4], BF16, name=tag or "h%d_%d" % (g, j0), align_bytes=64)
-            else:
-                h = late.tile([P, w, 4], BF16, name="h%d_%d" % (g, j0), align_bytes=64, offset=offset)
+            h = keep.tile([P, w, 4], BF16, name=tag or "h%d_%d" % (g, j0), align_bytes=64)
             nc.vector.tensor_tensor(
-                out=h[:].rearrange("p (c i) t -> p c t i", i=4),
-                in0=by_fours(act[g, j0 // HALF][:, :, j0 % HALF : j0 % HALF + w]),
-                in1=sm_sb[:, g, :].unsqueeze(1).unsqueeze(3).to_broadcast([P, w // 4, 4, 4]),
+                out=h[:],
+                in0=woven(g, j0, j1),
+                in1=sm_sb[:, g, :].unsqueeze(1).to_broadcast([P, w, 4]),
                 op=MULT,
             )
             return h
@@ -184,7 +213,7 @@ def tile_list_msg_tanh_res_bias_kernel(
             for t in range(4):
                 nc.scalar.activation(
                     out=scaled[:, t, :],
-                    in_=act[g, j0 // HALF][:, t, j0 % HALF : j0 % HALF + CHUNK],
+                    in_=planar(g, j0)[:, t, :],
                     func=ACT.Copy,
                     scale=sm_sb[:, g, t : t + 1],
                 )
@@ -237,7 +266,6 @@ def tile_list_msg_tanh_res_bias_kernel(
             out=tab_sc[SCALE_ROWS_AT:P].bitcast(I32), in_=tab_scales.rearrange("a q t -> (a q) t").bitcast(I32)
         )
         load_w(0)
-        nc.sync.dma_start(out=tab_w[:], in_=tab_words[0].rearrange("p t b -> p (t b)").bitcast(I32))
         warm = keep.tile([P, 1], F32, name="warm")
         nc.vector.memset(warm[:], 0.0)
         warmed = keep.tile([P, 1], F32, name="warmed")
@@ -246,13 +274,12 @@ def tile_list_msg_tanh_res_bias_kernel(
             nc.vector.memset(plane[:].bitcast(I32), 0)
 
         gather_scales()
-        clear(0, "page0")
         round_w(0, 0, P, "scalar")
         quantize_w(0)
-        gather_words(0, "picked0")
         nc.sync.dma_start(out=sm_sb[:], in_=sm.rearrange("(g p t) -> p g t", g=2, t=4))
         load_w(1)
         load_w(2)
+        nc.sync.dma_start(out=tab_w[:], in_=tab_words[0].rearrange("p t b -> p (t b)").bitcast(I32))
         move_scales(0)
         load_w(3)
         load_w(4)
@@ -272,42 +299,35 @@ def tile_list_msg_tanh_res_bias_kernel(
         for n in range(1, 4):
             round_w(n, 0, P, "scalar")
             quantize_w(n)
+        gather_words(0, "picked0")
         gather_words(1, "raw2_0")
-        sums = [bank(t) for t in range(4)]
-        for k in range(4):
-            for t in range(4):
-                first_pass(0, 0, sums[t], t, k)
+        for i in range(4):
+            clear(i, "page%d" % i)
+        sums = narrow_sums(0, 0, range(4))
         round_w(4, 0, P, "scalar")
-        for t in range(4):
-            activate(0, sums[t], t, 0, HALF)
-        round_w(5, 0, P, "vector")
-        quantize_w(4, tag="raw5_0")
-        quantize_w(5)
-        round_w(6, 0, P, "vector")
+        quantize_w(4)
+        round_w(5, 0, P, "scalar")
+        round_w(6, 0, 96, "vector")
+        round_w(6, 96, P, "scalar")
+        quantize_w(5, tag="raw6_0")
         quantize_w(6)
         round_w(7, 0, P // 2, "scalar")
-        round_w(7, P // 2, 104, "vector", PASS // 2)
-        round_w(7, 104, P, "scalar", PASS // 2)
+        for x in range(4):
+            activate_woven(0, sums[x], NARROW * x)
+        round_w(7, P // 2, P, "vector", PASS // 2)
         quantize_w(7, 4)
-        sums = [bank(4 + t) for t in range(4)]
-        for k in range(4):
-            for t in range(4):
-                first_pass(1, 0, sums[t], t, k)
+        sums = narrow_sums(1, 0, range(4, 8))
         quantize_h(0, 0, CHUNK, smooth_on_vector(0, 0, CHUNK, "last"))
         for j0 in range(0, CHUNK, NARROW):
-            for t in range(4):
-                activate(1, sums[t], t, j0, j0 + NARROW)
-            quantize_h(1, j0, j0 + NARROW, smooth_on_vector(1, j0, j0 + NARROW, offset=(2 * PAGE, PAGE - 512)[j0 // NARROW]))
-        h = smooth_on_vector(0, CHUNK, HALF, offset=PAGE - 2048)
-        clear_late(1, 2 * PAGE)
-        clear_late(2, PAGE)
-        for t in range(4):
-            activate(1, sums[t], t, CHUNK, HALF)
+            activate_woven(1, sums[j0 // NARROW], j0)
+            quantize_h(1, j0, j0 + NARROW, smooth_on_vector(1, j0, j0 + NARROW))
+        h = smooth_on_vector(0, CHUNK, HALF, "h1_%d" % NARROW)
+        for x in range(2, 4):
+            activate_planar(1, sums[x], NARROW * x)
 
         c0, c1, c2, c3 = 0, CHUNK, 2 * CHUNK, 3 * CHUNK
         message(0, c0, c1, (0, 1))
         quantize_h(0, c1, c2, h)
-        clear_late(3, 0)
         scaled = scale_on_scalar(1, c1)
         message(1, c0, c1, (0, 1))
         weave_on_scalar(1, c1, scaled)
@@ -322,13 +342,13 @@ def tile_list_msg_tanh_res_bias_kernel(
         message(1, c1, c2, (0, 1))
         weave_on_scalar(1, c2, scaled)
         message(2, c1, c2, (0, 1))
-        sums = [first_sum(0, 1, t, (2, 3, 4, 5)[t]) for t in range(4)]
-        for t in range(4):
-            activate(0, sums[t], t, c2, c3)
+        sums = narrow_sums(0, c2, (2, 3)) + narrow_sums(0, c3, (4, 5))
+        for x in range(2):
+            activate_woven(0, sums[x], c2 + NARROW * x)
         quantize_h(0, c2, c3, smooth_on_vector(0, c2, c3))
         message(3, c1, c2, (0, 1))
-        for t in range(4):
-            activate(0, sums[t], t, c3, J)
+        for x in range(2, 4):
+            activate_planar(0, sums[x], c2 + NARROW * x)
         weave_on_scalar(1, c3, scale_on_scalar(1, c3))
         message(0, c2, c3, (1, 0))
         scaled = scale_on_scalar(0, c3)

@@ -46,6 +46,7 @@ def tile_list_msg_tanh_res_bias_kernel(
         wgo_sb = keep.tile([P, J], F32, name="wgo_sb")
         placed = {}
         biased = [keep.tile([P, J], F32, name="biased%d" % i, align_bytes=64) for i in range(4)]
+        weighted = [keep.tile([P, J], F32, name="weighted%d" % i, align_bytes=64) for i in range(4)]
         h_codes = [keep.tile([P, J], U32, name="hc%d" % g, align_bytes=64) for g in range(2)]
         h_sc = [keep.tile([P, J], U8, name="hsc%d" % g, align_bytes=64) for g in range(2)]
 
@@ -253,9 +254,8 @@ def tile_list_msg_tanh_res_bias_kernel(
                     stop=(number == len(passes) - 1),
                 )
             nc.scalar.activation(out=biased[i][:, j0:j1], in_=y[:], func=ACT.Identity, bias=b_sb[:, i : i + 1])
-            nc.vector.tensor_tensor(
-                out=placed[i][:].indirect(entries(1, j0, j1)), in0=biased[i][:, j0:j1], in1=wgo_sb[:, j0:j1], op=MULT
-            )
+            nc.gpsimd.tensor_tensor(out=weighted[i][:, j0:j1], in0=biased[i][:, j0:j1], in1=wgo_sb[:, j0:j1], op=MULT)
+            nc.vector.tensor_copy(placed[i][:].indirect(entries(1, j0, j1)), weighted[i][:, j0:j1])
             if j1 == J:
                 nc.sync.dma_start(out=out[n, :], in_=placed[i][:])
 

@@ -15,6 +15,7 @@ FP8X4 = mybir.dt.float8_e4m3fn_x4
 FP4X4 = mybir.dt.float4_e2m1fn_x4
 ACT = mybir.ActivationFunctionType
 MULT = mybir.AluOpType.mult
+ADD = mybir.AluOpType.add
 
 P = 128
 PASS = 512
@@ -45,10 +46,7 @@ def tile_list_msg_tanh_res_bias_kernel(
         wd8 = keep.tile([P, 2, N], I32, name="wd8", align_bytes=64)
         wgo_sb = keep.tile([P, J], F32, name="wgo_sb")
         placed = {}
-        biased = [keep.tile([P, J], F32, name="biased%d" % i, align_bytes=64) for i in range(4)]
-        weighted = [keep.tile([P, J], F32, name="weighted%d" % i, align_bytes=64) for i in range(4)]
-        h_codes = [keep.tile([P, J], U32, name="hc%d" % g, align_bytes=64) for g in range(2)]
-        h_sc = [keep.tile([P, J], U8, name="hsc%d" % g, align_bytes=64) for g in range(2)]
+        h_codes, h_sc = {}, {}
 
         weights = (ws, wt)
         steps = [(s, a) for a in range(2) for s in range(2)]
@@ -65,8 +63,8 @@ def tile_list_msg_tanh_res_bias_kernel(
 
         def round_w(n, m0, m1, engine, c0=0):
             if n not in rounded:
-                if n == 7:
-                    rounded[n] = keep.tile([P, 4 * PASS], BF16, name="last", align_bytes=64)
+                if n in (2, 7):
+                    rounded[n] = keep.tile([P, 4 * PASS], BF16, name="last" if n == 7 else "parted1", align_bytes=64)
                 else:
                     rounded[n] = ring.tile([P, 4 * PASS], BF16, name="rounded", align_bytes=64, bufs=4)
             dst = rounded[n][:].rearrange("p (t m j) -> p m j t", t=4, j=4)[:, m0:m1]
@@ -89,7 +87,7 @@ def tile_list_msg_tanh_res_bias_kernel(
 
         def clear(i, tag):
             placed[i] = keep.tile([P, T], F32, name=tag, align_bytes=64)
-            nc.vector.memset(placed[i][:].bitcast(I32), 0)
+            nc.gpsimd.memset(placed[i][:].bitcast(I32), 0)
 
         def gather_scales():
             for s in range(2):
@@ -102,11 +100,14 @@ def tile_list_msg_tanh_res_bias_kernel(
                     out=planes[a][32 * q : 32 * q + 4].bitcast(I32), in_=picked_sc[row : row + 4].bitcast(I32)
                 )
 
-        def gather_words(half, tag):
+        def gather_words(half):
             j0, j1 = HALF * half, HALF * (half + 1)
-            picked_w = keep.tile([P, 2, HALF], I32, name=tag, align_bytes=64)
+            picked_w = keep.tile([P, 2, HALF], I32, name="picked%d" % half, align_bytes=64)
             for s in range(2):
                 nc.vector.tensor_copy(picked_w[:, s, :].bitcast(U32), tab_w[:].bitcast(U32).indirect(entries(s, j0, j1)))
+            return picked_w
+
+        def part_words(half, picked_w):
             parted[half] = keep.tile([P, 2, 2, 2 * HALF], U8, name="parted%d" % half, align_bytes=64)
             for s in range(2):
                 nc.vector.tensor_copy(
@@ -125,121 +126,89 @@ def tile_list_msg_tanh_res_bias_kernel(
         def bank(number, width=HALF):
             return psum.tile([P, width], F32, name="bank%d" % number)
 
-        def first_pass(g, half, sums, t, k):
-            s, a = steps[k]
-            m = slice(P * t, P * (t + 1))
-            nc.tensor.matmul_mx(
-                out=sums[:],
-                lhsT=w_codes[4 * g + k][:, m].bitcast(FP8X4),
-                lhsT_scale=w_sc[4 * g + k][:, m],
-                rhs=parted[half][:, s, a, :].bitcast(FP4X4),
-                rhs_scale=planes[a][:, s, HALF * half : HALF * (half + 1)],
-                start=(k == 0),
-                stop=(k == 3),
-            )
-
-        def first_sum(g, half, t, number):
-            sums = bank(number)
-            for k in range(4):
-                first_pass(g, half, sums, t, k)
-            return sums
-
-        def narrow_passes(g, j0, sums, k):
+        def passes_of(g, j0, width, slices, sums, k, first, last):
             s, a = steps[k]
             c0 = j0 % HALF
-            for t in range(4):
+            for x, t in enumerate(slices):
                 m = slice(P * t, P * (t + 1))
                 nc.tensor.matmul_mx(
-                    out=sums[:, NARROW * t : NARROW * (t + 1)],
+                    out=sums[:, width * x : width * (x + 1)],
                     lhsT=w_codes[4 * g + k][:, m].bitcast(FP8X4),
                     lhsT_scale=w_sc[4 * g + k][:, m],
-                    rhs=parted[j0 // HALF][:, s, a, 2 * c0 : 2 * (c0 + NARROW)].bitcast(FP4X4),
-                    rhs_scale=planes[a][:, s, j0 : j0 + NARROW],
-                    start=(k == 0 and t == 0),
-                    stop=(k == 3 and t == 3),
+                    rhs=parted[j0 // HALF][:, s, a, 2 * c0 : 2 * (c0 + width)].bitcast(FP4X4),
+                    rhs_scale=planes[a][:, s, j0 : j0 + width],
+                    start=(first and x == 0),
+                    stop=(last and x == len(slices) - 1),
                 )
 
-        def narrow_sums(g, j0, numbers):
+        def narrow_sums(g, c, numbers):
             sums = [bank(number) for number in numbers]
-            for k in range(4):
-                for x in range(len(numbers)):
-                    narrow_passes(g, j0 + NARROW * x, sums[x], k)
-            return sums
+            return [(g, CHUNK * c + NARROW * x, NARROW, range(4), sums[x]) for x in range(2)]
 
-        def act_tile(g, half):
-            if (g, half) not in act:
-                act[g, half] = keep.tile([P, 4 * HALF], F32, name=("raw7_0", "raw0_0", "raw1_0", "raw3_0")[len(act)], align_bytes=64)
-            return act[g, half]
+        def paired_sums(g, c, numbers):
+            sums = [bank(number) for number in numbers]
+            return [(g, CHUNK * c, CHUNK, range(2 * x, 2 * x + 2), sums[x]) for x in range(2)]
 
-        def woven(g, j0, j1):
-            return act_tile(g, j0 // HALF)[:, 4 * (j0 % HALF) : 4 * (j0 % HALF + j1 - j0)].rearrange("p (j t) -> p j t", t=4)
+        def add_up(groups, order=(0, 1, 2, 3)):
+            for k in order:
+                for group in groups:
+                    passes_of(*group, k, k == order[0], k == order[-1])
+            return [group[-1] for group in groups]
 
-        def planar(g, j0):
-            return act_tile(g, j0 // HALF)[:, 4 * (j0 % HALF) : 4 * (j0 % HALF + CHUNK)].rearrange("p (t j) -> p t j", t=4)
+        def bank_by_bank(groups, order=(0, 1, 2, 3)):
+            return [add_up([group], order)[0] for group in groups]
 
-        def activate_woven(g, sums, j0):
-            nc.scalar.activation(out=woven(g, j0, j0 + NARROW), in_=sums[:].rearrange("p (t j) -> p j t", t=4), func=ACT.Tanh)
+        def act_tiles(units, tag):
+            both = keep.tile([P, len(units), 4 * CHUNK], F32, name=tag, align_bytes=64)
+            for x, unit in enumerate(units):
+                act[unit] = both[:, x, :]
 
-        def activate_planar(g, sums, j0):
-            c0 = j0 % CHUNK
-            nc.scalar.activation(
-                out=planar(g, j0 - c0)[:, :, c0 : c0 + NARROW], in_=sums[:].rearrange("p (t j) -> p t j", t=4), func=ACT.Tanh
-            )
+        def woven(g, c, x0, x1):
+            return act[g, c][:, 4 * NARROW * x0 : 4 * NARROW * x1].rearrange("p (j t) -> p j t", t=4)
 
-        def activate(g, sums, t, j0, j1):
-            out_view = act_tile(g, j0 // HALF)[:].rearrange("p (c t j) -> p c t j", c=2, t=4)[:, :, t, :]
-            nc.scalar.activation(out=out_view, in_=sums[:].rearrange("p (c j) -> p c j", c=2), func=ACT.Tanh)
+        def tanh_woven(g, c, x, sums):
+            nc.scalar.activation(out=woven(g, c, x, x + 1), in_=sums[:].rearrange("p (t j) -> p j t", t=4), func=ACT.Tanh)
 
-        def quantize_h(g, j0, j1, h):
-            nc.vector.quantize_mx(
-                out=h_codes[g][:, j0:j1].bitcast(FP8X4), scales=h_sc[g][:, j0:j1], in_=h[:].rearrange("p w t -> p (w t)")
-            )
+        def tanh_planar(g, c, x, sums):
+            nc.scalar.activation(out=act[g, c][:, HALF * x : HALF * (x + 1)], in_=sums[:], func=ACT.Tanh)
+
+        def smooth(engine, g, c, x0, x1, out_view):
+            factors = sm_sb[:, g, :].unsqueeze(1).to_broadcast([P, NARROW * (x1 - x0), 4])
+            engine.tensor_tensor(out=out_view, in0=woven(g, c, x0, x1), in1=factors, op=MULT)
 
         def by_fours(view):
             return view.rearrange("p t (c i) -> p c t i", i=4)
 
-        def smooth_on_vector(g, j0, j1, tag=None):
-            w = j1 - j0
-            h = keep.tile([P, w, 4], BF16, name=tag or "h%d_%d" % (g, j0), align_bytes=64)
-            nc.vector.tensor_tensor(
-                out=h[:],
-                in0=woven(g, j0, j1),
-                in1=sm_sb[:, g, :].unsqueeze(1).to_broadcast([P, w, 4]),
-                op=MULT,
-            )
-            return h
-
-        def scale_on_scalar(g, j0):
-            scaled = ring.tile([P, 4, CHUNK], BF16, name="scaled", bufs=2)
+        def scale_on_scalar(g, c):
+            scaled = keep.tile([P, 4, CHUNK], BF16, name="relay%d" % (c % 2), align_bytes=64)
             for t in range(4):
                 nc.scalar.activation(
                     out=scaled[:, t, :],
-                    in_=planar(g, j0)[:, t, :],
+                    in_=act[g, c][:, CHUNK * t : CHUNK * (t + 1)],
                     func=ACT.Copy,
                     scale=sm_sb[:, g, t : t + 1],
                 )
             return scaled
 
-        def weave_on_scalar(g, j0, scaled):
-            h = keep.tile([P, CHUNK, 4], BF16, name="h%d_%d" % (g, j0), align_bytes=64)
-            nc.scalar.copy(out=h[:].rearrange("p (c i) t -> p c t i", i=4), in_=by_fours(scaled[:]))
-            quantize_h(g, j0, j0 + CHUNK, h)
+        def weave_on_scalar(scaled, out_view):
+            nc.scalar.copy(out=out_view.rearrange("p (c i) t -> p c t i", i=4), in_=by_fours(scaled[:]))
 
-        sent = []
+        def h_tile():
+            return keep.tile([P, 8 * CHUNK], BF16, name="h", align_bytes=64)
 
-        def message(i, j0, j1, groups):
-            w = j1 - j0
-            y = bank(len(sent) if len(sent) < 4 else len(sent) % 2, w)
-            sent.append((i, j0))
+        def words(h, j0, j1):
+            return h[:, 4 * j0 : 4 * j1].rearrange("p (j t) -> p j t", t=4)
+
+        def code_tiles(c, tag):
+            h_codes[c] = keep.tile([P, 2 * CHUNK], U32, name=tag, align_bytes=64)
+            h_sc[c] = keep.tile([P, 2 * CHUNK], U8, name="hsc%d" % c, align_bytes=64)
+
+        def quantize_h(c, c0, c1, values):
+            nc.vector.quantize_mx(out=h_codes[c][:, c0:c1].bitcast(FP8X4), scales=h_sc[c][:, c0:c1], in_=values)
+
+        def second_sum(y, i, c, pieces):
             n = slice(P * i, P * (i + 1))
-            passes = []
-            for g in groups:
-                narrow = [(c, c + NARROW) for c in range(0, w, NARROW)] if w < HALF else [(0, w)]
-                if j0 == 0 and g == groups[-1]:
-                    passes += [(g, tier, cols) for cols in narrow for tier in (1, 0)]
-                else:
-                    passes += [(g, 1, (0, w))] + [(g, 0, cols) for cols in narrow]
-            for number, (g, tier, (c0, c1)) in enumerate(passes):
+            for number, (g, tier, c0, c1) in enumerate(pieces):
                 if tier == 0:
                     lhs = wd4[:, g, P // 2 * i : P // 2 * (i + 1)].bitcast(FP4X4)
                 else:
@@ -248,113 +217,139 @@ def tile_list_msg_tanh_res_bias_kernel(
                     out=y[:, c0:c1],
                     lhsT=lhs,
                     lhsT_scale=wd_sc[tier][:, g, n],
-                    rhs=h_codes[g][:, j0 + c0 : j0 + c1].bitcast(FP8X4),
-                    rhs_scale=h_sc[g][:, j0 + c0 : j0 + c1],
+                    rhs=h_codes[c][:, CHUNK * g + c0 : CHUNK * g + c1].bitcast(FP8X4),
+                    rhs_scale=h_sc[c][:, CHUNK * g + c0 : CHUNK * g + c1],
                     start=(number == 0),
-                    stop=(number == len(passes) - 1),
+                    stop=(number == len(pieces) - 1),
                 )
-            nc.scalar.activation(out=biased[i][:, j0:j1], in_=y[:], func=ACT.Identity, bias=b_sb[:, i : i + 1])
-            nc.gpsimd.tensor_tensor(out=weighted[i][:, j0:j1], in0=biased[i][:, j0:j1], in1=wgo_sb[:, j0:j1], op=MULT)
-            nc.vector.tensor_copy(placed[i][:].indirect(entries(1, j0, j1)), weighted[i][:, j0:j1])
-            if j1 == J:
-                nc.sync.dma_start(out=out[n, :], in_=placed[i][:])
 
-        nc.vector.memset(tab_sc[0:SCALE_ROWS_AT].bitcast(I32), 0)
+        whole = [(g, tier, 0, CHUNK) for g in range(2) for tier in (1, 0)]
+        by_halves = whole[:2] + [(1, tier, c0, c0 + NARROW) for c0 in (0, NARROW) for tier in (1, 0)]
+        sent = []
+
+
+        def message(i, chunks, biased=None):
+            j0, j1 = CHUNK * chunks[0], CHUNK * (chunks[-1] + 1)
+            y = bank(2 + len(sent) % 4, j1 - j0)
+            for x, c in enumerate(chunks):
+                second_sum(y[:, CHUNK * x : CHUNK * (x + 1)], i, c, by_halves if not sent else whole)
+            weighted = keep.tile([P, j1 - j0], F32, name="weighted%d_%d" % (chunks[0], i), align_bytes=64)
+            if len(sent) in (0, 1, 11):
+                nc.vector.scalar_tensor_tensor(
+                    out=weighted[:], in0=y[:], scalar=b_sb[:, i : i + 1], in1=wgo_sb[:, j0:j1], op0=ADD, op1=MULT
+                )
+            else:
+                if biased is None:
+                    biased = keep.tile([P, j1 - j0], F32, name="biased%d" % (len(sent) % 3), align_bytes=64)[:]
+                nc.scalar.activation(out=biased, in_=y[:], func=ACT.Identity, bias=b_sb[:, i : i + 1])
+                nc.gpsimd.tensor_tensor(out=weighted[:], in0=biased, in1=wgo_sb[:, j0:j1], op=MULT)
+            sent.append((i, j0))
+            nc.vector.tensor_copy(placed[i][:].indirect(entries(1, j0, j1)), weighted[:])
+            if j1 == J:
+                nc.sync.dma_start(out=out[P * i : P * (i + 1), :], in_=placed[i][:])
+
+        nc.gpsimd.memset(tab_sc[0:SCALE_ROWS_AT].bitcast(I32), 0)
+        for plane in wd_sc[::-1] + planes:
+            nc.gpsimd.memset(plane[:].bitcast(I32), 0)
+        for i in range(4):
+            clear(i, "page%d" % i)
         nc.sync.dma_start(lists[0][:], offs)
         nc.sync.dma_start(lists[1][:], offs2)
         nc.sync.dma_start(
             out=tab_sc[SCALE_ROWS_AT:P].bitcast(I32), in_=tab_scales.rearrange("a q t -> (a q) t").bitcast(I32)
         )
         load_w(0)
-        warm = keep.tile([P, 1], F32, name="warm")
-        nc.vector.memset(warm[:], 0.0)
-        warmed = keep.tile([P, 1], F32, name="warmed")
-        nc.scalar.activation(out=warmed[:], in_=warm[:], func=ACT.Tanh)
-        for plane in planes + wd_sc:
-            nc.vector.memset(plane[:].bitcast(I32), 0)
-
-        gather_scales()
-        round_w(0, 0, P, "scalar")
-        quantize_w(0)
-        nc.sync.dma_start(out=sm_sb[:], in_=sm.rearrange("(g p t) -> p g t", g=2, t=4))
-        load_w(1)
-        load_w(2)
         nc.sync.dma_start(out=tab_w[:], in_=tab_words[0].rearrange("p t b -> p (t b)").bitcast(I32))
+        gather_scales()
+        picked = [gather_words(half) for half in range(2)]
+        nc.sync.dma_start(out=sm_sb[:], in_=sm.rearrange("(g p t) -> p g t", g=2, t=4))
+        with nc.allow_non_contiguous_dma(reason="one bias value for each partition"):
+            nc.sync.dma_start(out=b_sb[:], in_=b.rearrange("(i p) -> p i", p=P))
+        load_w(1)
+        load_wd_scales(1)
+        load_w(2)
         move_scales(0)
         load_w(3)
-        load_w(4)
         move_scales(1)
+        load_w(4)
+        load_wd_scales(0)
         load_w(5)
         load_w(6)
-        load_wd_scales(1)
         load_w(7, 0, PASS // 2)
         load_w(7, PASS // 2, PASS)
         nc.sync.dma_start(out=wd8[:], in_=wd8_words.rearrange("a p n i -> p a (n i)").bitcast(I32))
         nc.sync.dma_start(out=wd4[:], in_=wd4_words.rearrange("a p n -> p a n").bitcast(I32))
-        load_wd_scales(0)
-        with nc.allow_non_contiguous_dma(reason="one bias value for each partition"):
-            nc.sync.dma_start(out=b_sb[:], in_=b.rearrange("(i p) -> p i", p=P))
         nc.sync.dma_start(out=wgo_sb[:], in_=wgo)
 
-        for n in range(1, 4):
+        round_w(0, 0, P, "scalar")
+        quantize_w(0, tag="tab_w")
+        part_words(0, picked[0])
+        for n in range(1, 3):
             round_w(n, 0, P, "scalar")
             quantize_w(n)
-        gather_words(0, "picked0")
-        gather_words(1, "raw2_0")
-        for i in range(4):
-            clear(i, "page%d" % i)
-        sums = narrow_sums(0, 0, range(4))
-        round_w(4, 0, P, "scalar")
+        part_words(1, picked[1])
+        round_w(3, 0, P, "scalar")
+        quantize_w(3)
+        early = [sums for c in range(2) for sums in add_up(narrow_sums(0, c, (2 * c, 2 * c + 1)))]
+        third = add_up(narrow_sums(0, 2, (6, 7)))
+        round_w(4, 0, P, "vector")
         quantize_w(4)
         round_w(5, 0, P, "scalar")
-        round_w(6, 0, 96, "vector")
-        round_w(6, 96, P, "scalar")
+        act_tiles([(0, 0)], "raw5_0")
+        for x in range(2):
+            tanh_woven(0, 0, x, early[x])
+        round_w(6, 0, P, "vector")
         quantize_w(5, tag="raw6_0")
         quantize_w(6)
         round_w(7, 0, P // 2, "scalar")
-        for x in range(4):
-            activate_woven(0, sums[x], NARROW * x)
+        act_tiles([(0, 1)], "raw7_0")
+        for x in range(2):
+            tanh_woven(0, 1, x, early[2 + x])
         round_w(7, P // 2, P, "vector", PASS // 2)
         quantize_w(7, 4)
-        sums = narrow_sums(1, 0, range(4, 8))
-        quantize_h(0, 0, CHUNK, smooth_on_vector(0, 0, CHUNK, "last"))
-        for j0 in range(0, CHUNK, NARROW):
-            activate_woven(1, sums[j0 // NARROW], j0)
-            quantize_h(1, j0, j0 + NARROW, smooth_on_vector(1, j0, j0 + NARROW))
-        h = smooth_on_vector(0, CHUNK, HALF, "h1_%d" % NARROW)
-        for x in range(2, 4):
-            activate_planar(1, sums[x], NARROW * x)
+        sums = add_up(narrow_sums(1, 0, (4, 5))) + bank_by_bank(paired_sums(1, 1, (0, 1)), (3, 0, 1, 2))
 
-        c0, c1, c2, c3 = 0, CHUNK, 2 * CHUNK, 3 * CHUNK
-        message(0, c0, c1, (0, 1))
-        quantize_h(0, c1, c2, h)
-        scaled = scale_on_scalar(1, c1)
-        message(1, c0, c1, (0, 1))
-        weave_on_scalar(1, c1, scaled)
-        message(2, c0, c1, (0, 1))
-        for t in range(2):
-            activate(1, first_sum(1, 1, t, 4 + t), t, HALF, J)
-        message(3, c0, c1, (0, 1))
-        for t in range(2, 4):
-            activate(1, first_sum(1, 1, t, 4 + t), t, HALF, J)
-        message(0, c1, c2, (0, 1))
-        scaled = scale_on_scalar(1, c2)
-        message(1, c1, c2, (0, 1))
-        weave_on_scalar(1, c2, scaled)
-        message(2, c1, c2, (0, 1))
-        sums = narrow_sums(0, c2, (2, 3)) + narrow_sums(0, c3, (4, 5))
+        code_tiles(0, "hc0")
+        first = keep.tile([P, CHUNK, 4], BF16, name="last", align_bytes=64)
+        smooth(nc.vector, 0, 0, 0, 2, first[:])
+        quantize_h(0, 0, CHUNK, first[:].rearrange("p j t -> p (j t)"))
+        act_tiles([(1, 0)], "raw1_0")
+        h = h_tile()
         for x in range(2):
-            activate_woven(0, sums[x], c2 + NARROW * x)
-        quantize_h(0, c2, c3, smooth_on_vector(0, c2, c3))
-        message(3, c1, c2, (0, 1))
-        for x in range(2, 4):
-            activate_planar(0, sums[x], c2 + NARROW * x)
-        weave_on_scalar(1, c3, scale_on_scalar(1, c3))
-        message(0, c2, c3, (1, 0))
-        scaled = scale_on_scalar(0, c3)
-        message(1, c2, c3, (1, 0))
-        weave_on_scalar(0, c3, scaled)
-        message(2, c2, c3, (1, 0))
+            tanh_woven(1, 0, x, sums[x])
+            smooth(nc.vector, 1, 0, x, x + 1, words(h, NARROW * x, NARROW * (x + 1)))
+            quantize_h(0, CHUNK + NARROW * x, CHUNK + NARROW * (x + 1), h[:, HALF * x : HALF * (x + 1)])
+        act_tiles([(1, 1)], "raw2_0")
+        for x in range(2):
+            tanh_planar(1, 1, x, sums[2 + x])
+
+        for c in range(1, 4):
+            h = h_tile()
+            smooth(nc.gpsimd, 0, c, 0, 1, words(h, 0, NARROW))
+            message(0, [c - 1], h[:, HALF : 2 * HALF].bitcast(F32))
+            message(1, [c - 1])
+            smooth(nc.gpsimd, 0, c, 1, 2, words(h, NARROW, CHUNK))
+            weave_on_scalar(scale_on_scalar(1, c), words(h, CHUNK, 2 * CHUNK))
+            code_tiles(c, "weighted%d_1" % (c - 1))
+            quantize_h(c, 0, 2 * CHUNK, h[:])
+            pair = keep.tile([P, 2, CHUNK], F32, name="relay%d" % (c % 2), align_bytes=64)
+            for i in range(2, 4 if c < 3 else 3):
+                message(i, [c - 1], pair[:, i - 2, :])
+            if c == 1:
+                narrow = third
+                act_tiles([(0, 2)], "relay1")
+                act_tiles([(1, 2)], "raw5_0")
+            if c == 2:
+                narrow = bank_by_bank(narrow_sums(0, 3, (6, 7)))
+                act_tiles([(0, 3)], "relay0")
+                act_tiles([(1, 3)], "raw5_0")
+            if c < 3:
+                paired = bank_by_bank(paired_sums(1, c + 1, (0, 1)))
+            if c < 3:
+                for x in range(2):
+                    tanh_woven(0, c + 1, x, narrow[x])
+                for x in range(2):
+                    tanh_planar(1, c + 1, x, paired[x])
         for i in range(3):
-            message(i, c3, J, (1, 0))
-        message(3, c2, J, (1, 0))
+            message(i, [3])
+        message(3, [2, 3])

@@ -23,6 +23,7 @@ HALF = 512
 CHUNK = 256
 NARROW = 128
 SCALE_ROWS_AT = 96
+KB = 1024
 
 
 def tile_list_msg_tanh_res_bias_kernel(
@@ -32,6 +33,8 @@ def tile_list_msg_tanh_res_bias_kernel(
     with ExitStack() as ctx:
         keep = ctx.enter_context(tc.tile_pool(name="keep", bufs=1))
         ring = ctx.enter_context(tc.tile_pool(name="ring", bufs=3))
+        relay = ctx.enter_context(tc.tile_pool(name="relay", bufs=1))
+        reuse = ctx.enter_context(tc.tile_pool(name="reuse", bufs=1))
         psum = ctx.enter_context(tc.psum_pool(name="psum", bufs=1))
 
         lists = [keep.tile([P, J // 16], U16, name="list%d" % s) for s in range(2)]
@@ -40,8 +43,7 @@ def tile_list_msg_tanh_res_bias_kernel(
         sm_sb = keep.tile([P, 2, 4], F32, name="sm_sb")
         b_sb = keep.tile([P, 4], F32, name="b_sb")
         picked_sc = keep.tile([P, 2, J], U8, name="picked_sc", align_bytes=64)
-        planes = [keep.tile([P, 2, J], U8, name="plane%d" % a, align_bytes=64) for a in range(2)]
-        wd_sc = [keep.tile([P, 2, N], U8, name="wd_sc%d" % tier, align_bytes=64) for tier in range(2)]
+        planes, wd_sc = {}, {}
         wd4 = keep.tile([P, 2, N // 2], I32, name="wd4", align_bytes=64)
         wd8 = keep.tile([P, 2, N], I32, name="wd8", align_bytes=64)
         wgo_sb = keep.tile([P, J], F32, name="wgo_sb")
@@ -63,10 +65,13 @@ def tile_list_msg_tanh_res_bias_kernel(
 
         def round_w(n, m0, m1, engine, c0=0):
             if n not in rounded:
-                if n in (2, 7):
-                    rounded[n] = keep.tile([P, 4 * PASS], BF16, name="last" if n == 7 else "parted1", align_bytes=64)
+                if n == 1:
+                    rounded[n] = reuse.tile([P, 4 * PASS], BF16, name="rounded1", align_bytes=64, offset=6 * KB)
+                elif n in (3, 7):
+                    tag = {3: "page3", 7: "last"}[n]
+                    rounded[n] = keep.tile([P, 4 * PASS], BF16, name=tag, align_bytes=64)
                 else:
-                    rounded[n] = ring.tile([P, 4 * PASS], BF16, name="rounded", align_bytes=64, bufs=4)
+                    rounded[n] = ring.tile([P, 4 * PASS], BF16, name="rounded", align_bytes=64, bufs=3)
             dst = rounded[n][:].rearrange("p (t m j) -> p m j t", t=4, j=4)[:, m0:m1]
             src = raw[n, c0][:].rearrange("p j (m t) -> p m j t", t=4)[:, m0 - c0 // 4 : m1 - c0 // 4]
             if engine == "vector":
@@ -78,22 +83,48 @@ def tile_list_msg_tanh_res_bias_kernel(
             w_codes[n] = keep.tile([P, PASS], U32, name=tag or "wc%d" % n, align_bytes=64)
             w_sc[n] = keep.tile([P, PASS], U8, name="wsc%d" % n, align_bytes=64)
             step = PASS // pieces
-            for c in range(0, PASS, step):
+            starts = range(0, PASS, step)
+            for c in list(starts[0::2]) + list(starts[1::2]):
                 nc.vector.quantize_mx(
                     out=w_codes[n][:, c : c + step].bitcast(FP8X4),
                     scales=w_sc[n][:, c : c + step],
                     in_=rounded[n][:, 4 * c : 4 * (c + step)],
                 )
 
+        def last_weight_tile():
+            halves = [keep.tile([P, 4, P // 2, 4], BF16, name="last%d" % x, align_bytes=64) for x in range(2)]
+            for x, copy in enumerate((nc.scalar.copy, nc.vector.tensor_copy)):
+                copy(
+                    out=halves[x][:].rearrange("p t m j -> p m j t"),
+                    in_=raw[7, PASS // 2 * x][:].rearrange("p j (m t) -> p m j t", t=4),
+                )
+            w_codes[7] = keep.tile([P, PASS], U32, name="wc7", align_bytes=64)
+            w_sc[7] = keep.tile([P, PASS], U8, name="wsc7", align_bytes=64)
+            for x in range(2):
+                for t in range(4):
+                    m = slice(P * t + P // 2 * x, P * t + P // 2 * (x + 1))
+                    nc.vector.quantize_mx(
+                        out=w_codes[7][:, m].bitcast(FP8X4),
+                        scales=w_sc[7][:, m],
+                        in_=halves[x][:, t].rearrange("p m j -> p (m j)"),
+                    )
+
         def clear(i, tag):
-            placed[i] = keep.tile([P, T], F32, name=tag, align_bytes=64)
-            nc.gpsimd.memset(placed[i][:].bitcast(I32), 0)
+            if i == 2:
+                placed[i] = reuse.tile([P, T], F32, name=tag, align_bytes=64, offset=8 * KB)
+            else:
+                placed[i] = keep.tile([P, T], F32, name=tag, align_bytes=64)
+            nc.vector.memset(placed[i][:].bitcast(I32), 0)
 
         def gather_scales():
             for s in range(2):
                 nc.vector.tensor_copy(picked_sc[:, s, :], tab_sc[:].indirect(lists[s][:]))
 
         def move_scales(a):
+            if a == 0:
+                planes[a] = keep.tile([P, 2, J], U8, name="tab_sc", align_bytes=64)
+            else:
+                planes[a] = reuse.tile([P, 2, J], U8, name="plane1", align_bytes=64, offset=0)
             for q in range(4):
                 row = SCALE_ROWS_AT + 16 * a + 4 * q
                 nc.sync.dma_start(
@@ -102,13 +133,19 @@ def tile_list_msg_tanh_res_bias_kernel(
 
         def gather_words(half):
             j0, j1 = HALF * half, HALF * (half + 1)
-            picked_w = keep.tile([P, 2, HALF], I32, name="picked%d" % half, align_bytes=64)
+            if half == 0:
+                picked_w = reuse.tile([P, 2, HALF], I32, name="picked0", align_bytes=64, offset=0)
+            else:
+                picked_w = keep.tile([P, 2, HALF], I32, name="picked1", align_bytes=64)
             for s in range(2):
                 nc.vector.tensor_copy(picked_w[:, s, :].bitcast(U32), tab_w[:].bitcast(U32).indirect(entries(s, j0, j1)))
             return picked_w
 
         def part_words(half, picked_w):
-            parted[half] = keep.tile([P, 2, 2, 2 * HALF], U8, name="parted%d" % half, align_bytes=64)
+            if half == 0:
+                parted[half] = keep.tile([P, 2, 2, 2 * HALF], U8, name="parted0", align_bytes=64)
+            else:
+                parted[half] = reuse.tile([P, 2, 2, 2 * HALF], U8, name="parted1", align_bytes=64, offset=4 * KB)
             for s in range(2):
                 nc.vector.tensor_copy(
                     out=parted[half][:, s, :, :].bitcast(U16),
@@ -117,6 +154,7 @@ def tile_list_msg_tanh_res_bias_kernel(
 
         def load_wd_scales(tier):
             scales = (wd4_scales, wd8_scales)[tier]
+            wd_sc[tier] = reuse.tile([P, 2, N], U8, name="wd_sc%d" % tier, align_bytes=64, offset=(2 + tier) * KB)
             for q in range(4):
                 nc.sync.dma_start(
                     out=wd_sc[tier][32 * q : 32 * q + 4].bitcast(I32),
@@ -158,6 +196,9 @@ def tile_list_msg_tanh_res_bias_kernel(
         def bank_by_bank(groups, order=(0, 1, 2, 3)):
             return [add_up([group], order)[0] for group in groups]
 
+        def planar_tile(c):
+            act[1, c] = relay.tile([P, 4 * CHUNK], F32, name="planar%d" % c, align_bytes=64, offset=(5 * c + 1) * KB)[:]
+
         def act_tiles(units, tag):
             both = keep.tile([P, len(units), 4 * CHUNK], F32, name=tag, align_bytes=64)
             for x, unit in enumerate(units):
@@ -180,7 +221,7 @@ def tile_list_msg_tanh_res_bias_kernel(
             return view.rearrange("p t (c i) -> p c t i", i=4)
 
         def scale_on_scalar(g, c):
-            scaled = keep.tile([P, 4, CHUNK], BF16, name="relay%d" % (c % 2), align_bytes=64)
+            scaled = keep.tile([P, 4, CHUNK], BF16, name="scaled", align_bytes=64)
             for t in range(4):
                 nc.scalar.activation(
                     out=scaled[:, t, :],
@@ -199,8 +240,8 @@ def tile_list_msg_tanh_res_bias_kernel(
         def words(h, j0, j1):
             return h[:, 4 * j0 : 4 * j1].rearrange("p (j t) -> p j t", t=4)
 
-        def code_tiles(c, tag):
-            h_codes[c] = keep.tile([P, 2 * CHUNK], U32, name=tag, align_bytes=64)
+        def code_tiles(c):
+            h_codes[c] = relay.tile([P, 2 * CHUNK], U32, name="hc%d" % c, align_bytes=64, offset=(5 * c if c < 3 else 20) * KB)
             h_sc[c] = keep.tile([P, 2 * CHUNK], U8, name="hsc%d" % c, align_bytes=64)
 
         def quantize_h(c, c0, c1, values):
@@ -229,12 +270,15 @@ def tile_list_msg_tanh_res_bias_kernel(
 
 
         def message(i, chunks, biased=None):
+            scatter(i, chunks, weigh(i, chunks, biased))
+
+        def weigh(i, chunks, biased=None):
             j0, j1 = CHUNK * chunks[0], CHUNK * (chunks[-1] + 1)
             y = bank(2 + len(sent) % 4, j1 - j0)
             for x, c in enumerate(chunks):
                 second_sum(y[:, CHUNK * x : CHUNK * (x + 1)], i, c, by_halves if not sent else whole)
             weighted = keep.tile([P, j1 - j0], F32, name="weighted%d_%d" % (chunks[0], i), align_bytes=64)
-            if len(sent) in (0, 1, 11):
+            if len(sent) < 2:
                 nc.vector.scalar_tensor_tensor(
                     out=weighted[:], in0=y[:], scalar=b_sb[:, i : i + 1], in1=wgo_sb[:, j0:j1], op0=ADD, op1=MULT
                 )
@@ -244,14 +288,16 @@ def tile_list_msg_tanh_res_bias_kernel(
                 nc.scalar.activation(out=biased, in_=y[:], func=ACT.Identity, bias=b_sb[:, i : i + 1])
                 nc.gpsimd.tensor_tensor(out=weighted[:], in0=biased, in1=wgo_sb[:, j0:j1], op=MULT)
             sent.append((i, j0))
+            return weighted
+
+        def scatter(i, chunks, weighted):
+            j0, j1 = CHUNK * chunks[0], CHUNK * (chunks[-1] + 1)
             nc.vector.tensor_copy(placed[i][:].indirect(entries(1, j0, j1)), weighted[:])
             if j1 == J:
                 nc.sync.dma_start(out=out[P * i : P * (i + 1), :], in_=placed[i][:])
 
-        nc.gpsimd.memset(tab_sc[0:SCALE_ROWS_AT].bitcast(I32), 0)
-        for plane in wd_sc[::-1] + planes:
-            nc.gpsimd.memset(plane[:].bitcast(I32), 0)
-        for i in range(4):
+        nc.vector.memset(tab_sc[0:SCALE_ROWS_AT].bitcast(I32), 0)
+        for i in range(2):
             clear(i, "page%d" % i)
         nc.sync.dma_start(lists[0][:], offs)
         nc.sync.dma_start(lists[1][:], offs2)
@@ -261,56 +307,54 @@ def tile_list_msg_tanh_res_bias_kernel(
         load_w(0)
         nc.sync.dma_start(out=tab_w[:], in_=tab_words[0].rearrange("p t b -> p (t b)").bitcast(I32))
         gather_scales()
-        picked = [gather_words(half) for half in range(2)]
+        picked = gather_words(0)
         nc.sync.dma_start(out=sm_sb[:], in_=sm.rearrange("(g p t) -> p g t", g=2, t=4))
         with nc.allow_non_contiguous_dma(reason="one bias value for each partition"):
             nc.sync.dma_start(out=b_sb[:], in_=b.rearrange("(i p) -> p i", p=P))
         load_w(1)
-        load_wd_scales(1)
         load_w(2)
         move_scales(0)
         load_w(3)
-        move_scales(1)
         load_w(4)
-        load_wd_scales(0)
+        round_w(0, 0, P, "scalar")
+        quantize_w(0)
+        part_words(0, picked)
+        move_scales(1)
         load_w(5)
+        load_wd_scales(1)
         load_w(6)
+        load_wd_scales(0)
         load_w(7, 0, PASS // 2)
         load_w(7, PASS // 2, PASS)
         nc.sync.dma_start(out=wd8[:], in_=wd8_words.rearrange("a p n i -> p a (n i)").bitcast(I32))
         nc.sync.dma_start(out=wd4[:], in_=wd4_words.rearrange("a p n -> p a n").bitcast(I32))
         nc.sync.dma_start(out=wgo_sb[:], in_=wgo)
 
-        round_w(0, 0, P, "scalar")
-        quantize_w(0, tag="tab_w")
-        part_words(0, picked[0])
-        for n in range(1, 3):
-            round_w(n, 0, P, "scalar")
-            quantize_w(n)
-        part_words(1, picked[1])
+        round_w(1, 0, P, "scalar")
+        quantize_w(1)
+        picked = gather_words(1)
+        round_w(2, 0, P, "scalar")
+        quantize_w(2)
+        part_words(1, picked)
+        clear(2, "page2")
         round_w(3, 0, P, "scalar")
         quantize_w(3)
+        clear(3, "page3")
         early = [sums for c in range(2) for sums in add_up(narrow_sums(0, c, (2 * c, 2 * c + 1)))]
-        third = add_up(narrow_sums(0, 2, (6, 7)))
-        round_w(4, 0, P, "vector")
+        round_w(4, 0, P, "scalar")
+        act_tiles([(0, 0), (0, 1)], "raw4_0")
+        for x in range(4):
+            tanh_woven(0, x // 2, x % 2, early[x])
         quantize_w(4)
-        round_w(5, 0, P, "scalar")
-        act_tiles([(0, 0)], "raw5_0")
-        for x in range(2):
-            tanh_woven(0, 0, x, early[x])
+        round_w(5, 0, P, "vector")
+        quantize_w(5)
         round_w(6, 0, P, "vector")
-        quantize_w(5, tag="raw6_0")
         quantize_w(6)
-        round_w(7, 0, P // 2, "scalar")
-        act_tiles([(0, 1)], "raw7_0")
-        for x in range(2):
-            tanh_woven(0, 1, x, early[2 + x])
-        round_w(7, P // 2, P, "vector", PASS // 2)
-        quantize_w(7, 4)
-        sums = add_up(narrow_sums(1, 0, (4, 5))) + bank_by_bank(paired_sums(1, 1, (0, 1)), (3, 0, 1, 2))
+        last_weight_tile()
+        sums = add_up(narrow_sums(1, 0, (4, 5))) + bank_by_bank(paired_sums(1, 1, (6, 7)), (1, 0, 3, 2))
 
-        code_tiles(0, "hc0")
-        first = keep.tile([P, CHUNK, 4], BF16, name="last", align_bytes=64)
+        code_tiles(0)
+        first = keep.tile([P, CHUNK, 4], BF16, name="last0", align_bytes=64)
         smooth(nc.vector, 0, 0, 0, 2, first[:])
         quantize_h(0, 0, CHUNK, first[:].rearrange("p j t -> p (j t)"))
         act_tiles([(1, 0)], "raw1_0")
@@ -319,7 +363,7 @@ def tile_list_msg_tanh_res_bias_kernel(
             tanh_woven(1, 0, x, sums[x])
             smooth(nc.vector, 1, 0, x, x + 1, words(h, NARROW * x, NARROW * (x + 1)))
             quantize_h(0, CHUNK + NARROW * x, CHUNK + NARROW * (x + 1), h[:, HALF * x : HALF * (x + 1)])
-        act_tiles([(1, 1)], "raw2_0")
+        planar_tile(1)
         for x in range(2):
             tanh_planar(1, 1, x, sums[2 + x])
 
@@ -327,25 +371,25 @@ def tile_list_msg_tanh_res_bias_kernel(
             h = h_tile()
             smooth(nc.gpsimd, 0, c, 0, 1, words(h, 0, NARROW))
             message(0, [c - 1], h[:, HALF : 2 * HALF].bitcast(F32))
-            message(1, [c - 1])
+            lead = 2 if c < 3 else 1
+            for i in range(1, lead):
+                message(i, [c - 1])
             smooth(nc.gpsimd, 0, c, 1, 2, words(h, NARROW, CHUNK))
             weave_on_scalar(scale_on_scalar(1, c), words(h, CHUNK, 2 * CHUNK))
-            code_tiles(c, "weighted%d_1" % (c - 1))
+            biased = [
+                relay.tile([P, CHUNK], F32, name="late%d_%d" % (c, x), align_bytes=64, offset=(5 * c + 1 + x) * KB)
+                for x in range(2)
+            ]
+            ready = [weigh(lead + x, [c - 1], biased[x][:]) for x in range(2)]
+            code_tiles(c)
             quantize_h(c, 0, 2 * CHUNK, h[:])
-            pair = keep.tile([P, 2, CHUNK], F32, name="relay%d" % (c % 2), align_bytes=64)
-            for i in range(2, 4 if c < 3 else 3):
-                message(i, [c - 1], pair[:, i - 2, :])
-            if c == 1:
-                narrow = third
-                act_tiles([(0, 2)], "relay1")
-                act_tiles([(1, 2)], "raw5_0")
-            if c == 2:
-                narrow = bank_by_bank(narrow_sums(0, 3, (6, 7)))
-                act_tiles([(0, 3)], "relay0")
-                act_tiles([(1, 3)], "raw5_0")
+            for x in range(2):
+                scatter(lead + x, [c - 1], ready[x])
             if c < 3:
-                paired = bank_by_bank(paired_sums(1, c + 1, (0, 1)))
-            if c < 3:
+                narrow = bank_by_bank(narrow_sums(0, c + 1, (6, 7)))
+                paired = bank_by_bank(paired_sums(1, c + 1, (0, 1)), (3, 0, 1, 2))
+                planar_tile(c + 1)
+                act_tiles([(0, c + 1)], "raw%d_0" % (2 * c - 2))
                 for x in range(2):
                     tanh_woven(0, c + 1, x, narrow[x])
                 for x in range(2):

@@ -342,16 +342,19 @@ def tile_list_msg_tanh_res_bias_kernel(
         clear(3, "page3")
         early = [sums for c in range(2) for sums in add_up(narrow_sums(0, c, (2 * c, 2 * c + 1)))]
         round_w(4, 0, P, "scalar")
-        act_tiles([(0, 0), (0, 1)], "raw4_0")
-        for x in range(4):
-            tanh_woven(0, x // 2, x % 2, early[x])
         quantize_w(4)
-        round_w(5, 0, P, "vector")
+        round_w(5, 0, P, "scalar")
         quantize_w(5)
+        act_tiles([(0, 0)], "raw5_0")
+        for x in range(2):
+            tanh_woven(0, 0, x, early[x])
         round_w(6, 0, P, "vector")
         quantize_w(6)
         last_weight_tile()
-        sums = add_up(narrow_sums(1, 0, (4, 5))) + bank_by_bank(paired_sums(1, 1, (6, 7)), (1, 0, 3, 2))
+        act_tiles([(0, 1)], "raw7_0")
+        for x in range(2):
+            tanh_woven(0, 1, x, early[2 + x])
+        sums = add_up(narrow_sums(1, 0, (4, 5))) + bank_by_bank(paired_sums(1, 1, (6, 7)), (0, 1, 3, 2))
 
         code_tiles(0)
         first = keep.tile([P, CHUNK, 4], BF16, name="last0", align_bytes=64)

@@ -34,7 +34,6 @@ def tile_list_msg_tanh_res_bias_kernel(
         keep = ctx.enter_context(tc.tile_pool(name="keep", bufs=1))
         ring = ctx.enter_context(tc.tile_pool(name="ring", bufs=3))
         relay = ctx.enter_context(tc.tile_pool(name="relay", bufs=1))
-        reuse = ctx.enter_context(tc.tile_pool(name="reuse", bufs=1))
         psum = ctx.enter_context(tc.psum_pool(name="psum", bufs=1))
 
         lists = [keep.tile([P, J // 16], U16, name="list%d" % s) for s in range(2)]
@@ -43,7 +42,9 @@ def tile_list_msg_tanh_res_bias_kernel(
         sm_sb = keep.tile([P, 2, 4], F32, name="sm_sb")
         b_sb = keep.tile([P, 4], F32, name="b_sb")
         picked_sc = keep.tile([P, 2, J], U8, name="picked_sc", align_bytes=64)
-        planes, wd_sc = {}, {}
+        planes = {}
+        wd_planes = keep.tile([P, 2, 2, N], U8, name="wd_planes", align_bytes=64)
+        wd_sc = [wd_planes[:, tier] for tier in range(2)]
         wd4 = keep.tile([P, 2, N // 2], I32, name="wd4", align_bytes=64)
         wd8 = keep.tile([P, 2, N], I32, name="wd8", align_bytes=64)
         wgo_sb = keep.tile([P, J], F32, name="wgo_sb")
@@ -63,13 +64,17 @@ def tile_list_msg_tanh_res_bias_kernel(
             rows = weights[s][PASS * a : PASS * (a + 1), PASS * g + c0 : PASS * g + c1]
             nc.sync.dma_start(out=raw[n, c0][:], in_=rows.rearrange("(p j) c -> p j c", j=4))
 
+        def load_both_groups(k):
+            s, a = steps[k]
+            both = keep.tile([P, 4, R], F32, name="both%d" % k, align_bytes=64)
+            nc.sync.dma_start(out=both[:], in_=weights[s][PASS * a : PASS * (a + 1), :].rearrange("(p j) c -> p j c", j=4))
+            for g in range(2):
+                raw[4 * g + k, 0] = both[:, :, PASS * g : PASS * (g + 1)]
+
         def round_w(n, m0, m1, engine, c0=0):
             if n not in rounded:
-                if n == 1:
-                    rounded[n] = reuse.tile([P, 4 * PASS], BF16, name="rounded1", align_bytes=64, offset=6 * KB)
-                elif n in (3, 7):
-                    tag = {3: "page3", 7: "last"}[n]
-                    rounded[n] = keep.tile([P, 4 * PASS], BF16, name=tag, align_bytes=64)
+                if n == 2:
+                    rounded[n] = keep.tile([P, 4 * PASS], BF16, name="parted1", align_bytes=64)
                 else:
                     rounded[n] = ring.tile([P, 4 * PASS], BF16, name="rounded", align_bytes=64, bufs=3)
             dst = rounded[n][:].rearrange("p (t m j) -> p m j t", t=4, j=4)[:, m0:m1]
@@ -110,10 +115,7 @@ def tile_list_msg_tanh_res_bias_kernel(
                     )
 
         def clear(i, tag):
-            if i == 2:
-                placed[i] = reuse.tile([P, T], F32, name=tag, align_bytes=64, offset=8 * KB)
-            else:
-                placed[i] = keep.tile([P, T], F32, name=tag, align_bytes=64)
+            placed[i] = keep.tile([P, T], F32, name=tag, align_bytes=64)
             nc.vector.memset(placed[i][:].bitcast(I32), 0)
 
         def gather_scales():
@@ -124,7 +126,7 @@ def tile_list_msg_tanh_res_bias_kernel(
             if a == 0:
                 planes[a] = keep.tile([P, 2, J], U8, name="tab_sc", align_bytes=64)
             else:
-                planes[a] = reuse.tile([P, 2, J], U8, name="plane1", align_bytes=64, offset=0)
+                planes[a] = keep.tile([P, 2, J], U8, name="picked0", align_bytes=64)
             for q in range(4):
                 row = SCALE_ROWS_AT + 16 * a + 4 * q
                 nc.sync.dma_start(
@@ -133,19 +135,13 @@ def tile_list_msg_tanh_res_bias_kernel(
 
         def gather_words(half):
             j0, j1 = HALF * half, HALF * (half + 1)
-            if half == 0:
-                picked_w = reuse.tile([P, 2, HALF], I32, name="picked0", align_bytes=64, offset=0)
-            else:
-                picked_w = keep.tile([P, 2, HALF], I32, name="picked1", align_bytes=64)
+            picked_w = keep.tile([P, 2, HALF], I32, name="picked%d" % half, align_bytes=64)
             for s in range(2):
                 nc.vector.tensor_copy(picked_w[:, s, :].bitcast(U32), tab_w[:].bitcast(U32).indirect(entries(s, j0, j1)))
             return picked_w
 
         def part_words(half, picked_w):
-            if half == 0:
-                parted[half] = keep.tile([P, 2, 2, 2 * HALF], U8, name="parted0", align_bytes=64)
-            else:
-                parted[half] = reuse.tile([P, 2, 2, 2 * HALF], U8, name="parted1", align_bytes=64, offset=4 * KB)
+            parted[half] = keep.tile([P, 2, 2, 2 * HALF], U8, name="parted%d" % half, align_bytes=64)
             for s in range(2):
                 nc.vector.tensor_copy(
                     out=parted[half][:, s, :, :].bitcast(U16),
@@ -154,7 +150,6 @@ def tile_list_msg_tanh_res_bias_kernel(
 
         def load_wd_scales(tier):
             scales = (wd4_scales, wd8_scales)[tier]
-            wd_sc[tier] = reuse.tile([P, 2, N], U8, name="wd_sc%d" % tier, align_bytes=64, offset=(2 + tier) * KB)
             for q in range(4):
                 nc.sync.dma_start(
                     out=wd_sc[tier][32 * q : 32 * q + 4].bitcast(I32),
@@ -187,10 +182,10 @@ def tile_list_msg_tanh_res_bias_kernel(
             sums = [bank(number) for number in numbers]
             return [(g, CHUNK * c, CHUNK, range(2 * x, 2 * x + 2), sums[x]) for x in range(2)]
 
-        def add_up(groups, order=(0, 1, 2, 3)):
+        def add_up(groups, order=(0, 1, 2, 3), begin=True, close=True):
             for k in order:
                 for group in groups:
-                    passes_of(*group, k, k == order[0], k == order[-1])
+                    passes_of(*group, k, begin and k == order[0], close and k == order[-1])
             return [group[-1] for group in groups]
 
         def bank_by_bank(groups, order=(0, 1, 2, 3)):
@@ -296,6 +291,7 @@ def tile_list_msg_tanh_res_bias_kernel(
             if j1 == J:
                 nc.sync.dma_start(out=out[P * i : P * (i + 1), :], in_=placed[i][:])
 
+        nc.vector.memset(wd_planes[:].bitcast(I32), 0)
         nc.vector.memset(tab_sc[0:SCALE_ROWS_AT].bitcast(I32), 0)
         for i in range(2):
             clear(i, "page%d" % i)
@@ -304,63 +300,62 @@ def tile_list_msg_tanh_res_bias_kernel(
         nc.sync.dma_start(
             out=tab_sc[SCALE_ROWS_AT:P].bitcast(I32), in_=tab_scales.rearrange("a q t -> (a q) t").bitcast(I32)
         )
-        load_w(0)
+        load_both_groups(0)
         nc.sync.dma_start(out=tab_w[:], in_=tab_words[0].rearrange("p t b -> p (t b)").bitcast(I32))
         gather_scales()
+        for i in range(2, 4):
+            clear(i, "page%d" % i)
         picked = gather_words(0)
-        nc.sync.dma_start(out=sm_sb[:], in_=sm.rearrange("(g p t) -> p g t", g=2, t=4))
-        with nc.allow_non_contiguous_dma(reason="one bias value for each partition"):
-            nc.sync.dma_start(out=b_sb[:], in_=b.rearrange("(i p) -> p i", p=P))
-        load_w(1)
-        load_w(2)
+        load_wd_scales(1)
+        load_both_groups(1)
         move_scales(0)
+        load_w(2)
+        load_wd_scales(0)
         load_w(3)
-        load_w(4)
         round_w(0, 0, P, "scalar")
         quantize_w(0)
         part_words(0, picked)
         move_scales(1)
-        load_w(5)
-        load_wd_scales(1)
         load_w(6)
-        load_wd_scales(0)
         load_w(7, 0, PASS // 2)
         load_w(7, PASS // 2, PASS)
+        nc.sync.dma_start(out=sm_sb[:], in_=sm.rearrange("(g p t) -> p g t", g=2, t=4))
         nc.sync.dma_start(out=wd8[:], in_=wd8_words.rearrange("a p n i -> p a (n i)").bitcast(I32))
         nc.sync.dma_start(out=wd4[:], in_=wd4_words.rearrange("a p n -> p a n").bitcast(I32))
         nc.sync.dma_start(out=wgo_sb[:], in_=wgo)
+        with nc.allow_non_contiguous_dma(reason="one bias value for each partition"):
+            nc.sync.dma_start(out=b_sb[:], in_=b.rearrange("(i p) -> p i", p=P))
 
+        round_w(4, 0, P, "scalar")
+        quantize_w(4)
         round_w(1, 0, P, "scalar")
         quantize_w(1)
         picked = gather_words(1)
-        round_w(2, 0, P, "scalar")
+        round_w(5, 0, P, "scalar")
+        round_w(2, 0, P, "vector")
+        quantize_w(5, tag="raw2_0")
         quantize_w(2)
         part_words(1, picked)
-        clear(2, "page2")
         round_w(3, 0, P, "scalar")
         quantize_w(3)
-        clear(3, "page3")
-        early = [sums for c in range(2) for sums in add_up(narrow_sums(0, c, (2 * c, 2 * c + 1)))]
-        round_w(4, 0, P, "scalar")
-        quantize_w(4)
-        round_w(5, 0, P, "scalar")
-        quantize_w(5)
-        act_tiles([(0, 0)], "raw5_0")
-        for x in range(2):
-            tanh_woven(0, 0, x, early[x])
-        round_w(6, 0, P, "vector")
+        head = narrow_sums(0, 0, (0, 1)) + narrow_sums(0, 1, (2, 3)) + narrow_sums(1, 0, (4, 5)) + paired_sums(1, 1, (6, 7))
+        add_up(head, (0, 1), close=False)
+        early = add_up(head[0:2], (2, 3), begin=False) + add_up(head[2:4], (2, 3), begin=False)
+        round_w(6, 0, P // 2, "vector")
+        round_w(6, P // 2, P, "scalar")
         quantize_w(6)
         last_weight_tile()
-        act_tiles([(0, 1)], "raw7_0")
-        for x in range(2):
-            tanh_woven(0, 1, x, early[2 + x])
-        sums = add_up(narrow_sums(1, 0, (4, 5))) + bank_by_bank(paired_sums(1, 1, (6, 7)), (0, 1, 3, 2))
+        act_tiles([(0, 0), (0, 1)], "raw7_0")
+        for x in range(4):
+            tanh_woven(0, x // 2, x % 2, early[x])
+        sums = add_up(head[4:6], (2, 3), begin=False)
+        sums = sums + [add_up([group], (3, 2), begin=False)[0] for group in head[6:8]]
 
         code_tiles(0)
         first = keep.tile([P, CHUNK, 4], BF16, name="last0", align_bytes=64)
         smooth(nc.vector, 0, 0, 0, 2, first[:])
         quantize_h(0, 0, CHUNK, first[:].rearrange("p j t -> p (j t)"))
-        act_tiles([(1, 0)], "raw1_0")
+        act_tiles([(1, 0)], "both0")
         h = h_tile()
         for x in range(2):
             tanh_woven(1, 0, x, sums[x])
@@ -392,7 +387,7 @@ def tile_list_msg_tanh_res_bias_kernel(
                 narrow = bank_by_bank(narrow_sums(0, c + 1, (6, 7)))
                 paired = bank_by_bank(paired_sums(1, c + 1, (0, 1)), (3, 0, 1, 2))
                 planar_tile(c + 1)
-                act_tiles([(0, c + 1)], "raw%d_0" % (2 * c - 2))
+                act_tiles([(0, c + 1)], ("raw3_0", "raw6_0")[c - 1])
                 for x in range(2):
                     tanh_woven(0, c + 1, x, narrow[x])
                 for x in range(2):

@@ -43,8 +43,7 @@ def tile_list_msg_tanh_res_bias_kernel(
         b_sb = keep.tile([P, 4], F32, name="b_sb")
         picked_sc = keep.tile([P, 2, J], U8, name="picked_sc", align_bytes=64)
         planes = {}
-        wd_planes = keep.tile([P, 2, 2, N], U8, name="wd_planes", align_bytes=64)
-        wd_sc = [wd_planes[:, tier] for tier in range(2)]
+        wd_sc = []
         wd4 = keep.tile([P, 2, N // 2], I32, name="wd4", align_bytes=64)
         wd8 = keep.tile([P, 2, N], I32, name="wd8", align_bytes=64)
         wgo_sb = keep.tile([P, J], F32, name="wgo_sb")
@@ -126,7 +125,7 @@ def tile_list_msg_tanh_res_bias_kernel(
             if a == 0:
                 planes[a] = keep.tile([P, 2, J], U8, name="tab_sc", align_bytes=64)
             else:
-                planes[a] = keep.tile([P, 2, J], U8, name="picked0", align_bytes=64)
+                planes[a] = late_planes[:, 0]
             for q in range(4):
                 row = SCALE_ROWS_AT + 16 * a + 4 * q
                 nc.sync.dma_start(
@@ -289,9 +288,12 @@ def tile_list_msg_tanh_res_bias_kernel(
             j0, j1 = CHUNK * chunks[0], CHUNK * (chunks[-1] + 1)
             nc.vector.tensor_copy(placed[i][:].indirect(entries(1, j0, j1)), weighted[:])
             if j1 == J:
-                nc.sync.dma_start(out=out[P * i : P * (i + 1), :], in_=placed[i][:])
+                if i < 3:
+                    nc.sync.dma_start(out=out[P * i : P * (i + 1), :], in_=placed[i][:])
+                else:
+                    for queue, t0 in ((nc.sync, 0), (nc.scalar, T // 2)):
+                        queue.dma_start(out=out[P * i : P * (i + 1), t0 : t0 + T // 2], in_=placed[i][:, t0 : t0 + T // 2])
 
-        nc.vector.memset(wd_planes[:].bitcast(I32), 0)
         nc.vector.memset(tab_sc[0:SCALE_ROWS_AT].bitcast(I32), 0)
         for i in range(2):
             clear(i, "page%d" % i)
@@ -306,17 +308,20 @@ def tile_list_msg_tanh_res_bias_kernel(
         for i in range(2, 4):
             clear(i, "page%d" % i)
         picked = gather_words(0)
-        load_wd_scales(1)
         load_both_groups(1)
         move_scales(0)
         load_w(2)
-        load_wd_scales(0)
-        load_w(3)
         round_w(0, 0, P, "scalar")
+        round_w(4, 0, P, "scalar")
+        late_planes = keep.tile([P, 2, 2, J], U8, name="both0", align_bytes=64)
+        wd_sc.extend(late_planes[:, 1, tier].rearrange("p (a n) -> p a n", a=2) for tier in range(2))
+        load_wd_scales(1)
+        load_w(3)
         quantize_w(0)
         part_words(0, picked)
         move_scales(1)
         load_w(6)
+        load_wd_scales(0)
         load_w(7, 0, PASS // 2)
         load_w(7, PASS // 2, PASS)
         nc.sync.dma_start(out=sm_sb[:], in_=sm.rearrange("(g p t) -> p g t", g=2, t=4))
@@ -326,7 +331,6 @@ def tile_list_msg_tanh_res_bias_kernel(
         with nc.allow_non_contiguous_dma(reason="one bias value for each partition"):
             nc.sync.dma_start(out=b_sb[:], in_=b.rearrange("(i p) -> p i", p=P))
 
-        round_w(4, 0, P, "scalar")
         quantize_w(4)
         round_w(1, 0, P, "scalar")
         quantize_w(1)
@@ -355,7 +359,7 @@ def tile_list_msg_tanh_res_bias_kernel(
         first = keep.tile([P, CHUNK, 4], BF16, name="last0", align_bytes=64)
         smooth(nc.vector, 0, 0, 0, 2, first[:])
         quantize_h(0, 0, CHUNK, first[:].rearrange("p j t -> p (j t)"))
-        act_tiles([(1, 0)], "both0")
+        act_tiles([(1, 0)], "act10")
         h = h_tile()
         for x in range(2):
             tanh_woven(1, 0, x, sums[x])

@@ -24,6 +24,9 @@ CHUNK = 256
 NARROW = 128
 SCALE_ROWS_AT = 96
 KB = 1024
+RUN = 32
+PITCH = 36
+FIRST_RUNS = 17
 
 
 def tile_list_msg_tanh_res_bias_kernel(
@@ -34,6 +37,7 @@ def tile_list_msg_tanh_res_bias_kernel(
         keep = ctx.enter_context(tc.tile_pool(name="keep", bufs=1))
         ring = ctx.enter_context(tc.tile_pool(name="ring", bufs=3))
         relay = ctx.enter_context(tc.tile_pool(name="relay", bufs=1))
+        shared = ctx.enter_context(tc.tile_pool(name="shared", bufs=1))
         psum = ctx.enter_context(tc.psum_pool(name="psum", bufs=1))
 
         lists = [keep.tile([P, J // 16], U16, name="list%d" % s) for s in range(2)]
@@ -74,6 +78,9 @@ def tile_list_msg_tanh_res_bias_kernel(
             if n not in rounded:
                 if n == 2:
                     rounded[n] = keep.tile([P, 4 * PASS], BF16, name="parted1", align_bytes=64)
+                elif n in (0, 4):
+                    at = 0 if n == 0 else 11 * KB
+                    rounded[n] = shared.tile([P, 4 * PASS], BF16, name="rounded%d" % n, align_bytes=64, offset=at)
                 else:
                     rounded[n] = ring.tile([P, 4 * PASS], BF16, name="rounded", align_bytes=64, bufs=3)
             dst = rounded[n][:].rearrange("p (t m j) -> p m j t", t=4, j=4)[:, m0:m1]
@@ -117,6 +124,10 @@ def tile_list_msg_tanh_res_bias_kernel(
             placed[i] = keep.tile([P, T], F32, name=tag, align_bytes=64)
             nc.vector.memset(placed[i][:].bitcast(I32), 0)
 
+        def clear_on_gpsimd(i, at):
+            placed[i] = shared.tile([P, T], F32, name="page%d" % i, align_bytes=64, offset=at)
+            nc.gpsimd.memset(placed[i][:].bitcast(I32), 0)
+
         def gather_scales():
             for s in range(2):
                 nc.vector.tensor_copy(picked_sc[:, s, :], tab_sc[:].indirect(lists[s][:]))
@@ -133,19 +144,27 @@ def tile_list_msg_tanh_res_bias_kernel(
                 )
 
         def gather_words(half):
-            j0, j1 = HALF * half, HALF * (half + 1)
-            picked_w = keep.tile([P, 2, HALF], I32, name="picked%d" % half, align_bytes=64)
-            for s in range(2):
-                nc.vector.tensor_copy(picked_w[:, s, :].bitcast(U32), tab_w[:].bitcast(U32).indirect(entries(s, j0, j1)))
-            return picked_w
-
-        def part_words(half, picked_w):
-            parted[half] = keep.tile([P, 2, 2, 2 * HALF], U8, name="parted%d" % half, align_bytes=64)
+            r0, r1 = ((0, FIRST_RUNS), (FIRST_RUNS, J // RUN))[half]
+            if half == 0:
+                picked_w = keep.tile([P, 2, r1 - r0, PITCH], I32, name="picked0", align_bytes=64)
+            else:
+                picked_w = shared.tile([P, 2, r1 - r0, PITCH], I32, name="picked1", align_bytes=64, offset=8 * KB)
             for s in range(2):
                 nc.vector.tensor_copy(
-                    out=parted[half][:, s, :, :].bitcast(U16),
-                    in_=picked_w[:, s, :].bitcast(U16).rearrange("p (j d) -> p d j", d=2),
+                    picked_w[:, s, :, 0:RUN].bitcast(U32), tab_w[:].bitcast(U32).indirect(entries(s, RUN * r0, RUN * r1))
                 )
+            return picked_w
+
+        def part_words(half, pieces):
+            parted[half] = keep.tile([P, 2, 2, 2 * HALF], U8, name="parted%d" % half, align_bytes=64)
+            for picked_w, r0, r1, at in pieces:
+                for s in range(2):
+                    nc.vector.tensor_copy(
+                        out=parted[half][:, s, :, 2 * RUN * at : 2 * RUN * (at + r1 - r0)]
+                        .bitcast(U16)
+                        .rearrange("p d (r j) -> p d r j", j=RUN),
+                        in_=picked_w[:, s, r0:r1, 0:RUN].bitcast(U16).rearrange("p r (j d) -> p d r j", d=2),
+                    )
 
         def load_wd_scales(tier):
             scales = (wd4_scales, wd8_scales)[tier]
@@ -305,9 +324,7 @@ def tile_list_msg_tanh_res_bias_kernel(
         load_both_groups(0)
         nc.sync.dma_start(out=tab_w[:], in_=tab_words[0].rearrange("p t b -> p (t b)").bitcast(I32))
         gather_scales()
-        for i in range(2, 4):
-            clear(i, "page%d" % i)
-        picked = gather_words(0)
+        first_picked = gather_words(0)
         load_both_groups(1)
         move_scales(0)
         load_w(2)
@@ -318,7 +335,8 @@ def tile_list_msg_tanh_res_bias_kernel(
         load_wd_scales(1)
         load_w(3)
         quantize_w(0)
-        part_words(0, picked)
+        clear_on_gpsimd(2, 0)
+        part_words(0, [(first_picked, 0, HALF // RUN, 0)])
         move_scales(1)
         load_w(6)
         load_wd_scales(0)
@@ -332,14 +350,15 @@ def tile_list_msg_tanh_res_bias_kernel(
             nc.sync.dma_start(out=b_sb[:], in_=b.rearrange("(i p) -> p i", p=P))
 
         quantize_w(4)
+        clear_on_gpsimd(3, 13 * KB)
+        picked = gather_words(1)
         round_w(1, 0, P, "scalar")
         quantize_w(1)
-        picked = gather_words(1)
         round_w(5, 0, P, "scalar")
         round_w(2, 0, P, "vector")
         quantize_w(5, tag="raw2_0")
         quantize_w(2)
-        part_words(1, picked)
+        part_words(1, [(first_picked, HALF // RUN, FIRST_RUNS, 0), (picked, 0, J // RUN - FIRST_RUNS, FIRST_RUNS - HALF // RUN)])
         round_w(3, 0, P, "scalar")
         quantize_w(3)
         head = narrow_sums(0, 0, (0, 1)) + narrow_sums(0, 1, (2, 3)) + narrow_sums(1, 0, (4, 5)) + paired_sums(1, 1, (6, 7))

@@ -41,7 +41,8 @@ def tile_list_msg_tanh_res_bias_kernel(
         psum = ctx.enter_context(tc.psum_pool(name="psum", bufs=1))
 
         lists = [keep.tile([P, J // 16], U16, name="list%d" % s) for s in range(2)]
-        tab_sc = keep.tile([P, T], U8, name="tab_sc", align_bytes=64)
+        tab_sc = shared.tile([P, T], U8, name="tab_sc", align_bytes=64, offset=7 * KB)
+        first_plane = keep.tile([P, 2, J], U8, name="first_plane", align_bytes=64)
         tab_w = keep.tile([P, T], I32, name="tab_w", align_bytes=64)
         sm_sb = keep.tile([P, 2, 4], F32, name="sm_sb")
         b_sb = keep.tile([P, 4], F32, name="b_sb")
@@ -76,11 +77,8 @@ def tile_list_msg_tanh_res_bias_kernel(
 
         def round_w(n, m0, m1, engine, c0=0):
             if n not in rounded:
-                if n == 2:
+                if n == 0:
                     rounded[n] = keep.tile([P, 4 * PASS], BF16, name="parted1", align_bytes=64)
-                elif n in (0, 4):
-                    at = 0 if n == 0 else 11 * KB
-                    rounded[n] = shared.tile([P, 4 * PASS], BF16, name="rounded%d" % n, align_bytes=64, offset=at)
                 else:
                     rounded[n] = ring.tile([P, 4 * PASS], BF16, name="rounded", align_bytes=64, bufs=3)
             dst = rounded[n][:].rearrange("p (t m j) -> p m j t", t=4, j=4)[:, m0:m1]
@@ -134,7 +132,7 @@ def tile_list_msg_tanh_res_bias_kernel(
 
         def move_scales(a):
             if a == 0:
-                planes[a] = keep.tile([P, 2, J], U8, name="tab_sc", align_bytes=64)
+                planes[a] = first_plane
             else:
                 planes[a] = late_planes[:, 0]
             for q in range(4):
@@ -143,28 +141,24 @@ def tile_list_msg_tanh_res_bias_kernel(
                     out=planes[a][32 * q : 32 * q + 4].bitcast(I32), in_=picked_sc[row : row + 4].bitcast(I32)
                 )
 
-        def gather_words(half):
-            r0, r1 = ((0, FIRST_RUNS), (FIRST_RUNS, J // RUN))[half]
-            if half == 0:
-                picked_w = keep.tile([P, 2, r1 - r0, PITCH], I32, name="picked0", align_bytes=64)
-            else:
-                picked_w = shared.tile([P, 2, r1 - r0, PITCH], I32, name="picked1", align_bytes=64, offset=8 * KB)
-            for s in range(2):
-                nc.vector.tensor_copy(
-                    picked_w[:, s, :, 0:RUN].bitcast(U32), tab_w[:].bitcast(U32).indirect(entries(s, RUN * r0, RUN * r1))
-                )
-            return picked_w
-
-        def part_words(half, pieces):
-            parted[half] = keep.tile([P, 2, 2, 2 * HALF], U8, name="parted%d" % half, align_bytes=64)
-            for picked_w, r0, r1, at in pieces:
+        def gather_words():
+            picked_w = keep.tile([P, 2, J // RUN, PITCH], I32, name="picked", align_bytes=64)
+            for r0, r1 in ((0, FIRST_RUNS), (FIRST_RUNS, J // RUN)):
                 for s in range(2):
                     nc.vector.tensor_copy(
-                        out=parted[half][:, s, :, 2 * RUN * at : 2 * RUN * (at + r1 - r0)]
-                        .bitcast(U16)
-                        .rearrange("p d (r j) -> p d r j", j=RUN),
-                        in_=picked_w[:, s, r0:r1, 0:RUN].bitcast(U16).rearrange("p r (j d) -> p d r j", d=2),
+                        picked_w[:, s, r0:r1, 0:RUN].bitcast(U32),
+                        tab_w[:].bitcast(U32).indirect(entries(s, RUN * r0, RUN * r1)),
                     )
+            return picked_w
+
+        def part_words(half, picked_w):
+            parted[half] = keep.tile([P, 2, 2, 2 * HALF], U8, name="parted%d" % half, align_bytes=64)
+            runs = slice(HALF // RUN * half, HALF // RUN * (half + 1))
+            for s in range(2):
+                nc.vector.tensor_copy(
+                    out=parted[half][:, s].bitcast(U16).rearrange("p d (r j) -> p d r j", j=RUN),
+                    in_=picked_w[:, s, runs, 0:RUN].bitcast(U16).rearrange("p r (j d) -> p d r j", d=2),
+                )
 
         def load_wd_scales(tier):
             scales = (wd4_scales, wd8_scales)[tier]
@@ -314,6 +308,7 @@ def tile_list_msg_tanh_res_bias_kernel(
                         queue.dma_start(out=out[P * i : P * (i + 1), t0 : t0 + T // 2], in_=placed[i][:, t0 : t0 + T // 2])
 
         nc.vector.memset(tab_sc[0:SCALE_ROWS_AT].bitcast(I32), 0)
+        nc.vector.memset(first_plane[:].bitcast(I32), 0)
         for i in range(2):
             clear(i, "page%d" % i)
         nc.sync.dma_start(lists[0][:], offs)
@@ -321,10 +316,12 @@ def tile_list_msg_tanh_res_bias_kernel(
         nc.sync.dma_start(
             out=tab_sc[SCALE_ROWS_AT:P].bitcast(I32), in_=tab_scales.rearrange("a q t -> (a q) t").bitcast(I32)
         )
-        load_both_groups(0)
         nc.sync.dma_start(out=tab_w[:], in_=tab_words[0].rearrange("p t b -> p (t b)").bitcast(I32))
+        load_both_groups(0)
         gather_scales()
-        first_picked = gather_words(0)
+        clear_on_gpsimd(2, 8 * KB)
+        clear_on_gpsimd(3, 0)
+        picked = gather_words()
         load_both_groups(1)
         move_scales(0)
         load_w(2)
@@ -335,8 +332,7 @@ def tile_list_msg_tanh_res_bias_kernel(
         load_wd_scales(1)
         load_w(3)
         quantize_w(0)
-        clear_on_gpsimd(2, 0)
-        part_words(0, [(first_picked, 0, HALF // RUN, 0)])
+        part_words(0, picked)
         move_scales(1)
         load_w(6)
         load_wd_scales(0)
@@ -350,15 +346,14 @@ def tile_list_msg_tanh_res_bias_kernel(
             nc.sync.dma_start(out=b_sb[:], in_=b.rearrange("(i p) -> p i", p=P))
 
         quantize_w(4)
-        clear_on_gpsimd(3, 13 * KB)
-        picked = gather_words(1)
+        part_words(1, picked)
+        round_w(5, 0, P // 2, "vector")
         round_w(1, 0, P, "scalar")
         quantize_w(1)
-        round_w(5, 0, P, "scalar")
+        round_w(5, P // 2, P, "scalar")
         round_w(2, 0, P, "vector")
         quantize_w(5, tag="raw2_0")
         quantize_w(2)
-        part_words(1, [(first_picked, HALF // RUN, FIRST_RUNS, 0), (picked, 0, J // RUN - FIRST_RUNS, FIRST_RUNS - HALF // RUN)])
         round_w(3, 0, P, "scalar")
         quantize_w(3)
         head = narrow_sums(0, 0, (0, 1)) + narrow_sums(0, 1, (2, 3)) + narrow_sums(1, 0, (4, 5)) + paired_sums(1, 1, (6, 7))

@@ -27,6 +27,7 @@ KB = 1024
 RUN = 32
 PITCH = 36
 FIRST_RUNS = 17
+VECTOR_SHARE_3 = 86
 
 
 def tile_list_msg_tanh_res_bias_kernel(
@@ -42,13 +43,13 @@ def tile_list_msg_tanh_res_bias_kernel(
 
         lists = [keep.tile([P, J // 16], U16, name="list%d" % s) for s in range(2)]
         tab_sc = shared.tile([P, T], U8, name="tab_sc", align_bytes=64, offset=7 * KB)
-        first_plane = keep.tile([P, 2, J], U8, name="first_plane", align_bytes=64)
+        early_planes = keep.tile([P, 2, 2, J], U8, name="early_planes", align_bytes=64)
         tab_w = keep.tile([P, T], I32, name="tab_w", align_bytes=64)
         sm_sb = keep.tile([P, 2, 4], F32, name="sm_sb")
         b_sb = keep.tile([P, 4], F32, name="b_sb")
         picked_sc = keep.tile([P, 2, J], U8, name="picked_sc", align_bytes=64)
         planes = {}
-        wd_sc = []
+        wd_sc = [early_planes[:, 1, tier].rearrange("p (a n) -> p a n", a=2) for tier in range(2)]
         wd4 = keep.tile([P, 2, N // 2], I32, name="wd4", align_bytes=64)
         wd8 = keep.tile([P, 2, N], I32, name="wd8", align_bytes=64)
         wgo_sb = keep.tile([P, J], F32, name="wgo_sb")
@@ -80,7 +81,7 @@ def tile_list_msg_tanh_res_bias_kernel(
                 if n == 0:
                     rounded[n] = keep.tile([P, 4 * PASS], BF16, name="parted1", align_bytes=64)
                 else:
-                    rounded[n] = ring.tile([P, 4 * PASS], BF16, name="rounded", align_bytes=64, bufs=3)
+                    rounded[n] = ring.tile([P, 4 * PASS], BF16, name="rounded", align_bytes=64, bufs=4)
             dst = rounded[n][:].rearrange("p (t m j) -> p m j t", t=4, j=4)[:, m0:m1]
             src = raw[n, c0][:].rearrange("p j (m t) -> p m j t", t=4)[:, m0 - c0 // 4 : m1 - c0 // 4]
             if engine == "vector":
@@ -132,9 +133,9 @@ def tile_list_msg_tanh_res_bias_kernel(
 
         def move_scales(a):
             if a == 0:
-                planes[a] = first_plane
+                planes[a] = early_planes[:, 0]
             else:
-                planes[a] = late_planes[:, 0]
+                planes[a] = keep.tile([P, 2, J], U8, name="both0", align_bytes=64)
             for q in range(4):
                 row = SCALE_ROWS_AT + 16 * a + 4 * q
                 nc.sync.dma_start(
@@ -308,7 +309,7 @@ def tile_list_msg_tanh_res_bias_kernel(
                         queue.dma_start(out=out[P * i : P * (i + 1), t0 : t0 + T // 2], in_=placed[i][:, t0 : t0 + T // 2])
 
         nc.vector.memset(tab_sc[0:SCALE_ROWS_AT].bitcast(I32), 0)
-        nc.vector.memset(first_plane[:].bitcast(I32), 0)
+        nc.vector.memset(early_planes[:].bitcast(I32), 0)
         for i in range(2):
             clear(i, "page%d" % i)
         nc.sync.dma_start(lists[0][:], offs)
@@ -317,25 +318,22 @@ def tile_list_msg_tanh_res_bias_kernel(
             out=tab_sc[SCALE_ROWS_AT:P].bitcast(I32), in_=tab_scales.rearrange("a q t -> (a q) t").bitcast(I32)
         )
         nc.sync.dma_start(out=tab_w[:], in_=tab_words[0].rearrange("p t b -> p (t b)").bitcast(I32))
+        load_wd_scales(1)
         load_both_groups(0)
+        load_wd_scales(0)
         gather_scales()
         clear_on_gpsimd(2, 8 * KB)
         clear_on_gpsimd(3, 0)
         picked = gather_words()
         load_both_groups(1)
         move_scales(0)
-        load_w(2)
+        load_both_groups(2)
         round_w(0, 0, P, "scalar")
         round_w(4, 0, P, "scalar")
-        late_planes = keep.tile([P, 2, 2, J], U8, name="both0", align_bytes=64)
-        wd_sc.extend(late_planes[:, 1, tier].rearrange("p (a n) -> p a n", a=2) for tier in range(2))
-        load_wd_scales(1)
+        move_scales(1)
         load_w(3)
         quantize_w(0)
         part_words(0, picked)
-        move_scales(1)
-        load_w(6)
-        load_wd_scales(0)
         load_w(7, 0, PASS // 2)
         load_w(7, PASS // 2, PASS)
         nc.sync.dma_start(out=sm_sb[:], in_=sm.rearrange("(g p t) -> p g t", g=2, t=4))
@@ -352,16 +350,16 @@ def tile_list_msg_tanh_res_bias_kernel(
         quantize_w(1)
         round_w(5, P // 2, P, "scalar")
         round_w(2, 0, P, "vector")
-        quantize_w(5, tag="raw2_0")
+        quantize_w(5)
+        round_w(6, 0, P, "scalar")
         quantize_w(2)
-        round_w(3, 0, P, "scalar")
+        round_w(3, 0, VECTOR_SHARE_3, "vector")
+        round_w(3, VECTOR_SHARE_3, P, "scalar")
         quantize_w(3)
         head = narrow_sums(0, 0, (0, 1)) + narrow_sums(0, 1, (2, 3)) + narrow_sums(1, 0, (4, 5)) + paired_sums(1, 1, (6, 7))
         add_up(head, (0, 1), close=False)
         early = add_up(head[0:2], (2, 3), begin=False) + add_up(head[2:4], (2, 3), begin=False)
-        round_w(6, 0, P // 2, "vector")
-        round_w(6, P // 2, P, "scalar")
-        quantize_w(6)
+        quantize_w(6, tag="raw3_0")
         last_weight_tile()
         act_tiles([(0, 0), (0, 1)], "raw7_0")
         for x in range(4):
@@ -405,7 +403,7 @@ def tile_list_msg_tanh_res_bias_kernel(
                 narrow = bank_by_bank(narrow_sums(0, c + 1, (6, 7)))
                 paired = bank_by_bank(paired_sums(1, c + 1, (0, 1)), (3, 0, 1, 2))
                 planar_tile(c + 1)
-                act_tiles([(0, c + 1)], ("raw3_0", "raw6_0")[c - 1])
+                act_tiles([(0, c + 1)], ("both1", "both2")[c - 1])
                 for x in range(2):
                     tanh_woven(0, c + 1, x, narrow[x])
                 for x in range(2):

from contextlib import ExitStack

import concourse.mybir as mybir

K, R, N, T, J = 1024, 1024, 512, 2048, 1024
FLOPS = 2 * (2 * K * R * J + 2 * R * N * J)

F32 = mybir.dt.float32
BF16 = mybir.dt.bfloat16
I32 = mybir.dt.int32
U32 = mybir.dt.uint32
U16 = mybir.dt.uint16
U8 = mybir.dt.uint8
FP8X4 = mybir.dt.float8_e4m3fn_x4
FP4X4 = mybir.dt.float4_e2m1fn_x4
ACT = mybir.ActivationFunctionType
MULT = mybir.AluOpType.mult
ADD = mybir.AluOpType.add

P = 128
PASS = 512
HALF = 512
CHUNK = 256
NARROW = 128
SCALE_ROWS_AT = 96
KB = 1024
RUN = 32
PITCH = 36
FIRST_RUNS = 17
VECTOR_SHARE_3 = 86


def tile_list_msg_tanh_res_bias_kernel(
    tc, tab_words, tab_scales, ws, wt, sm, wd4_words, wd4_scales, wd8_words, wd8_scales, b, wgo, offs, offs2, out
):
    nc = tc.nc
    with ExitStack() as ctx:
        keep = ctx.enter_context(tc.tile_pool(name="keep", bufs=1))
        ring = ctx.enter_context(tc.tile_pool(name="ring", bufs=3))
        relay = ctx.enter_context(tc.tile_pool(name="relay", bufs=1))
        shared = ctx.enter_context(tc.tile_pool(name="shared", bufs=1))
        psum = ctx.enter_context(tc.psum_pool(name="psum", bufs=1))

        lists = [keep.tile([P, J // 16], U16, name="list%d" % s) for s in range(2)]
        tab_sc = shared.tile([P, T], U8, name="tab_sc", align_bytes=64, offset=7 * KB)
        early_planes = keep.tile([P, 2, 2, J], U8, name="early_planes", align_bytes=64)
        tab_w = keep.tile([P, T], I32, name="tab_w", align_bytes=64)
        sm_sb = keep.tile([P, 2, 4], F32, name="sm_sb")
        b_sb = keep.tile([P, 4], F32, name="b_sb")
        picked_sc = keep.tile([P, 2, J], U8, name="picked_sc", align_bytes=64)
        planes = {}
        wd_sc = [early_planes[:, 1, tier].rearrange("p (a n) -> p a n", a=2) for tier in range(2)]
        wd4 = keep.tile([P, 2, N // 2], I32, name="wd4", align_bytes=64)
        wd8 = keep.tile([P, 2, N], I32, name="wd8", align_bytes=64)
        wgo_sb = keep.tile([P, J], F32, name="wgo_sb")
        placed = {}
        h_codes, h_sc = {}, {}

        weights = (ws, wt)
        steps = [(s, a) for a in range(2) for s in range(2)]
        raw, rounded, w_codes, w_sc, parted, act = {}, {}, {}, {}, {}, {}

        def entries(s, j0, j1):
            return lists[s][:, j0 // 16 : j1 // 16]

        def load_w(n, c0=0, c1=PASS):
            g, (s, a) = n // 4, steps[n % 4]
            raw[n, c0] = keep.tile([P, 4, c1 - c0], F32, name="raw%d_%d" % (n, c0), align_bytes=64)
            rows = weights[s][PASS * a : PASS * (a + 1), PASS * g + c0 : PASS * g + c1]
            nc.sync.dma_start(out=raw[n, c0][:], in_=rows.rearrange("(p j) c -> p j c", j=4))

        def load_both_groups(k):
            s, a = steps[k]
            both = keep.tile([P, 4, R], F32, name="both%d" % k, align_bytes=64)
            nc.sync.dma_start(out=both[:], in_=weights[s][PASS * a : PASS * (a + 1), :].rearrange("(p j) c -> p j c", j=4))
            for g in range(2):
                raw[4 * g + k, 0] = both[:, :, PASS * g : PASS * (g + 1)]

        def round_w(n, m0, m1, engine, c0=0):
            if n not in rounded:
                if n == 0:
                    rounded[n] = keep.tile([P, 4 * PASS], BF16, name="parted1", align_bytes=64)
                else:
                    rounded[n] = ring.tile([P, 4 * PASS], BF16, name="rounded", align_bytes=64, bufs=4)
            dst = rounded[n][:].rearrange("p (t m j) -> p m j t", t=4, j=4)[:, m0:m1]
            src = raw[n, c0][:].rearrange("p j (m t) -> p m j t", t=4)[:, m0 - c0 // 4 : m1 - c0 // 4]
            if engine == "vector":
                nc.vector.tensor_copy(out=dst, in_=src)
            else:
                nc.scalar.copy(out=dst, in_=src)

        def quantize_w(n, pieces=1, tag=None):
            w_codes[n] = keep.tile([P, PASS], U32, name=tag or "wc%d" % n, align_bytes=64)
            w_sc[n] = keep.tile([P, PASS], U8, name="wsc%d" % n, align_bytes=64)
            step = PASS // pieces
            starts = range(0, PASS, step)
            for c in list(starts[0::2]) + list(starts[1::2]):
                nc.vector.quantize_mx(
                    out=w_codes[n][:, c : c + step].bitcast(FP8X4),
                    scales=w_sc[n][:, c : c + step],
                    in_=rounded[n][:, 4 * c : 4 * (c + step)],
                )

        def last_weight_tile():
            halves = [keep.tile([P, 4, P // 2, 4], BF16, name="last%d" % x, align_bytes=64) for x in range(2)]
            for x, copy in enumerate((nc.scalar.copy, nc.vector.tensor_copy)):
                copy(
                    out=halves[x][:].rearrange("p t m j -> p m j t"),
                    in_=raw[7, PASS // 2 * x][:].rearrange("p j (m t) -> p m j t", t=4),
                )
            w_codes[7] = keep.tile([P, PASS], U32, name="wc7", align_bytes=64)
            w_sc[7] = keep.tile([P, PASS], U8, name="wsc7", align_bytes=64)
            for x in range(2):
                for t in range(4):
                    m = slice(P * t + P // 2 * x, P * t + P // 2 * (x + 1))
                    nc.vector.quantize_mx(
                        out=w_codes[7][:, m].bitcast(FP8X4),
                        scales=w_sc[7][:, m],
                        in_=halves[x][:, t].rearrange("p m j -> p (m j)"),
                    )

        def clear(i, tag):
            placed[i] = keep.tile([P, T], F32, name=tag, align_bytes=64)
            nc.vector.memset(placed[i][:].bitcast(I32), 0)

        def clear_on_gpsimd(i, at):
            placed[i] = shared.tile([P, T], F32, name="page%d" % i, align_bytes=64, offset=at)
            nc.gpsimd.memset(placed[i][:].bitcast(I32), 0)

        def gather_scales():
            for s in range(2):
                nc.vector.tensor_copy(picked_sc[:, s, :], tab_sc[:].indirect(lists[s][:]))

        def move_scales(a):
            if a == 0:
                planes[a] = early_planes[:, 0]
            else:
                planes[a] = keep.tile([P, 2, J], U8, name="both0", align_bytes=64)
            for q in range(4):
                row = SCALE_ROWS_AT + 16 * a + 4 * q
                nc.sync.dma_start(
                    out=planes[a][32 * q : 32 * q + 4].bitcast(I32), in_=picked_sc[row : row + 4].bitcast(I32)
                )

        def gather_words():
            picked_w = keep.tile([P, 2, J // RUN, PITCH], I32, name="picked", align_bytes=64)
            for r0, r1 in ((0, FIRST_RUNS), (FIRST_RUNS, J // RUN)):
                for s in range(2):
                    nc.vector.tensor_copy(
                        picked_w[:, s, r0:r1, 0:RUN].bitcast(U32),
                        tab_w[:].bitcast(U32).indirect(entries(s, RUN * r0, RUN * r1)),
                    )
            return picked_w

        def part_words(half, picked_w):
            parted[half] = keep.tile([P, 2, 2, 2 * HALF], U8, name="parted%d" % half, align_bytes=64)
            runs = slice(HALF // RUN * half, HALF // RUN * (half + 1))
            for s in range(2):
                nc.vector.tensor_copy(
                    out=parted[half][:, s].bitcast(U16).rearrange("p d (r j) -> p d r j", j=RUN),
                    in_=picked_w[:, s, runs, 0:RUN].bitcast(U16).rearrange("p r (j d) -> p d r j", d=2),
                )

        def load_wd_scales(tier):
            scales = (wd4_scales, wd8_scales)[tier]
            for q in range(4):
                nc.sync.dma_start(
                    out=wd_sc[tier][32 * q : 32 * q + 4].bitcast(I32),
                    in_=scales[:, 4 * q : 4 * q + 4, :].rearrange("a r n -> r a n").bitcast(I32),
                )

        def bank(number, width=HALF):
            return psum.tile([P, width], F32, name="bank%d" % number)

        def passes_of(g, j0, width, slices, sums, k, first, last):
            s, a = steps[k]
            c0 = j0 % HALF
            for x, t in enumerate(slices):
                m = slice(P * t, P * (t + 1))
                nc.tensor.matmul_mx(
                    out=sums[:, width * x : width * (x + 1)],
                    lhsT=w_codes[4 * g + k][:, m].bitcast(FP8X4),
                    lhsT_scale=w_sc[4 * g + k][:, m],
                    rhs=parted[j0 // HALF][:, s, a, 2 * c0 : 2 * (c0 + width)].bitcast(FP4X4),
                    rhs_scale=planes[a][:, s, j0 : j0 + width],
                    start=(first and x == 0),
                    stop=(last and x == len(slices) - 1),
                )

        def narrow_sums(g, c, numbers):
            sums = [bank(number) for number in numbers]
            return [(g, CHUNK * c + NARROW * x, NARROW, range(4), sums[x]) for x in range(2)]

        def paired_sums(g, c, numbers):
            sums = [bank(number) for number in numbers]
            return [(g, CHUNK * c, CHUNK, range(2 * x, 2 * x + 2), sums[x]) for x in range(2)]

        def add_up(groups, order=(0, 1, 2, 3), begin=True, close=True):
            for k in order:
                for group in groups:
                    passes_of(*group, k, begin and k == order[0], close and k == order[-1])
            return [group[-1] for group in groups]

        def bank_by_bank(groups, order=(0, 1, 2, 3)):
            return [add_up([group], order)[0] for group in groups]

        def planar_tile(c):
            act[1, c] = relay.tile([P, 4 * CHUNK], F32, name="planar%d" % c, align_bytes=64, offset=(5 * c + 1) * KB)[:]

        def act_tiles(units, tag):
            both = keep.tile([P, len(units), 4 * CHUNK], F32, name=tag, align_bytes=64)
            for x, unit in enumerate(units):
                act[unit] = both[:, x, :]

        def woven(g, c, x0, x1):
            return act[g, c][:, 4 * NARROW * x0 : 4 * NARROW * x1].rearrange("p (j t) -> p j t", t=4)

        def tanh_woven(g, c, x, sums):
            nc.scalar.activation(out=woven(g, c, x, x + 1), in_=sums[:].rearrange("p (t j) -> p j t", t=4), func=ACT.Tanh)

        def tanh_planar(g, c, x, sums):
            nc.scalar.activation(out=act[g, c][:, HALF * x : HALF * (x + 1)], in_=sums[:], func=ACT.Tanh)

        def smooth(engine, g, c, x0, x1, out_view):
            factors = sm_sb[:, g, :].unsqueeze(1).to_broadcast([P, NARROW * (x1 - x0), 4])
            engine.tensor_tensor(out=out_view, in0=woven(g, c, x0, x1), in1=factors, op=MULT)

        def by_fours(view):
            return view.rearrange("p t (c i) -> p c t i", i=4)

        def scale_on_scalar(g, c):
            scaled = keep.tile([P, 4, CHUNK], BF16, name="scaled", align_bytes=64)
            for t in range(4):
                nc.scalar.activation(
                    out=scaled[:, t, :],
                    in_=act[g, c][:, CHUNK * t : CHUNK * (t + 1)],
                    func=ACT.Copy,
                    scale=sm_sb[:, g, t : t + 1],
                )
            return scaled

        def weave_on_scalar(scaled, out_view):
            nc.scalar.copy(out=out_view.rearrange("p (c i) t -> p c t i", i=4), in_=by_fours(scaled[:]))

        def h_tile():
            return keep.tile([P, 8 * CHUNK], BF16, name="h", align_bytes=64)

        def words(h, j0, j1):
            return h[:, 4 * j0 : 4 * j1].rearrange("p (j t) -> p j t", t=4)

        def code_tiles(c):
            h_codes[c] = relay.tile([P, 2 * CHUNK], U32, name="hc%d" % c, align_bytes=64, offset=(5 * c if c < 3 else 20) * KB)
            h_sc[c] = keep.tile([P, 2 * CHUNK], U8, name="hsc%d" % c, align_bytes=64)

        def quantize_h(c, c0, c1, values):
            nc.vector.quantize_mx(out=h_codes[c][:, c0:c1].bitcast(FP8X4), scales=h_sc[c][:, c0:c1], in_=values)

        def second_sum(y, i, c, pieces):
            n = slice(P * i, P * (i + 1))
            for number, (g, tier, c0, c1) in enumerate(pieces):
                if tier == 0:
                    lhs = wd4[:, g, P // 2 * i : P // 2 * (i + 1)].bitcast(FP4X4)
                else:
                    lhs = wd8[:, g, n].bitcast(FP8X4)
                nc.tensor.matmul_mx(
                    out=y[:, c0:c1],
                    lhsT=lhs,
                    lhsT_scale=wd_sc[tier][:, g, n],
                    rhs=h_codes[c][:, CHUNK * g + c0 : CHUNK * g + c1].bitcast(FP8X4),
                    rhs_scale=h_sc[c][:, CHUNK * g + c0 : CHUNK * g + c1],
                    start=(number == 0),
                    stop=(number == len(pieces) - 1),
                )

        whole = [(g, tier, 0, CHUNK) for g in range(2) for tier in (1, 0)]
        by_halves = whole[:2] + [(1, tier, c0, c0 + NARROW) for c0 in (0, NARROW) for tier in (1, 0)]
        sent = []


        def message(i, chunks, biased=None):
            scatter(i, chunks, weigh(i, chunks, biased))

        def weigh(i, chunks, biased=None):
            j0, j1 = CHUNK * chunks[0], CHUNK * (chunks[-1] + 1)
            y = bank(2 + len(sent) % 4, j1 - j0)
            for x, c in enumerate(chunks):
                second_sum(y[:, CHUNK * x : CHUNK * (x + 1)], i, c, by_halves if not sent else whole)
            weighted = keep.tile([P, j1 - j0], F32, name="weighted%d_%d" % (chunks[0], i), align_bytes=64)
            if len(sent) < 2:
                nc.vector.scalar_tensor_tensor(
                    out=weighted[:], in0=y[:], scalar=b_sb[:, i : i + 1], in1=wgo_sb[:, j0:j1], op0=ADD, op1=MULT
                )
            else:
                if biased is None:
                    biased = keep.tile([P, j1 - j0], F32, name="biased%d" % (len(sent) % 3), align_bytes=64)[:]
                nc.scalar.activation(out=biased, in_=y[:], func=ACT.Identity, bias=b_sb[:, i : i + 1])
                nc.gpsimd.tensor_tensor(out=weighted[:], in0=biased, in1=wgo_sb[:, j0:j1], op=MULT)
            sent.append((i, j0))
            return weighted

        def scatter(i, chunks, weighted):
            j0, j1 = CHUNK * chunks[0], CHUNK * (chunks[-1] + 1)
            nc.vector.tensor_copy(placed[i][:].indirect(entries(1, j0, j1)), weighted[:])
            if j1 == J:
                if i < 3:
                    nc.sync.dma_start(out=out[P * i : P * (i + 1), :], in_=placed[i][:])
                else:
                    for queue, t0 in ((nc.sync, 0), (nc.scalar, T // 2)):
                        queue.dma_start(out=out[P * i : P * (i + 1), t0 : t0 + T // 2], in_=placed[i][:, t0 : t0 + T // 2])

        nc.vector.memset(tab_sc[0:SCALE_ROWS_AT].bitcast(I32), 0)
        nc.vector.memset(early_planes[:].bitcast(I32), 0)
        for i in range(2):
            clear(i, "page%d" % i)
        nc.sync.dma_start(lists[0][:], offs)
        nc.sync.dma_start(lists[1][:], offs2)
        nc.sync.dma_start(
            out=tab_sc[SCALE_ROWS_AT:P].bitcast(I32), in_=tab_scales.rearrange("a q t -> (a q) t").bitcast(I32)
        )
        nc.sync.dma_start(out=tab_w[:], in_=tab_words[0].rearrange("p t b -> p (t b)").bitcast(I32))
        load_wd_scales(1)
        load_both_groups(0)
        load_wd_scales(0)
        gather_scales()
        clear_on_gpsimd(2, 8 * KB)
        clear_on_gpsimd(3, 0)
        picked = gather_words()
        load_both_groups(1)
        move_scales(0)
        load_both_groups(2)
        round_w(0, 0, P, "scalar")
        round_w(4, 0, P, "scalar")
        move_scales(1)
        load_w(3)
        quantize_w(0)
        part_words(0, picked)
        load_w(7, 0, PASS // 2)
        load_w(7, PASS // 2, PASS)
        nc.sync.dma_start(out=sm_sb[:], in_=sm.rearrange("(g p t) -> p g t", g=2, t=4))
        nc.sync.dma_start(out=wd8[:], in_=wd8_words.rearrange("a p n i -> p a (n i)").bitcast(I32))
        nc.sync.dma_start(out=wd4[:], in_=wd4_words.rearrange("a p n -> p a n").bitcast(I32))
        nc.sync.dma_start(out=wgo_sb[:], in_=wgo)
        with nc.allow_non_contiguous_dma(reason="one bias value for each partition"):
            nc.sync.dma_start(out=b_sb[:], in_=b.rearrange("(i p) -> p i", p=P))

        quantize_w(4)
        part_words(1, picked)
        round_w(5, 0, P // 2, "vector")
        round_w(1, 0, P, "scalar")
        quantize_w(1)
        round_w(5, P // 2, P, "scalar")
        round_w(2, 0, P, "vector")
        quantize_w(5)
        round_w(6, 0, P, "scalar")
        quantize_w(2)
        round_w(3, 0, VECTOR_SHARE_3, "vector")
        round_w(3, VECTOR_SHARE_3, P, "scalar")
        quantize_w(3)
        head = narrow_sums(0, 0, (0, 1)) + narrow_sums(0, 1, (2, 3)) + narrow_sums(1, 0, (4, 5)) + paired_sums(1, 1, (6, 7))
        add_up(head, (0, 1), close=False)
        early = add_up(head[0:2], (2, 3), begin=False) + add_up(head[2:4], (2, 3), begin=False)
        quantize_w(6, tag="raw3_0")
        last_weight_tile()
        act_tiles([(0, 0), (0, 1)], "raw7_0")
        for x in range(4):
            tanh_woven(0, x // 2, x % 2, early[x])
        sums = add_up(head[4:6], (2, 3), begin=False)
        sums = sums + [add_up([group], (3, 2), begin=False)[0] for group in head[6:8]]

        code_tiles(0)
        first = keep.tile([P, CHUNK, 4], BF16, name="last0", align_bytes=64)
        smooth(nc.vector, 0, 0, 0, 2, first[:])
        quantize_h(0, 0, CHUNK, first[:].rearrange("p j t -> p (j t)"))
        act_tiles([(1, 0)], "act10")
        h = h_tile()
        for x in range(2):
            tanh_woven(1, 0, x, sums[x])
            smooth(nc.vector, 1, 0, x, x + 1, words(h, NARROW * x, NARROW * (x + 1)))
            quantize_h(0, CHUNK + NARROW * x, CHUNK + NARROW * (x + 1), h[:, HALF * x : HALF * (x + 1)])
        planar_tile(1)
        for x in range(2):
            tanh_planar(1, 1, x, sums[2 + x])

        for c in range(1, 4):
            h = h_tile()
            smooth(nc.gpsimd, 0, c, 0, 1, words(h, 0, NARROW))
            message(0, [c - 1], h[:, HALF : 2 * HALF].bitcast(F32))
            lead = 2 if c < 3 else 1
            for i in range(1, lead):
                message(i, [c - 1])
            smooth(nc.gpsimd, 0, c, 1, 2, words(h, NARROW, CHUNK))
            weave_on_scalar(scale_on_scalar(1, c), words(h, CHUNK, 2 * CHUNK))
            biased = [
                relay.tile([P, CHUNK], F32, name="late%d_%d" % (c, x), align_bytes=64, offset=(5 * c + 1 + x) * KB)
                for x in range(2)
            ]
            ready = [weigh(lead + x, [c - 1], biased[x][:]) for x in range(2)]
            code_tiles(c)
            quantize_h(c, 0, 2 * CHUNK, h[:])
            for x in range(2):
                scatter(lead + x, [c - 1], ready[x])
            if c < 3:
                narrow = bank_by_bank(narrow_sums(0, c + 1, (6, 7)))
                paired = bank_by_bank(paired_sums(1, c + 1, (0, 1)), (3, 0, 1, 2))
                planar_tile(c + 1)
                act_tiles([(0, c + 1)], ("both1", "both2")[c - 1])
                for x in range(2):
                    tanh_woven(0, c + 1, x, narrow[x])
                for x in range(2):
                    tanh_planar(1, c + 1, x, paired[x])
        for i in range(3):
            message(i, [3])
        message(3, [2, 3])
